import numpy as np
import ml_dtypes


def mxq(x, axis, fmt="e4m3"):
    dtype, down = {"e4m3": (ml_dtypes.float8_e4m3fn, 7), "e5m2": (ml_dtypes.float8_e5m2, 14)}[fmt]
    v = np.moveaxis(np.asarray(x, np.float32).astype(ml_dtypes.bfloat16).astype(np.float64), axis, -1)
    blocks = v.reshape(v.shape[:-1] + (-1, 32))
    amax = np.abs(blocks).max(-1, keepdims=True)
    byte = np.maximum(np.where(amax > 0, np.frexp(amax)[1] - 1 + 127, 0) - down, 1)
    scale = np.exp2(byte - 127.0)
    codes = (blocks / scale).astype(np.float32).astype(dtype).astype(np.float64)
    return np.moveaxis((codes * scale).reshape(v.shape), -1, axis)


WIDE = False


def mx_kscale(k):
    if not WIDE:
        return np.ones(k)
    levels = np.array([10, -10, 5, -5, 0])
    if k % 512:
        return np.exp2(np.random.permutation(np.resize(levels, k // 32))).repeat(32)
    a = np.empty((k // 512, 16))
    for p in range(k // 512):
        a[p, :8] = np.random.permutation(np.resize(levels, 8))
        for g in range(8):
            far = levels[np.abs(levels - a[p, g]) >= 10]
            a[p, g + 8] = far[np.random.randint(len(far))]
    return np.exp2(a.ravel()).repeat(32)


def f64(x):
    return np.asarray(x).astype(np.float64)


def striped(idx):
    return np.tile(idx.reshape(-1, 16).T, (8, 1)).astype(np.uint16)


def unstriped(offs):
    return offs[:16].T.reshape(-1).astype(np.int64)


E2M1 = np.array([0.0, 0.5, 1.0, 1.5, 2.0, 3.0, 4.0, 6.0, -0.0, -0.5, -1.0, -1.5, -2.0, -3.0, -4.0, -6.0])


def pack_weight(w, fmt):
    k, n = w.shape
    w = f64(np.asarray(w, np.float32).astype(ml_dtypes.bfloat16)).reshape(k // 32, 32, n)
    amax = np.abs(w).max(1)
    if fmt == "e4m3":
        byte = np.frexp(amax)[1] - 1 + 127 - 7
    else:
        mant, ex = np.frexp(amax / 6.0)
        byte = np.where(mant > 0.5, ex, ex - 1) + 127
    byte = np.clip(np.where(amax > 0, byte, 1), 1, 254)
    scaled = (w * np.exp2(127.0 - byte)[:, None, :]).reshape(k, n).astype(np.float32)
    by_word = np.ascontiguousarray(scaled.reshape(k // 512, 128, 4, n).transpose(0, 1, 3, 2))
    if fmt == "e4m3":
        words = by_word.astype(ml_dtypes.float8_e4m3fn).view(np.uint8)
    else:
        c = by_word.astype(ml_dtypes.float4_e2m1fn).view(np.uint8) & 0xF
        words = (c[..., 0::2] | (c[..., 1::2] << 4)).reshape(k // 512, 128, 2 * n)
    return np.ascontiguousarray(words), np.ascontiguousarray(byte.astype(np.uint8).reshape(k // 512, 16, n))


def unpack_weight(words, scales, fmt):
    g, _, n = scales.shape
    words = np.ascontiguousarray(words).reshape(g, 128, n, -1)
    if fmt == "e4m3":
        vals = words.view(ml_dtypes.float8_e4m3fn).astype(np.float64)
    else:
        nib = np.empty((g, 128, n, 4), np.uint8)
        nib[..., 0::2] = words & 0xF
        nib[..., 1::2] = words >> 4
        vals = E2M1[nib]
    vals = vals * np.repeat(np.exp2(scales.astype(np.float64) - 127.0), 8, axis=1)[..., None]
    return vals.transpose(0, 1, 3, 2).reshape(g * 512, n)


def gelu(v):
    return 0.5 * v * (1.0 + np.tanh(np.sqrt(2.0 / np.pi) * (v + 0.044715 * v**3)))


def bf(x):
    return np.asarray(x, np.float32).astype(ml_dtypes.bfloat16)

def planes(Y):
    n, m = Y.shape
    b = f64(bf(Y)).reshape(n // 32, 32, m)
    amax = np.abs(b).max(1)
    byte = np.clip(np.where(amax > 0, np.frexp(amax)[1] - 1 + 127 - 7, 1), 1, 254)
    codes = (b * np.exp2(127.0 - byte)[:, None, :]).reshape(n, m).astype(np.float32).astype(ml_dtypes.float8_e4m3fn).view(np.uint8)
    words = codes.reshape(n // 512, 128, 4, m).transpose(0, 1, 3, 2)
    return np.ascontiguousarray(words), np.ascontiguousarray(byte.astype(np.uint8).reshape(n // 512, 16, m))


K, K2, H, N, T, T2, S = 1024, 512, 1024, 1024, 2048, 4096, 1024

def setup_inputs():
    n = np.random.standard_normal
    s = mx_kscale(K)[:, None]
    s2 = mx_kscale(K2)[:, None]
    u = mx_kscale(H)[:, None]
    tab_words, tab_scales = pack_weight(n((K, T)) * s, "e4m3")
    tab2_words, tab2_scales = pack_weight(n((K2, T2)) * s2, "e4m3")
    w4_words, w4_scales = pack_weight(n((K, H)) / np.sqrt(K) / s * u.T, "e2m1")
    w1 = (n((K2, H)) / np.sqrt(K2) / s2 * u.T).astype(np.float32)
    gain = np.exp(0.8 * n(N))
    skin = (n((H, N)) / np.sqrt(H) / u * gain).astype(np.float32)
    return {"tab_words": tab_words, "tab_scales": tab_scales,
            "tab2_words": tab2_words, "tab2_scales": tab2_scales,
            "offs": striped(np.random.permutation(T)[:S]),
            "offs2": striped(np.random.permutation(T2)[:S]),
            "w4_words": w4_words, "w4_scales": w4_scales, "w1": w1,
            "phase": np.random.random((H, S)).astype(np.float32),
            "skin": skin, "rest": (0.5 * gain * n(N)).astype(np.float32)}

def reference(tab_words, tab_scales, tab2_words, tab2_scales, offs, offs2,
              w4_words, w4_scales, w1, phase, skin, rest):
    v = unpack_weight(tab_words, tab_scales, "e4m3")[:, unstriped(offs)]
    v2 = unpack_weight(tab2_words, tab2_scales, "e4m3")[:, unstriped(offs2)]
    w4 = unpack_weight(w4_words, w4_scales, "e2m1")
    a = w4.T @ v
    b = mxq(f64(w1), 0, "e4m3").T @ v2
    h = a + f64(phase) * (b - a)
    y = mxq(f64(skin), 0, "e4m3").T @ mxq(h, 0, "e4m3")
    y = y + f64(rest)[:, None]
    words, scales = planes(y)
    return y, words, scales

@@ -1,0 +1,269 @@
+from contextlib import ExitStack
+
+import concourse.mybir as mybir
+
+F32 = mybir.dt.float32
+BF16 = mybir.dt.bfloat16
+I32 = mybir.dt.int32
+U32 = mybir.dt.uint32
+U16 = mybir.dt.uint16
+U8 = mybir.dt.uint8
+FP8X4 = mybir.dt.float8_e4m3fn_x4
+FP4X4 = mybir.dt.float4_e2m1fn_x4
+MULT = mybir.AluOpType.mult
+SUB = mybir.AluOpType.subtract
+IDENT = mybir.ActivationFunctionType.Identity
+
+K, K2, H, N, T, T2, S = 1024, 512, 1024, 1024, 2048, 4096, 1024
+P = 128
+G = 512
+HALF = 512
+UNIT = 128
+CHUNK = 256
+
+FLOPS = 2 * S * (K * H + K2 * H + H * N)
+
+
+def tile_list_keyframe_blend_skinning_kernel(
+    tc, tab_words, tab_scales, tab2_words, tab2_scales, offs, offs2,
+    w4_words, w4_scales, w1, phase, skin, rest, out_0, out_1, out_2,
+):
+    nc = tc.nc
+    with ExitStack() as ctx:
+        keep = ctx.enter_context(tc.tile_pool(name="keep", bufs=1))
+        ring = ctx.enter_context(tc.tile_pool(name="ring", bufs=2))
+        psum = ctx.enter_context(tc.psum_pool(name="psum", bufs=2))
+
+        def held(shape, dtype, name):
+            return keep.tile(shape, dtype, name=name, align_bytes=64)
+
+        idx = held([P, S // 16], U16, "idx")
+        idx2 = held([P, S // 16], U16, "idx2")
+        tab_s = held([P, 2 * T], U8, "tab_s")
+        tab2_s = held([P, T2], U8, "tab2_s")
+        w4_s_raw = held([P, 2 * H], U8, "w4_s_raw")
+        tab_w = [held([P, T], I32, "tab_w%d" % a) for a in range(2)]
+        tab2_w = held([P, T2], I32, "tab2_w")
+        w4_raw = held([P, 4 * H], U8, "w4_raw")
+        w4_c = held([P, 4 * H], U8, "w4_c")
+        w4_s = held([P, 2 * H], U8, "w4_s")
+        v_s = [held([P, S], U8, "v_s%d" % a) for a in range(2)]
+        v2_s = held([P, S], U8, "v2_s")
+        v_c = [[held([P, HALF], U32, "v_c%d%d" % (a, h)) for h in range(2)] for a in range(2)]
+        v2_c = [held([P, HALF], U32, "v2_c%d" % h) for h in range(2)]
+        w1_raw = [held([P, 4, G], F32, "w1_raw%d" % g) for g in range(2)]
+        w1_c = [held([P, G], U32, "w1_c%d" % g) for g in range(2)]
+        w1_s = [held([P, G], U8, "w1_s%d" % g) for g in range(2)]
+        skin_raw = [[held([P, 4, G], F32, "skin_raw%d%d" % (g, o)) for o in range(2)] for g in range(2)]
+        skin_c = [[held([P, G], U32, "skin_c%d%d" % (g, o)) for o in range(2)] for g in range(2)]
+        skin_s = [[held([P, G], U8, "skin_s%d%d" % (g, o)) for o in range(2)] for g in range(2)]
+        ph = [[held([P, 4, HALF], F32, "ph%d%d" % (g, h)) for h in range(2)] for g in range(2)]
+        rest_t = held([P, 2, 4], F32, "rest_t")
+        y_s = held([P, 2 * S], U8, "y_s")
+
+        nc.gpsimd.memset(tab_s[:].bitcast(I32), 0)
+        nc.vector.memset(tab2_s[:].bitcast(I32), 0)
+        nc.vector.memset(w4_s_raw[:].bitcast(I32), 0)
+
+        def load_rows(tile, rows):
+            nc.sync.dma_start(out=tile[:], in_=rows.rearrange("(p t) c -> p t c", t=4))
+
+        def load_words(tile, words):
+            nc.sync.dma_start(out=tile[:], in_=words.rearrange("p t i -> p (t i)").bitcast(I32))
+
+        def load_scales(queue, tile, scales):
+            for q in range(4):
+                queue.dma_start(
+                    out=tile[32 * q : 32 * q + 4, :].bitcast(I32).rearrange("r (a c) -> r a c", a=scales.shape[0]),
+                    in_=scales[:, 4 * q : 4 * q + 4, :].bitcast(I32).rearrange("a r c -> r a c"),
+                )
+
+        load_words(tab_w[0], tab_words[0])
+        nc.sync.dma_start(idx[:], offs)
+        load_scales(nc.sync, tab_s, tab_scales)
+        nc.sync.dma_start(idx2[:], offs2)
+        load_rows(w1_raw[0], w1[:, 0:G])
+        load_scales(nc.scalar, tab2_s, tab2_scales)
+        load_words(tab_w[1], tab_words[1])
+        load_scales(nc.scalar, w4_s_raw, w4_scales)
+        nc.sync.dma_start(
+            out=w4_raw[:].bitcast(I32).rearrange("p (a c) -> p a c", a=2),
+            in_=w4_words.bitcast(I32).rearrange("a p c -> p a c"),
+        )
+        load_words(tab2_w, tab2_words[0])
+        load_rows(ph[0][0], phase[0:G, 0:HALF])
+        load_rows(w1_raw[1], w1[:, G : 2 * G])
+        load_rows(skin_raw[0][0], skin[0:G, 0:G])
+        load_rows(ph[1][0], phase[G : 2 * G, 0:HALF])
+        load_rows(skin_raw[1][0], skin[G : 2 * G, 0:G])
+        nc.sync.dma_start(out=rest_t[:], in_=rest.rearrange("(g p t) -> p g t", g=2, t=4))
+        load_rows(skin_raw[0][1], skin[0:G, G : 2 * G])
+        load_rows(skin_raw[1][1], skin[G : 2 * G, G : 2 * G])
+        load_rows(ph[0][1], phase[0:G, HALF:S])
+        load_rows(ph[1][1], phase[G : 2 * G, HALF:S])
+
+        def gather_words(h):
+            cols = slice(h * HALF // 16, (h + 1) * HALF // 16)
+            for a in range(2):
+                nc.vector.tensor_copy(v_c[a][h][:], tab_w[a][:].bitcast(U32).indirect(idx[:, cols]))
+            nc.vector.tensor_copy(v2_c[h][:], tab2_w[:].bitcast(U32).indirect(idx2[:, cols]))
+
+        def round_weight(raw):
+            dealt = ring.tile([P, 4 * G], BF16, name="dealt", align_bytes=64)
+            nc.scalar.copy(
+                out=dealt[:].rearrange("p (t m j) -> p m t j", t=4, j=4),
+                in_=raw[:].rearrange("p j (m t) -> p m t j", t=4),
+            )
+            return dealt
+
+        def quantise(codes, scales, values):
+            nc.vector.quantize_mx(out=codes.bitcast(FP8X4), scales=scales, in_=values)
+
+        for a in range(2):
+            nc.vector.tensor_copy(v_s[a][:], tab_s[:, a * T : (a + 1) * T].indirect(idx[:]))
+        nc.vector.tensor_copy(v2_s[:], tab2_s[:].indirect(idx2[:]))
+        nc.vector.tensor_copy(
+            out=w4_s[:].rearrange("p (g t m) -> p g t m", g=4, t=4),
+            in_=w4_s_raw[:].rearrange("p (g m t) -> p g t m", g=4, t=4),
+        )
+        nc.vector.tensor_copy(
+            out=w4_c[:].bitcast(U16).rearrange("p (g t m) -> p g t m", g=4, t=4),
+            in_=w4_raw[:].bitcast(U16).rearrange("p (g m t) -> p g t m", g=4, t=4),
+        )
+        dealt = round_weight(w1_raw[0])
+        gather_words(0)
+        quantise(w1_c[0][:], w1_s[0][:], dealt[:])
+
+        h_b, h_c, h_s, terms = {}, {}, {}, {}
+
+        def blend_terms(g, j0):
+            h, c0 = divmod(j0, HALF)
+            a_ps = psum.tile([P, 4, UNIT], F32, name="a_ps", bufs=3)
+            b_ps = psum.tile([P, 4, UNIT], F32, name="b_ps", bufs=3)
+            for t in range(4):
+                m0 = t * P
+                nc.tensor.matmul_mx(
+                    out=b_ps[:, t, :],
+                    lhsT=w1_c[g][:, m0 : m0 + P].bitcast(FP8X4),
+                    lhsT_scale=w1_s[g][:, m0 : m0 + P],
+                    rhs=v2_c[h][:, c0 : c0 + UNIT].bitcast(FP8X4),
+                    rhs_scale=v2_s[:, j0 : j0 + UNIT],
+                    start=True,
+                    stop=True,
+                )
+            for t in range(4):
+                m0 = g * G + t * P
+                for a in range(2):
+                    nc.tensor.matmul_mx(
+                        out=a_ps[:, t, :],
+                        lhsT=w4_c[:, 2 * (a * H + m0) : 2 * (a * H + m0 + P)].bitcast(FP4X4),
+                        lhsT_scale=w4_s[:, a * H + m0 : a * H + m0 + P],
+                        rhs=v_c[a][h][:, c0 : c0 + UNIT].bitcast(FP8X4),
+                        rhs_scale=v_s[a][:, j0 : j0 + UNIT],
+                        start=(a == 0),
+                        stop=(a == 1),
+                    )
+            ph_cols = ph[g][h][:, :, c0 : c0 + UNIT]
+            b_term = ring.tile([P, 4, UNIT], F32, name="b_term", bufs=3)
+            a_term = ring.tile([P, 4, UNIT], F32, name="a_term", bufs=3)
+            nc.vector.tensor_tensor(b_term[:], b_ps[:], ph_cols, MULT)
+            nc.vector.scalar_tensor_tensor(a_term[:], ph_cols, 1.0, a_ps[:], SUB, MULT)
+            terms[g, j0] = (b_term, a_term)
+
+        def blend_sum(g, j0):
+            cc, c0 = divmod(j0, CHUNK)
+            if c0 == 0:
+                h_b[g, cc] = ring.tile([P, CHUNK, 4], BF16, name="h_b", align_bytes=64, bufs=3)
+            b_term, a_term = terms[g, j0]
+            nc.vector.tensor_tensor(
+                h_b[g, cc][:, c0 : c0 + UNIT, :].rearrange("p (c i) t -> p c t i", i=4),
+                b_term[:].rearrange("p t (c i) -> p c t i", i=4),
+                a_term[:].rearrange("p t (c i) -> p c t i", i=4),
+                SUB,
+            )
+
+        def quantise_h(g, cc):
+            h_c[g, cc] = held([P, CHUNK], U32, "h_c%d%d" % (g, cc))
+            h_s[g, cc] = held([P, CHUNK], U8, "h_s%d%d" % (g, cc))
+            quantise(h_c[g, cc][:], h_s[g, cc][:], h_b[g, cc][:].rearrange("p c t -> p (c t)"))
+
+        y_b = {}
+
+        def skin_product(cc, o):
+            cols = slice(cc * CHUNK, (cc + 1) * CHUNK)
+            y = ring.tile([P, 4, CHUNK], F32, name="y", bufs=3)
+            for pair in range(2):
+                y_ps = psum.tile([P, 2, CHUNK], F32, name="y_ps", bufs=2)
+                for k in range(2):
+                    m0 = (2 * pair + k) * P
+                    for g in range(2):
+                        nc.tensor.matmul_mx(
+                            out=y_ps[:, k, :],
+                            lhsT=skin_c[g][o][:, m0 : m0 + P].bitcast(FP8X4),
+                            lhsT_scale=skin_s[g][o][:, m0 : m0 + P],
+                            rhs=h_c[g, cc][:].bitcast(FP8X4),
+                            rhs_scale=h_s[g, cc][:],
+                            start=(g == 0),
+                            stop=(g == 1),
+                        )
+                for k in range(2):
+                    t = 2 * pair + k
+                    nc.scalar.activation(y[:, t, :], y_ps[:, k, :], IDENT, bias=rest_t[:, o, t : t + 1])
+            nc.sync.dma_start(
+                out=out_0[o * G : (o + 1) * G, cols].rearrange("(p t) j -> p t j", t=4), in_=y[:]
+            )
+            y_b[cc, o] = ring.tile([P, CHUNK, 4], BF16, name="y_b", align_bytes=64, bufs=3)
+            nc.scalar.copy(
+                out=y_b[cc, o][:].rearrange("p (c i) t -> p c t i", i=4),
+                in_=y[:].rearrange("p t (c i) -> p c t i", i=4),
+            )
+
+        def y_planes(cc, o):
+            cols = slice(cc * CHUNK, (cc + 1) * CHUNK)
+            y_c = ring.tile([P, CHUNK], I32, name="y_c", align_bytes=64, bufs=3)
+            j0 = o * S + cc * CHUNK
+            quantise(y_c[:], y_s[:, j0 : j0 + CHUNK], y_b[cc, o][:].rearrange("p c t -> p (c t)"))
+            nc.sync.dma_start(
+                out=out_1[o, :, cols, :].rearrange("p m t -> p (m t)").bitcast(I32), in_=y_c[:]
+            )
+
+        units = [(g, j0) for g in range(2) for j0 in range(0, HALF, UNIT)]
+        units = units + [
+            (g, cc * CHUNK + c0) for cc in (2, 3) for g in range(2) for c0 in range(0, CHUNK, UNIT)
+        ]
+        later = {}
+
+        def after(step, work):
+            later.setdefault(step, []).append(work)
+
+        def weight_steps(step, raw, codes, scales):
+            box = []
+            after(step, lambda: box.append(round_weight(raw)))
+            after(step + 1, lambda: quantise(codes[:], scales[:], box[0][:]))
+
+        weight_steps(1, w1_raw[1], w1_c[1], w1_s[1])
+        weight_steps(3, skin_raw[0][0], skin_c[0][0], skin_s[0][0])
+        weight_steps(4, skin_raw[1][0], skin_c[1][0], skin_s[1][0])
+        weight_steps(5, skin_raw[0][1], skin_c[0][1], skin_s[0][1])
+        weight_steps(6, skin_raw[1][1], skin_c[1][1], skin_s[1][1])
+        after(0, lambda: gather_words(1))
+        for u, (g, j0) in enumerate(units):
+            after(u + 1, lambda g=g, j0=j0: blend_sum(g, j0))
+            if (j0 + UNIT) % CHUNK == 0:
+                cc = j0 // CHUNK
+                after(u + 2, lambda g=g, cc=cc: quantise_h(g, cc))
+                if g == 1:
+                    for o in range(2):
+                        after(u + 2 + o, lambda cc=cc, o=o: skin_product(cc, o))
+                        after(u + 4 + o, lambda cc=cc, o=o: y_planes(cc, o))
+        for u in range(len(units) + 5):
+            if u < len(units):
+                blend_terms(*units[u])
+            for work in later.get(u, []):
+                work()
+
+        for q in range(4):
+            nc.sync.dma_start(
+                out=out_2[:, 4 * q : 4 * q + 4, :].bitcast(I32).rearrange("g r m -> r g m"),
+                in_=y_s[32 * q : 32 * q + 4, :].bitcast(I32).rearrange("r (g m) -> r g m", g=2),
+            )

@@ -12,6 +12,7 @@ FP8X4 = mybir.dt.float8_e4m3fn_x4
 FP4X4 = mybir.dt.float4_e2m1fn_x4
 MULT = mybir.AluOpType.mult
 SUB = mybir.AluOpType.subtract
+ADD = mybir.AluOpType.add
 IDENT = mybir.ActivationFunctionType.Identity
 
 K, K2, H, N, T, T2, S = 1024, 512, 1024, 1024, 2048, 4096, 1024
@@ -57,13 +58,15 @@ def tile_list_keyframe_blend_skinning_kernel(
         skin_raw = [[held([P, 4, G], F32, "skin_raw%d%d" % (g, o)) for o in range(2)] for g in range(2)]
         skin_c = [[held([P, G], U32, "skin_c%d%d" % (g, o)) for o in range(2)] for g in range(2)]
         skin_s = [[held([P, G], U8, "skin_s%d%d" % (g, o)) for o in range(2)] for g in range(2)]
-        ph = [[held([P, 4, HALF], F32, "ph%d%d" % (g, h)) for h in range(2)] for g in range(2)]
+        ph_cols = [(0, CHUNK), (CHUNK, HALF), (HALF, S)]
+        ph = [[held([P, 4, c1 - c0], F32, "ph%d%d" % (g, c0)) for c0, c1 in ph_cols] for g in range(2)]
         rest_t = held([P, 2, 4], F32, "rest_t")
         y_s = held([P, 2 * S], U8, "y_s")
 
-        nc.gpsimd.memset(tab_s[:].bitcast(I32), 0)
+        nc.gpsimd.memset(tab_s[:, 0:T].bitcast(I32), 0)
+        nc.vector.memset(tab_s[:, T : 2 * T].bitcast(I32), 0)
         nc.vector.memset(tab2_s[:].bitcast(I32), 0)
-        nc.vector.memset(w4_s_raw[:].bitcast(I32), 0)
+        nc.gpsimd.memset(w4_s_raw[:].bitcast(I32), 0)
 
         def load_rows(tile, rows):
             nc.sync.dma_start(out=tile[:], in_=rows.rearrange("(p t) c -> p t c", t=4))
@@ -78,35 +81,43 @@ def tile_list_keyframe_blend_skinning_kernel(
                     in_=scales[:, 4 * q : 4 * q + 4, :].bitcast(I32).rearrange("a r c -> r a c"),
                 )
 
-        load_words(tab_w[0], tab_words[0])
+        def load_phase(g, i):
+            load_rows(ph[g][i], phase[g * G : (g + 1) * G, ph_cols[i][0] : ph_cols[i][1]])
+
+        def load_skin(g, o):
+            load_rows(skin_raw[g][o], skin[g * G : (g + 1) * G, o * G : (o + 1) * G])
+
+        nc.sync.dma_start(
+            out=w4_raw[:].bitcast(I32).rearrange("p (a c) -> p a c", a=2),
+            in_=w4_words.bitcast(I32).rearrange("a p c -> p a c"),
+        )
         nc.sync.dma_start(idx[:], offs)
         load_scales(nc.sync, tab_s, tab_scales)
         nc.sync.dma_start(idx2[:], offs2)
         load_rows(w1_raw[0], w1[:, 0:G])
         load_scales(nc.scalar, tab2_s, tab2_scales)
-        load_words(tab_w[1], tab_words[1])
         load_scales(nc.scalar, w4_s_raw, w4_scales)
-        nc.sync.dma_start(
-            out=w4_raw[:].bitcast(I32).rearrange("p (a c) -> p a c", a=2),
-            in_=w4_words.bitcast(I32).rearrange("a p c -> p a c"),
-        )
-        load_words(tab2_w, tab2_words[0])
-        load_rows(ph[0][0], phase[0:G, 0:HALF])
         load_rows(w1_raw[1], w1[:, G : 2 * G])
-        load_rows(skin_raw[0][0], skin[0:G, 0:G])
-        load_rows(ph[1][0], phase[G : 2 * G, 0:HALF])
-        load_rows(skin_raw[1][0], skin[G : 2 * G, 0:G])
+        load_words(tab_w[0], tab_words[0])
+        load_words(tab2_w, tab2_words[0])
+        load_words(tab_w[1], tab_words[1])
+        load_skin(0, 0)
+        load_skin(1, 0)
+        load_phase(0, 0)
         nc.sync.dma_start(out=rest_t[:], in_=rest.rearrange("(g p t) -> p g t", g=2, t=4))
-        load_rows(skin_raw[0][1], skin[0:G, G : 2 * G])
-        load_rows(skin_raw[1][1], skin[G : 2 * G, G : 2 * G])
-        load_rows(ph[0][1], phase[0:G, HALF:S])
-        load_rows(ph[1][1], phase[G : 2 * G, HALF:S])
+        load_skin(0, 1)
+        load_phase(1, 0)
+        load_skin(1, 1)
+        load_phase(0, 1)
+        load_phase(1, 1)
+        load_phase(0, 2)
+        load_phase(1, 2)
 
         def gather_words(h):
             cols = slice(h * HALF // 16, (h + 1) * HALF // 16)
-            for a in range(2):
-                nc.vector.tensor_copy(v_c[a][h][:], tab_w[a][:].bitcast(U32).indirect(idx[:, cols]))
+            nc.vector.tensor_copy(v_c[0][h][:], tab_w[0][:].bitcast(U32).indirect(idx[:, cols]))
             nc.vector.tensor_copy(v2_c[h][:], tab2_w[:].bitcast(U32).indirect(idx2[:, cols]))
+            nc.vector.tensor_copy(v_c[1][h][:], tab_w[1][:].bitcast(U32).indirect(idx[:, cols]))
 
         def round_weight(raw):
             dealt = ring.tile([P, 4 * G], BF16, name="dealt", align_bytes=64)
@@ -130,72 +141,82 @@ def tile_list_keyframe_blend_skinning_kernel(
             out=w4_c[:].bitcast(U16).rearrange("p (g t m) -> p g t m", g=4, t=4),
             in_=w4_raw[:].bitcast(U16).rearrange("p (g m t) -> p g t m", g=4, t=4),
         )
-        dealt = round_weight(w1_raw[0])
+        w1_b = [round_weight(w1_raw[g]) for g in range(2)]
+        for g in range(2):
+            quantise(w1_c[g][:], w1_s[g][:], w1_b[g][:])
         gather_words(0)
-        quantise(w1_c[0][:], w1_s[0][:], dealt[:])
+        gather_words(1)
 
-        h_b, h_c, h_s, terms = {}, {}, {}, {}
+        h_b, h_c, h_s, terms, y_b = {}, {}, {}, {}, {}
+        chunks = [(0, 256), (256, 256), (512, 256), (768, 128), (896, 128)]
 
-        def blend_terms(g, j0):
+        def blend_terms(g, cc):
+            j0, w = chunks[cc]
             h, c0 = divmod(j0, HALF)
-            a_ps = psum.tile([P, 4, UNIT], F32, name="a_ps", bufs=3)
-            b_ps = psum.tile([P, 4, UNIT], F32, name="b_ps", bufs=3)
-            for t in range(4):
-                m0 = t * P
-                nc.tensor.matmul_mx(
-                    out=b_ps[:, t, :],
-                    lhsT=w1_c[g][:, m0 : m0 + P].bitcast(FP8X4),
-                    lhsT_scale=w1_s[g][:, m0 : m0 + P],
-                    rhs=v2_c[h][:, c0 : c0 + UNIT].bitcast(FP8X4),
-                    rhs_scale=v2_s[:, j0 : j0 + UNIT],
-                    start=True,
-                    stop=True,
-                )
-            for t in range(4):
-                m0 = g * G + t * P
-                for a in range(2):
+            piece = min(j0 // CHUNK, 2)
+            p0 = j0 - ph_cols[piece][0]
+            b_term = ring.tile([P, 2, w, 2], F32, name="b_term", bufs=3)
+            a_term = ring.tile([P, 2, w, 2], F32, name="a_term", bufs=3)
+            for u in range(2):
+                a_ps = psum.tile([P, 2, w], F32, name="a_ps", bufs=3)
+                b_ps = psum.tile([P, 2, w], F32, name="b_ps", bufs=3)
+                for e in range(2):
+                    m0 = (2 * u + e) * P
                     nc.tensor.matmul_mx(
-                        out=a_ps[:, t, :],
-                        lhsT=w4_c[:, 2 * (a * H + m0) : 2 * (a * H + m0 + P)].bitcast(FP4X4),
-                        lhsT_scale=w4_s[:, a * H + m0 : a * H + m0 + P],
-                        rhs=v_c[a][h][:, c0 : c0 + UNIT].bitcast(FP8X4),
-                        rhs_scale=v_s[a][:, j0 : j0 + UNIT],
-                        start=(a == 0),
-                        stop=(a == 1),
+                        out=b_ps[:, e, :],
+                        lhsT=w1_c[g][:, m0 : m0 + P].bitcast(FP8X4),
+                        lhsT_scale=w1_s[g][:, m0 : m0 + P],
+                        rhs=v2_c[h][:, c0 : c0 + w].bitcast(FP8X4),
+                        rhs_scale=v2_s[:, j0 : j0 + w],
+                        start=True,
+                        stop=True,
                     )
-            ph_cols = ph[g][h][:, :, c0 : c0 + UNIT]
-            b_term = ring.tile([P, 4, UNIT], F32, name="b_term", bufs=3)
-            a_term = ring.tile([P, 4, UNIT], F32, name="a_term", bufs=3)
-            nc.vector.tensor_tensor(b_term[:], b_ps[:], ph_cols, MULT)
-            nc.vector.scalar_tensor_tensor(a_term[:], ph_cols, 1.0, a_ps[:], SUB, MULT)
-            terms[g, j0] = (b_term, a_term)
+                for e in range(2):
+                    m0 = g * G + (2 * u + e) * P
+                    for n0 in range(0, w, UNIT):
+                        for a in range(2):
+                            nc.tensor.matmul_mx(
+                                out=a_ps[:, e, n0 : n0 + UNIT],
+                                lhsT=w4_c[:, 2 * (a * H + m0) : 2 * (a * H + m0 + P)].bitcast(FP4X4),
+                                lhsT_scale=w4_s[:, a * H + m0 : a * H + m0 + P],
+                                rhs=v_c[a][h][:, c0 + n0 : c0 + n0 + UNIT].bitcast(FP8X4),
+                                rhs_scale=v_s[a][:, j0 + n0 : j0 + n0 + UNIT],
+                                start=(a == 0),
+                                stop=(a == 1),
+                            )
+                ph_pair = ph[g][piece][:, 2 * u : 2 * u + 2, p0 : p0 + w].rearrange("p e j -> p j e")
+                nc.vector.tensor_tensor(b_term[:, u], b_ps[:].rearrange("p e j -> p j e"), ph_pair, MULT)
+                nc.vector.scalar_tensor_tensor(
+                    a_term[:, u], ph_pair, 1.0, a_ps[:].rearrange("p e j -> p j e"), SUB, MULT
+                )
+            terms[g, cc] = (b_term, a_term)
 
-        def blend_sum(g, j0):
-            cc, c0 = divmod(j0, CHUNK)
-            if c0 == 0:
-                h_b[g, cc] = ring.tile([P, CHUNK, 4], BF16, name="h_b", align_bytes=64, bufs=3)
-            b_term, a_term = terms[g, j0]
-            nc.vector.tensor_tensor(
-                h_b[g, cc][:, c0 : c0 + UNIT, :].rearrange("p (c i) t -> p c t i", i=4),
-                b_term[:].rearrange("p t (c i) -> p c t i", i=4),
-                a_term[:].rearrange("p t (c i) -> p c t i", i=4),
-                SUB,
-            )
+        def blend_sum(engine, g, cc):
+            w = chunks[cc][1]
+            h_b[g, cc] = ring.tile([P, w, 2, 2], BF16, name="h_b", align_bytes=64, bufs=3)
+            b_term, a_term = terms[g, cc]
+            for n0 in range(0, w, UNIT):
+                engine.tensor_tensor(
+                    h_b[g, cc][:, n0 : n0 + UNIT],
+                    b_term[:, :, n0 : n0 + UNIT, :].rearrange("p u j e -> p j u e"),
+                    a_term[:, :, n0 : n0 + UNIT, :].rearrange("p u j e -> p j u e"),
+                    SUB,
+                )
 
         def quantise_h(g, cc):
-            h_c[g, cc] = held([P, CHUNK], U32, "h_c%d%d" % (g, cc))
-            h_s[g, cc] = held([P, CHUNK], U8, "h_s%d%d" % (g, cc))
-            quantise(h_c[g, cc][:], h_s[g, cc][:], h_b[g, cc][:].rearrange("p c t -> p (c t)"))
+            w = chunks[cc][1]
+            h_c[g, cc] = held([P, w], U32, "h_c%d%d" % (g, cc))
+            h_s[g, cc] = held([P, w], U8, "h_s%d%d" % (g, cc))
+            quantise(h_c[g, cc][:], h_s[g, cc][:], h_b[g, cc][:].rearrange("p j u e -> p (j u e)"))
 
-        y_b = {}
-
-        def skin_product(cc, o):
-            cols = slice(cc * CHUNK, (cc + 1) * CHUNK)
-            y = ring.tile([P, 4, CHUNK], F32, name="y", bufs=3)
-            for pair in range(2):
-                y_ps = psum.tile([P, 2, CHUNK], F32, name="y_ps", bufs=2)
-                for k in range(2):
-                    m0 = (2 * pair + k) * P
+        def skin_product(cc, o, add_on_vector, round_on_vector):
+            j0, w = chunks[cc]
+            per_bank = G // w
+            y = ring.tile([P, 4, w], F32, name="y", bufs=3)
+            for t0 in range(0, 4, per_bank):
+                y_ps = psum.tile([P, per_bank, w], F32, name="y_ps", bufs=2)
+                for k in range(per_bank):
+                    m0 = (t0 + k) * P
                     for g in range(2):
                         nc.tensor.matmul_mx(
                             out=y_ps[:, k, :],
@@ -206,31 +227,37 @@ def tile_list_keyframe_blend_skinning_kernel(
                             start=(g == 0),
                             stop=(g == 1),
                         )
-                for k in range(2):
-                    t = 2 * pair + k
-                    nc.scalar.activation(y[:, t, :], y_ps[:, k, :], IDENT, bias=rest_t[:, o, t : t + 1])
+                if add_on_vector:
+                    nc.vector.tensor_tensor(
+                        y[:, t0 : t0 + per_bank, :],
+                        y_ps[:],
+                        rest_t[:, o, t0 : t0 + per_bank].unsqueeze(2).to_broadcast([P, per_bank, w]),
+                        ADD,
+                    )
+                else:
+                    for k in range(per_bank):
+                        t = t0 + k
+                        nc.scalar.activation(y[:, t, :], y_ps[:, k, :], IDENT, bias=rest_t[:, o, t : t + 1])
             nc.sync.dma_start(
-                out=out_0[o * G : (o + 1) * G, cols].rearrange("(p t) j -> p t j", t=4), in_=y[:]
+                out=out_0[o * G : (o + 1) * G, j0 : j0 + w].rearrange("(p t) j -> p t j", t=4), in_=y[:]
             )
-            y_b[cc, o] = ring.tile([P, CHUNK, 4], BF16, name="y_b", align_bytes=64, bufs=3)
-            nc.scalar.copy(
+            y_b[cc, o] = ring.tile([P, w, 4], BF16, name="y_b", align_bytes=64, bufs=3)
+            copy = nc.vector.tensor_copy if round_on_vector else nc.scalar.copy
+            copy(
                 out=y_b[cc, o][:].rearrange("p (c i) t -> p c t i", i=4),
                 in_=y[:].rearrange("p t (c i) -> p c t i", i=4),
             )
 
         def y_planes(cc, o):
-            cols = slice(cc * CHUNK, (cc + 1) * CHUNK)
-            y_c = ring.tile([P, CHUNK], I32, name="y_c", align_bytes=64, bufs=3)
-            j0 = o * S + cc * CHUNK
-            quantise(y_c[:], y_s[:, j0 : j0 + CHUNK], y_b[cc, o][:].rearrange("p c t -> p (c t)"))
+            j0, w = chunks[cc]
+            y_c = ring.tile([P, w], I32, name="y_c", align_bytes=64, bufs=3)
+            quantise(y_c[:], y_s[:, o * S + j0 : o * S + j0 + w], y_b[cc, o][:].rearrange("p c t -> p (c t)"))
             nc.sync.dma_start(
-                out=out_1[o, :, cols, :].rearrange("p m t -> p (m t)").bitcast(I32), in_=y_c[:]
+                out=out_1[o, :, j0 : j0 + w, :].rearrange("p m t -> p (m t)").bitcast(I32), in_=y_c[:]
             )
 
-        units = [(g, j0) for g in range(2) for j0 in range(0, HALF, UNIT)]
-        units = units + [
-            (g, cc * CHUNK + c0) for cc in (2, 3) for g in range(2) for c0 in range(0, CHUNK, UNIT)
-        ]
+        units = [(g, cc) for cc in range(len(chunks)) for g in range(2)]
+        last = len(units) - 1
         later = {}
 
         def after(step, work):
@@ -241,25 +268,23 @@ def tile_list_keyframe_blend_skinning_kernel(
             after(step, lambda: box.append(round_weight(raw)))
             after(step + 1, lambda: quantise(codes[:], scales[:], box[0][:]))
 
-        weight_steps(1, w1_raw[1], w1_c[1], w1_s[1])
-        weight_steps(3, skin_raw[0][0], skin_c[0][0], skin_s[0][0])
-        weight_steps(4, skin_raw[1][0], skin_c[1][0], skin_s[1][0])
-        weight_steps(5, skin_raw[0][1], skin_c[0][1], skin_s[0][1])
-        weight_steps(6, skin_raw[1][1], skin_c[1][1], skin_s[1][1])
-        after(0, lambda: gather_words(1))
-        for u, (g, j0) in enumerate(units):
-            after(u + 1, lambda g=g, j0=j0: blend_sum(g, j0))
-            if (j0 + UNIT) % CHUNK == 0:
-                cc = j0 // CHUNK
-                after(u + 2, lambda g=g, cc=cc: quantise_h(g, cc))
-                if g == 1:
-                    for o in range(2):
-                        after(u + 2 + o, lambda cc=cc, o=o: skin_product(cc, o))
-                        after(u + 4 + o, lambda cc=cc, o=o: y_planes(cc, o))
-        for u in range(len(units) + 5):
-            if u < len(units):
-                blend_terms(*units[u])
-            for work in later.get(u, []):
+        for s, (g, cc) in enumerate(units):
+            after(s, lambda s=s, g=g, cc=cc: blend_sum(nc.vector if s == last else nc.gpsimd, g, cc))
+            after(s + 1, lambda g=g, cc=cc: quantise_h(g, cc))
+        weight_steps(0, skin_raw[0][0], skin_c[0][0], skin_s[0][0])
+        weight_steps(0, skin_raw[1][0], skin_c[1][0], skin_s[1][0])
+        weight_steps(1, skin_raw[0][1], skin_c[0][1], skin_s[0][1])
+        weight_steps(2, skin_raw[1][1], skin_c[1][1], skin_s[1][1])
+        for cc in range(len(chunks)):
+            for o in range(2):
+                step = 2 * cc + 2 + o
+                tail = cc == len(chunks) - 1
+                after(step, lambda cc=cc, o=o, tail=tail: skin_product(cc, o, tail, tail))
+                after(step + 2, lambda cc=cc, o=o: y_planes(cc, o))
+        for s in range(len(units) + 4):
+            if s < len(units):
+                blend_terms(*units[s])
+            for work in later.get(s, []):
                 work()
 
         for q in range(4):

@@ -38,38 +38,46 @@ def tile_list_keyframe_blend_skinning_kernel(
         def held(shape, dtype, name):
             return keep.tile(shape, dtype, name=name, align_bytes=64)
 
+        def shared(shape, dtype, name, slot):
+            return keep.tile(shape, dtype, name=name, tag=slot, align_bytes=64)
+
         idx = held([P, S // 16], U16, "idx")
         idx2 = held([P, S // 16], U16, "idx2")
-        tab_s = held([P, 2 * T], U8, "tab_s")
-        tab2_s = held([P, T2], U8, "tab2_s")
+        tab_s = held([P, T], U8, "tab_s")
         w4_s_raw = held([P, 2 * H], U8, "w4_s_raw")
-        tab_w = [held([P, T], I32, "tab_w%d" % a) for a in range(2)]
-        tab2_w = held([P, T2], I32, "tab2_w")
-        w4_raw = held([P, 4 * H], U8, "w4_raw")
+        w4_raw = shared([P, 4 * H], U8, "w4_raw", "slot0")
+        tab_w = [shared([P, T], I32, "tab_w%d" % a, "slot%d" % (1 + 4 * a)) for a in range(2)]
+        tab2_s = shared([P, T2], U8, "tab2_s", "slot2")
+        w1_raw = [shared([P, 4, G], F32, "w1_raw0", "slot3")]
+        tab2_w = shared([P, T2], I32, "tab2_w", "slot4")
         w4_c = held([P, 4 * H], U8, "w4_c")
         w4_s = held([P, 2 * H], U8, "w4_s")
         v_s = [held([P, S], U8, "v_s%d" % a) for a in range(2)]
         v2_s = held([P, S], U8, "v2_s")
         v_c = [[held([P, HALF], U32, "v_c%d%d" % (a, h)) for h in range(2)] for a in range(2)]
         v2_c = [held([P, HALF], U32, "v2_c%d" % h) for h in range(2)]
-        w1_raw = [held([P, 4, G], F32, "w1_raw%d" % g) for g in range(2)]
         w1_c = [held([P, G], U32, "w1_c%d" % g) for g in range(2)]
         w1_s = [held([P, G], U8, "w1_s%d" % g) for g in range(2)]
-        skin_raw = [[held([P, 4, G], F32, "skin_raw%d%d" % (g, o)) for o in range(2)] for g in range(2)]
         skin_c = [[held([P, G], U32, "skin_c%d%d" % (g, o)) for o in range(2)] for g in range(2)]
         skin_s = [[held([P, G], U8, "skin_s%d%d" % (g, o)) for o in range(2)] for g in range(2)]
-        ph_cols = [(0, CHUNK), (CHUNK, HALF), (HALF, S)]
-        ph = [[held([P, 4, c1 - c0], F32, "ph%d%d" % (g, c0)) for c0, c1 in ph_cols] for g in range(2)]
         rest_t = held([P, 2, 4], F32, "rest_t")
         y_s = held([P, 2 * S], U8, "y_s")
+        ph_cols = [(0, CHUNK), (CHUNK, HALF), (HALF, S)]
+        ph, skin_raw = {}, {}
 
-        nc.gpsimd.memset(tab_s[:, 0:T].bitcast(I32), 0)
-        nc.vector.memset(tab_s[:, T : 2 * T].bitcast(I32), 0)
+        nc.gpsimd.memset(tab_s[:].bitcast(I32), 0)
         nc.vector.memset(tab2_s[:].bitcast(I32), 0)
         nc.gpsimd.memset(w4_s_raw[:].bitcast(I32), 0)
+        nc.gpsimd.memset(v_s[1][:].bitcast(I32), 0)
 
         def load_rows(tile, rows):
             nc.sync.dma_start(out=tile[:], in_=rows.rearrange("(p t) c -> p t c", t=4))
+
+        def load_dealt_rows(tile, rows):
+            for e in range(2):
+                nc.sync.dma_start(
+                    out=tile[e:P:2, :, :], in_=rows.rearrange("(m t e) c -> e m t c", t=4, e=2)[e]
+                )
 
         def load_words(tile, words):
             nc.sync.dma_start(out=tile[:], in_=words.rearrange("p t i -> p (t i)").bitcast(I32))
@@ -81,37 +89,34 @@ def tile_list_keyframe_blend_skinning_kernel(
                     in_=scales[:, 4 * q : 4 * q + 4, :].bitcast(I32).rearrange("a r c -> r a c"),
                 )
 
-        def load_phase(g, i):
-            load_rows(ph[g][i], phase[g * G : (g + 1) * G, ph_cols[i][0] : ph_cols[i][1]])
+        def load_phase(g, i, slot):
+            c0, c1 = ph_cols[i]
+            ph[g, i] = shared([P, 4, c1 - c0], F32, "ph%d%d" % (g, i), slot)
+            load_dealt_rows(ph[g, i], phase[g * G : (g + 1) * G, c0:c1])
 
-        def load_skin(g, o):
-            load_rows(skin_raw[g][o], skin[g * G : (g + 1) * G, o * G : (o + 1) * G])
+        def load_skin(g, o, slot):
+            skin_raw[g, o] = shared([P, 4, G], F32, "skin_raw%d%d" % (g, o), slot)
+            load_dealt_rows(skin_raw[g, o], skin[g * G : (g + 1) * G, o * G : (o + 1) * G])
 
+        nc.sync.dma_start(idx[:], offs)
+        for q in range(4):
+            nc.sync.dma_start(
+                out=tab_s[32 * q : 32 * q + 8, :].bitcast(I32),
+                in_=tab_scales[:, 4 * q : 4 * q + 4, :].bitcast(I32),
+            )
+        nc.sync.dma_start(idx2[:], offs2)
         nc.sync.dma_start(
             out=w4_raw[:].bitcast(I32).rearrange("p (a c) -> p a c", a=2),
             in_=w4_words.bitcast(I32).rearrange("a p c -> p a c"),
         )
-        nc.sync.dma_start(idx[:], offs)
-        load_scales(nc.sync, tab_s, tab_scales)
-        nc.sync.dma_start(idx2[:], offs2)
-        load_rows(w1_raw[0], w1[:, 0:G])
-        load_scales(nc.scalar, tab2_s, tab2_scales)
-        load_scales(nc.scalar, w4_s_raw, w4_scales)
-        load_rows(w1_raw[1], w1[:, G : 2 * G])
         load_words(tab_w[0], tab_words[0])
+        load_scales(nc.sync, tab2_s, tab2_scales)
+        load_rows(w1_raw[0], w1[:, 0:G])
         load_words(tab2_w, tab2_words[0])
-        load_words(tab_w[1], tab_words[1])
-        load_skin(0, 0)
-        load_skin(1, 0)
-        load_phase(0, 0)
+        load_scales(nc.sync, w4_s_raw, w4_scales)
         nc.sync.dma_start(out=rest_t[:], in_=rest.rearrange("(g p t) -> p g t", g=2, t=4))
-        load_skin(0, 1)
-        load_phase(1, 0)
-        load_skin(1, 1)
-        load_phase(0, 1)
-        load_phase(1, 1)
-        load_phase(0, 2)
-        load_phase(1, 2)
+        load_words(tab_w[1], tab_words[1])
+        load_phase(0, 0, "slot6")
 
         def gather_words(h):
             cols = slice(h * HALF // 16, (h + 1) * HALF // 16)
@@ -119,38 +124,50 @@ def tile_list_keyframe_blend_skinning_kernel(
             nc.vector.tensor_copy(v2_c[h][:], tab2_w[:].bitcast(U32).indirect(idx2[:, cols]))
             nc.vector.tensor_copy(v_c[1][h][:], tab_w[1][:].bitcast(U32).indirect(idx[:, cols]))
 
-        def round_weight(raw):
+        def round_weight(raw, run=1):
             dealt = ring.tile([P, 4 * G], BF16, name="dealt", align_bytes=64)
             nc.scalar.copy(
-                out=dealt[:].rearrange("p (t m j) -> p m t j", t=4, j=4),
-                in_=raw[:].rearrange("p j (m t) -> p m t j", t=4),
+                out=dealt[:].rearrange("p (t m e j) -> p m t e j", t=4, e=run, j=4),
+                in_=raw[:].rearrange("p j (m t e) -> p m t e j", t=4, e=run),
             )
             return dealt
 
         def quantise(codes, scales, values):
             nc.vector.quantize_mx(out=codes.bitcast(FP8X4), scales=scales, in_=values)
 
-        for a in range(2):
-            nc.vector.tensor_copy(v_s[a][:], tab_s[:, a * T : (a + 1) * T].indirect(idx[:]))
+        nc.vector.tensor_copy(v_s[0][:], tab_s[:].indirect(idx[:]))
+        for q in range(4):
+            nc.sync.dma_start(
+                out=v_s[1][32 * q : 32 * q + 4, :].bitcast(I32),
+                in_=v_s[0][32 * q + 4 : 32 * q + 8, :].bitcast(I32),
+            )
+        nc.vector.tensor_copy(
+            out=w4_c[:].bitcast(I32).rearrange("p (g t m) -> p g t m", g=4, t=4),
+            in_=w4_raw[:].bitcast(I32).rearrange("p (g m t) -> p g t m", g=4, t=4),
+        )
         nc.vector.tensor_copy(v2_s[:], tab2_s[:].indirect(idx2[:]))
         nc.vector.tensor_copy(
-            out=w4_s[:].rearrange("p (g t m) -> p g t m", g=4, t=4),
-            in_=w4_s_raw[:].rearrange("p (g m t) -> p g t m", g=4, t=4),
+            out=w4_s[:].bitcast(U16).rearrange("p (g t m) -> p g t m", g=4, t=4),
+            in_=w4_s_raw[:].bitcast(U16).rearrange("p (g m t) -> p g t m", g=4, t=4),
         )
-        nc.vector.tensor_copy(
-            out=w4_c[:].bitcast(U16).rearrange("p (g t m) -> p g t m", g=4, t=4),
-            in_=w4_raw[:].bitcast(U16).rearrange("p (g m t) -> p g t m", g=4, t=4),
-        )
-        w1_b = [round_weight(w1_raw[g]) for g in range(2)]
-        for g in range(2):
-            quantise(w1_c[g][:], w1_s[g][:], w1_b[g][:])
+        quantise(w1_c[0][:], w1_s[0][:], round_weight(w1_raw[0], 2)[:])
         gather_words(0)
         gather_words(1)
+
+        w1_raw.append(shared([P, 4, G], F32, "w1_raw1", "slot0"))
+        load_rows(w1_raw[1], w1[:, G : 2 * G])
+        load_phase(1, 0, "slot1")
+        load_skin(0, 0, "slot2")
+        load_skin(1, 0, "slot3")
+        load_phase(0, 1, "slot4")
+        load_skin(0, 1, "slot5")
+        w1_b = round_weight(w1_raw[1], 2)
+        load_phase(1, 1, "slot0")
 
         h_b, h_c, h_s, terms, y_b = {}, {}, {}, {}, {}
         chunks = [(0, 256), (256, 256), (512, 256), (768, 128), (896, 128)]
 
-        def blend_terms(g, cc):
+        def blend_terms(g, cc, between):
             j0, w = chunks[cc]
             h, c0 = divmod(j0, HALF)
             piece = min(j0 // CHUNK, 2)
@@ -184,24 +201,25 @@ def tile_list_keyframe_blend_skinning_kernel(
                                 start=(a == 0),
                                 stop=(a == 1),
                             )
-                ph_pair = ph[g][piece][:, 2 * u : 2 * u + 2, p0 : p0 + w].rearrange("p e j -> p j e")
+                ph_pair = ph[g, piece][:, 2 * u : 2 * u + 2, p0 : p0 + w].rearrange("p e j -> p j e")
                 nc.vector.tensor_tensor(b_term[:, u], b_ps[:].rearrange("p e j -> p j e"), ph_pair, MULT)
                 nc.vector.scalar_tensor_tensor(
                     a_term[:, u], ph_pair, 1.0, a_ps[:].rearrange("p e j -> p j e"), SUB, MULT
                 )
+                if u == 0:
+                    between()
             terms[g, cc] = (b_term, a_term)
 
-        def blend_sum(engine, g, cc):
+        def blend_sum(g, cc):
             w = chunks[cc][1]
             h_b[g, cc] = ring.tile([P, w, 2, 2], BF16, name="h_b", align_bytes=64, bufs=3)
             b_term, a_term = terms[g, cc]
-            for n0 in range(0, w, UNIT):
-                engine.tensor_tensor(
-                    h_b[g, cc][:, n0 : n0 + UNIT],
-                    b_term[:, :, n0 : n0 + UNIT, :].rearrange("p u j e -> p j u e"),
-                    a_term[:, :, n0 : n0 + UNIT, :].rearrange("p u j e -> p j u e"),
-                    SUB,
-                )
+            nc.vector.tensor_tensor(
+                h_b[g, cc][:],
+                b_term[:].rearrange("p u j e -> p j u e"),
+                a_term[:].rearrange("p u j e -> p j u e"),
+                SUB,
+            )
 
         def quantise_h(g, cc):
             w = chunks[cc][1]
@@ -257,33 +275,39 @@ def tile_list_keyframe_blend_skinning_kernel(
             )
 
         units = [(g, cc) for cc in range(len(chunks)) for g in range(2)]
-        last = len(units) - 1
         later = {}
 
         def after(step, work):
             later.setdefault(step, []).append(work)
 
-        def weight_steps(step, raw, codes, scales):
+        def weight_steps(step, g, o):
             box = []
-            after(step, lambda: box.append(round_weight(raw)))
-            after(step + 1, lambda: quantise(codes[:], scales[:], box[0][:]))
+            after(step, lambda: box.append(round_weight(skin_raw[g, o])))
+            after(step + 1, lambda: quantise(skin_c[g][o][:], skin_s[g][o][:], box[0][:]))
 
         for s, (g, cc) in enumerate(units):
-            after(s, lambda s=s, g=g, cc=cc: blend_sum(nc.vector if s == last else nc.gpsimd, g, cc))
             after(s + 1, lambda g=g, cc=cc: quantise_h(g, cc))
-        weight_steps(0, skin_raw[0][0], skin_c[0][0], skin_s[0][0])
-        weight_steps(0, skin_raw[1][0], skin_c[1][0], skin_s[1][0])
-        weight_steps(1, skin_raw[0][1], skin_c[0][1], skin_s[0][1])
-        weight_steps(2, skin_raw[1][1], skin_c[1][1], skin_s[1][1])
+        after(0, lambda: quantise(w1_c[1][:], w1_s[1][:], w1_b[:]))
+        after(0, lambda: load_skin(1, 1, "slot6"))
+        weight_steps(0, 0, 0)
+        after(0, lambda: load_phase(0, 2, "slot2"))
+        weight_steps(1, 1, 0)
+        after(1, lambda: load_phase(1, 2, "slot3"))
+        weight_steps(2, 0, 1)
+        weight_steps(3, 1, 1)
         for cc in range(len(chunks)):
             for o in range(2):
-                step = 2 * cc + 2 + o
+                step = max(2 * cc + 2 + o, 2 + 2 * o)
                 tail = cc == len(chunks) - 1
                 after(step, lambda cc=cc, o=o, tail=tail: skin_product(cc, o, tail, tail))
                 after(step + 2, lambda cc=cc, o=o: y_planes(cc, o))
         for s in range(len(units) + 4):
-            if s < len(units):
-                blend_terms(*units[s])
+            if s == 0:
+                blend_terms(*units[s], lambda: None)
+            elif s < len(units):
+                blend_terms(*units[s], lambda: blend_sum(*units[s - 1]))
+            elif s == len(units):
+                blend_sum(*units[s - 1])
             for work in later.get(s, []):
                 work()
 

@@ -17,10 +17,14 @@ IDENT = mybir.ActivationFunctionType.Identity
 
 K, K2, H, N, T, T2, S = 1024, 512, 1024, 1024, 2048, 4096, 1024
 P = 128
-G = 512
-HALF = 512
-UNIT = 128
-CHUNK = 256
+GROUP = 512
+BANK = 512
+W4_COLS = 128
+
+CHUNKS = [(0, 256), (256, 256), (512, 256), (768, 128), (896, 128)]
+PHASE_PARTS = [(0, 256), (256, 512), (512, 1024)]
+SKIN_PARTS = [(0, 0), (1, 0), (0, 1), (1, 1)]
+QUANTISE_LAG = 2
 
 FLOPS = 2 * S * (K * H + K2 * H + H * N)
 
@@ -32,38 +36,38 @@ def tile_list_keyframe_blend_skinning_kernel(
     nc = tc.nc
     with ExitStack() as ctx:
         keep = ctx.enter_context(tc.tile_pool(name="keep", bufs=1))
-        ring = ctx.enter_context(tc.tile_pool(name="ring", bufs=2))
+        ring = ctx.enter_context(tc.tile_pool(name="ring", bufs=3))
         psum = ctx.enter_context(tc.psum_pool(name="psum", bufs=2))
 
         def held(shape, dtype, name):
             return keep.tile(shape, dtype, name=name, align_bytes=64)
 
-        def shared(shape, dtype, name, slot):
-            return keep.tile(shape, dtype, name=name, tag=slot, align_bytes=64)
+        def staged(shape, dtype, name, area):
+            return keep.tile(shape, dtype, name=name, tag="area%d" % area, align_bytes=64)
 
         idx = held([P, S // 16], U16, "idx")
         idx2 = held([P, S // 16], U16, "idx2")
         tab_s = held([P, T], U8, "tab_s")
         w4_s_raw = held([P, 2 * H], U8, "w4_s_raw")
-        w4_raw = shared([P, 4 * H], U8, "w4_raw", "slot0")
-        tab_w = [shared([P, T], I32, "tab_w%d" % a, "slot%d" % (1 + 4 * a)) for a in range(2)]
-        tab2_s = shared([P, T2], U8, "tab2_s", "slot2")
-        w1_raw = [shared([P, 4, G], F32, "w1_raw0", "slot3")]
-        tab2_w = shared([P, T2], I32, "tab2_w", "slot4")
+        w4_raw = staged([P, 4 * H], U8, "w4_raw", 0)
+        tab_w = [staged([P, T], I32, "tab_w0", 1), staged([P, T], I32, "tab_w1", 5)]
+        tab2_s = staged([P, T2], U8, "tab2_s", 2)
+        w1_raw = [staged([P, 4, GROUP], F32, "w1_raw0", 3)]
+        tab2_w = staged([P, T2], I32, "tab2_w", 4)
         w4_c = held([P, 4 * H], U8, "w4_c")
         w4_s = held([P, 2 * H], U8, "w4_s")
         v_s = [held([P, S], U8, "v_s%d" % a) for a in range(2)]
         v2_s = held([P, S], U8, "v2_s")
-        v_c = [[held([P, HALF], U32, "v_c%d%d" % (a, h)) for h in range(2)] for a in range(2)]
-        v2_c = [held([P, HALF], U32, "v2_c%d" % h) for h in range(2)]
-        w1_c = [held([P, G], U32, "w1_c%d" % g) for g in range(2)]
-        w1_s = [held([P, G], U8, "w1_s%d" % g) for g in range(2)]
-        skin_c = [[held([P, G], U32, "skin_c%d%d" % (g, o)) for o in range(2)] for g in range(2)]
-        skin_s = [[held([P, G], U8, "skin_s%d%d" % (g, o)) for o in range(2)] for g in range(2)]
-        rest_t = held([P, 2, 4], F32, "rest_t")
+        v_c = [held([P, S], U32, "v_c%d" % a) for a in range(2)]
+        v2_c = held([P, S], U32, "v2_c")
+        w1_c = [held([P, GROUP], U32, "w1_c%d" % g) for g in range(2)]
+        w1_s = [held([P, GROUP], U8, "w1_s%d" % g) for g in range(2)]
+        skin_c = [[held([P, GROUP], U32, "skin_c%d%d" % (g, o)) for o in range(2)] for g in range(2)]
+        skin_s = [[held([P, GROUP], U8, "skin_s%d%d" % (g, o)) for o in range(2)] for g in range(2)]
+        rest_cols = held([P, 2, 4], F32, "rest_cols")
         y_s = held([P, 2 * S], U8, "y_s")
-        ph_cols = [(0, CHUNK), (CHUNK, HALF), (HALF, S)]
-        ph, skin_raw = {}, {}
+        phase_raw, skin_raw, skin_b = {}, {}, {}
+        terms, h_b, h_c, h_s, y_b, y_c = {}, {}, {}, {}, {}, {}
 
         nc.gpsimd.memset(tab_s[:].bitcast(I32), 0)
         nc.vector.memset(tab2_s[:].bitcast(I32), 0)
@@ -73,30 +77,35 @@ def tile_list_keyframe_blend_skinning_kernel(
         def load_rows(tile, rows):
             nc.sync.dma_start(out=tile[:], in_=rows.rearrange("(p t) c -> p t c", t=4))
 
-        def load_dealt_rows(tile, rows):
-            for e in range(2):
-                nc.sync.dma_start(
-                    out=tile[e:P:2, :, :], in_=rows.rearrange("(m t e) c -> e m t c", t=4, e=2)[e]
-                )
-
         def load_words(tile, words):
             nc.sync.dma_start(out=tile[:], in_=words.rearrange("p t i -> p (t i)").bitcast(I32))
 
-        def load_scales(queue, tile, scales):
+        def load_planes(tile, scales):
             for q in range(4):
-                queue.dma_start(
-                    out=tile[32 * q : 32 * q + 4, :].bitcast(I32).rearrange("r (a c) -> r a c", a=scales.shape[0]),
-                    in_=scales[:, 4 * q : 4 * q + 4, :].bitcast(I32).rearrange("a r c -> r a c"),
+                nc.sync.dma_start(
+                    out=tile[32 * q : 32 * q + 4, :].bitcast(I32).rearrange("i (a c) -> i a c", a=scales.shape[0]),
+                    in_=scales[:, 4 * q : 4 * q + 4, :].bitcast(I32).rearrange("a i c -> i a c"),
                 )
 
-        def load_phase(g, i, slot):
-            c0, c1 = ph_cols[i]
-            ph[g, i] = shared([P, 4, c1 - c0], F32, "ph%d%d" % (g, i), slot)
-            load_dealt_rows(ph[g, i], phase[g * G : (g + 1) * G, c0:c1])
+        def load_phase(g, part, area):
+            j0, j1 = PHASE_PARTS[part]
+            phase_raw[g, part] = staged([P, 4, j1 - j0], F32, "phase_raw%d%d" % (g, part), area)
+            load_rows(phase_raw[g, part], phase[g * GROUP : (g + 1) * GROUP, j0:j1])
 
-        def load_skin(g, o, slot):
-            skin_raw[g, o] = shared([P, 4, G], F32, "skin_raw%d%d" % (g, o), slot)
-            load_dealt_rows(skin_raw[g, o], skin[g * G : (g + 1) * G, o * G : (o + 1) * G])
+        def load_skin(g, o, area):
+            skin_raw[g, o] = staged([P, 4, GROUP], F32, "skin_raw%d%d" % (g, o), area)
+            load_rows(skin_raw[g, o], skin[g * GROUP : (g + 1) * GROUP, o * GROUP : (o + 1) * GROUP])
+
+        def round_and_deal(raw):
+            dealt = ring.tile([P, 4 * GROUP], BF16, name="dealt", align_bytes=64)
+            nc.scalar.copy(
+                out=dealt[:].rearrange("p (t m i) -> p m t i", t=4, i=4),
+                in_=raw[:].rearrange("p i (m t) -> p m t i", t=4),
+            )
+            return dealt
+
+        def quantise(codes, scales, values):
+            nc.vector.quantize_mx(out=codes.bitcast(FP8X4), scales=scales, in_=values)
 
         nc.sync.dma_start(idx[:], offs)
         for q in range(4):
@@ -110,109 +119,93 @@ def tile_list_keyframe_blend_skinning_kernel(
             in_=w4_words.bitcast(I32).rearrange("a p c -> p a c"),
         )
         load_words(tab_w[0], tab_words[0])
-        load_scales(nc.sync, tab2_s, tab2_scales)
-        load_rows(w1_raw[0], w1[:, 0:G])
+        load_planes(tab2_s, tab2_scales)
+        load_rows(w1_raw[0], w1[:, 0:GROUP])
+        load_planes(w4_s_raw, w4_scales)
         load_words(tab2_w, tab2_words[0])
-        load_scales(nc.sync, w4_s_raw, w4_scales)
-        nc.sync.dma_start(out=rest_t[:], in_=rest.rearrange("(g p t) -> p g t", g=2, t=4))
         load_words(tab_w[1], tab_words[1])
-        load_phase(0, 0, "slot6")
-
-        def gather_words(h):
-            cols = slice(h * HALF // 16, (h + 1) * HALF // 16)
-            nc.vector.tensor_copy(v_c[0][h][:], tab_w[0][:].bitcast(U32).indirect(idx[:, cols]))
-            nc.vector.tensor_copy(v2_c[h][:], tab2_w[:].bitcast(U32).indirect(idx2[:, cols]))
-            nc.vector.tensor_copy(v_c[1][h][:], tab_w[1][:].bitcast(U32).indirect(idx[:, cols]))
-
-        def round_weight(raw, run=1):
-            dealt = ring.tile([P, 4 * G], BF16, name="dealt", align_bytes=64)
-            nc.scalar.copy(
-                out=dealt[:].rearrange("p (t m e j) -> p m t e j", t=4, e=run, j=4),
-                in_=raw[:].rearrange("p j (m t e) -> p m t e j", t=4, e=run),
-            )
-            return dealt
-
-        def quantise(codes, scales, values):
-            nc.vector.quantize_mx(out=codes.bitcast(FP8X4), scales=scales, in_=values)
+        load_phase(0, 0, 6)
+        nc.sync.dma_start(out=rest_cols[:], in_=rest.rearrange("(o p t) -> p o t", o=2, t=4))
 
         nc.vector.tensor_copy(v_s[0][:], tab_s[:].indirect(idx[:]))
         for q in range(4):
-            nc.sync.dma_start(
+            nc.scalar.dma_start(
                 out=v_s[1][32 * q : 32 * q + 4, :].bitcast(I32),
                 in_=v_s[0][32 * q + 4 : 32 * q + 8, :].bitcast(I32),
             )
         nc.vector.tensor_copy(
-            out=w4_c[:].bitcast(I32).rearrange("p (g t m) -> p g t m", g=4, t=4),
-            in_=w4_raw[:].bitcast(I32).rearrange("p (g m t) -> p g t m", g=4, t=4),
+            out=w4_c[:].bitcast(U16).rearrange("p (run t m) -> p run t m", run=4, t=4),
+            in_=w4_raw[:].bitcast(U16).rearrange("p (run m t) -> p run t m", run=4, t=4),
         )
         nc.vector.tensor_copy(v2_s[:], tab2_s[:].indirect(idx2[:]))
         nc.vector.tensor_copy(
-            out=w4_s[:].bitcast(U16).rearrange("p (g t m) -> p g t m", g=4, t=4),
-            in_=w4_s_raw[:].bitcast(U16).rearrange("p (g m t) -> p g t m", g=4, t=4),
+            out=w4_s[:].rearrange("p (run t m) -> p run t m", run=4, t=4),
+            in_=w4_s_raw[:].rearrange("p (run m t) -> p run t m", run=4, t=4),
         )
-        quantise(w1_c[0][:], w1_s[0][:], round_weight(w1_raw[0], 2)[:])
-        gather_words(0)
-        gather_words(1)
+        quantise(w1_c[0][:], w1_s[0][:], round_and_deal(w1_raw[0])[:])
+        nc.vector.tensor_copy(v_c[0][:], tab_w[0][:].bitcast(U32).indirect(idx[:]))
+        nc.vector.tensor_copy(v2_c[:], tab2_w[:].bitcast(U32).indirect(idx2[:]))
+        for j0 in range(0, S, S // 2):
+            nc.vector.tensor_copy(
+                v_c[1][:, j0 : j0 + S // 2],
+                tab_w[1][:].bitcast(U32).indirect(idx[:, j0 // 16 : (j0 + S // 2) // 16]),
+            )
 
-        w1_raw.append(shared([P, 4, G], F32, "w1_raw1", "slot0"))
-        load_rows(w1_raw[1], w1[:, G : 2 * G])
-        load_phase(1, 0, "slot1")
-        load_skin(0, 0, "slot2")
-        load_skin(1, 0, "slot3")
-        load_phase(0, 1, "slot4")
-        load_skin(0, 1, "slot5")
-        w1_b = round_weight(w1_raw[1], 2)
-        load_phase(1, 1, "slot0")
+        w1_raw.append(staged([P, 4, GROUP], F32, "w1_raw1", 0))
+        load_rows(w1_raw[1], w1[:, GROUP : 2 * GROUP])
+        load_phase(1, 0, 1)
+        load_skin(0, 0, 2)
+        load_phase(0, 1, 3)
+        load_skin(1, 0, 4)
+        load_phase(1, 1, 5)
+        w1_b1 = round_and_deal(w1_raw[1])
+        load_skin(0, 1, 0)
 
-        h_b, h_c, h_s, terms, y_b = {}, {}, {}, {}, {}
-        chunks = [(0, 256), (256, 256), (512, 256), (768, 128), (896, 128)]
-
-        def blend_terms(g, cc, between):
-            j0, w = chunks[cc]
-            h, c0 = divmod(j0, HALF)
-            piece = min(j0 // CHUNK, 2)
-            p0 = j0 - ph_cols[piece][0]
-            b_term = ring.tile([P, 2, w, 2], F32, name="b_term", bufs=3)
-            a_term = ring.tile([P, 2, w, 2], F32, name="a_term", bufs=3)
-            for u in range(2):
-                a_ps = psum.tile([P, 2, w], F32, name="a_ps", bufs=3)
-                b_ps = psum.tile([P, 2, w], F32, name="b_ps", bufs=3)
-                for e in range(2):
-                    m0 = (2 * u + e) * P
-                    nc.tensor.matmul_mx(
-                        out=b_ps[:, e, :],
-                        lhsT=w1_c[g][:, m0 : m0 + P].bitcast(FP8X4),
-                        lhsT_scale=w1_s[g][:, m0 : m0 + P],
-                        rhs=v2_c[h][:, c0 : c0 + w].bitcast(FP8X4),
-                        rhs_scale=v2_s[:, j0 : j0 + w],
-                        start=True,
-                        stop=True,
-                    )
-                for e in range(2):
-                    m0 = g * G + (2 * u + e) * P
-                    for n0 in range(0, w, UNIT):
-                        for a in range(2):
-                            nc.tensor.matmul_mx(
-                                out=a_ps[:, e, n0 : n0 + UNIT],
-                                lhsT=w4_c[:, 2 * (a * H + m0) : 2 * (a * H + m0 + P)].bitcast(FP4X4),
-                                lhsT_scale=w4_s[:, a * H + m0 : a * H + m0 + P],
-                                rhs=v_c[a][h][:, c0 + n0 : c0 + n0 + UNIT].bitcast(FP8X4),
-                                rhs_scale=v_s[a][:, j0 + n0 : j0 + n0 + UNIT],
-                                start=(a == 0),
-                                stop=(a == 1),
-                            )
-                ph_pair = ph[g, piece][:, 2 * u : 2 * u + 2, p0 : p0 + w].rearrange("p e j -> p j e")
-                nc.vector.tensor_tensor(b_term[:, u], b_ps[:].rearrange("p e j -> p j e"), ph_pair, MULT)
-                nc.vector.scalar_tensor_tensor(
-                    a_term[:, u], ph_pair, 1.0, a_ps[:].rearrange("p e j -> p j e"), SUB, MULT
+        def blend_terms(g, cc, u):
+            j0, w = CHUNKS[cc]
+            part = min(cc, len(PHASE_PARTS) - 1)
+            p0 = j0 - PHASE_PARTS[part][0]
+            if u == 0:
+                b_term = ring.tile([P, 2, w, 2], F32, name="b_term")
+                a_term = ring.tile([P, 2, w, 2], F32, name="a_term")
+                terms[g, cc] = (b_term, a_term)
+            b_term, a_term = terms[g, cc]
+            a_ps = psum.tile([P, 2, w], F32, name="a_ps")
+            b_ps = psum.tile([P, 2, w], F32, name="b_ps")
+            for e in range(2):
+                m0 = (2 * u + e) * P
+                nc.tensor.matmul_mx(
+                    out=b_ps[:, e, :],
+                    lhsT=w1_c[g][:, m0 : m0 + P].bitcast(FP8X4),
+                    lhsT_scale=w1_s[g][:, m0 : m0 + P],
+                    rhs=v2_c[:, j0 : j0 + w].bitcast(FP8X4),
+                    rhs_scale=v2_s[:, j0 : j0 + w],
+                    start=True,
+                    stop=True,
                 )
-                if u == 0:
-                    between()
-            terms[g, cc] = (b_term, a_term)
+            for e in range(2):
+                for n0 in range(0, w, W4_COLS):
+                    cols = slice(j0 + n0, j0 + n0 + W4_COLS)
+                    for a in range(2):
+                        m0 = a * H + g * GROUP + (2 * u + e) * P
+                        nc.tensor.matmul_mx(
+                            out=a_ps[:, e, n0 : n0 + W4_COLS],
+                            lhsT=w4_c[:, 2 * m0 : 2 * (m0 + P)].bitcast(FP4X4),
+                            lhsT_scale=w4_s[:, m0 : m0 + P],
+                            rhs=v_c[a][:, cols].bitcast(FP8X4),
+                            rhs_scale=v_s[a][:, cols],
+                            start=(a == 0),
+                            stop=(a == 1),
+                        )
+            phase_pair = phase_raw[g, part][:, 2 * u : 2 * u + 2, p0 : p0 + w].rearrange("p e j -> p j e")
+            nc.vector.tensor_tensor(b_term[:, u], b_ps[:].rearrange("p e j -> p j e"), phase_pair, MULT)
+            nc.vector.scalar_tensor_tensor(
+                a_term[:, u], phase_pair, 1.0, a_ps[:].rearrange("p e j -> p j e"), SUB, MULT
+            )
 
         def blend_sum(g, cc):
-            w = chunks[cc][1]
-            h_b[g, cc] = ring.tile([P, w, 2, 2], BF16, name="h_b", align_bytes=64, bufs=3)
+            w = CHUNKS[cc][1]
+            h_b[g, cc] = ring.tile([P, w, 2, 2], BF16, name="h_b", align_bytes=64)
             b_term, a_term = terms[g, cc]
             nc.vector.tensor_tensor(
                 h_b[g, cc][:],
@@ -222,17 +215,18 @@ def tile_list_keyframe_blend_skinning_kernel(
             )
 
         def quantise_h(g, cc):
-            w = chunks[cc][1]
+            w = CHUNKS[cc][1]
             h_c[g, cc] = held([P, w], U32, "h_c%d%d" % (g, cc))
             h_s[g, cc] = held([P, w], U8, "h_s%d%d" % (g, cc))
             quantise(h_c[g, cc][:], h_s[g, cc][:], h_b[g, cc][:].rearrange("p j u e -> p (j u e)"))
 
-        def skin_product(cc, o, add_on_vector, round_on_vector):
-            j0, w = chunks[cc]
-            per_bank = G // w
-            y = ring.tile([P, 4, w], F32, name="y", bufs=3)
+        def skin_product(cc, o):
+            j0, w = CHUNKS[cc]
+            last_chunk = cc == len(CHUNKS) - 1
+            per_bank = BANK // w
+            y = ring.tile([P, 4, w], F32, name="y", bufs=4)
             for t0 in range(0, 4, per_bank):
-                y_ps = psum.tile([P, per_bank, w], F32, name="y_ps", bufs=2)
+                y_ps = psum.tile([P, per_bank, w], F32, name="y_ps", bufs=4)
                 for k in range(per_bank):
                     m0 = (t0 + k) * P
                     for g in range(2):
@@ -245,74 +239,78 @@ def tile_list_keyframe_blend_skinning_kernel(
                             start=(g == 0),
                             stop=(g == 1),
                         )
-                if add_on_vector:
+                if last_chunk and o == 1:
                     nc.vector.tensor_tensor(
                         y[:, t0 : t0 + per_bank, :],
                         y_ps[:],
-                        rest_t[:, o, t0 : t0 + per_bank].unsqueeze(2).to_broadcast([P, per_bank, w]),
+                        rest_cols[:, o, t0 : t0 + per_bank].unsqueeze(2).to_broadcast([P, per_bank, w]),
                         ADD,
                     )
                 else:
                     for k in range(per_bank):
                         t = t0 + k
-                        nc.scalar.activation(y[:, t, :], y_ps[:, k, :], IDENT, bias=rest_t[:, o, t : t + 1])
+                        nc.scalar.activation(y[:, t, :], y_ps[:, k, :], IDENT, bias=rest_cols[:, o, t : t + 1])
             nc.sync.dma_start(
-                out=out_0[o * G : (o + 1) * G, j0 : j0 + w].rearrange("(p t) j -> p t j", t=4), in_=y[:]
+                out=out_0[o * GROUP : (o + 1) * GROUP, j0 : j0 + w].rearrange("(p t) j -> p t j", t=4), in_=y[:]
             )
-            y_b[cc, o] = ring.tile([P, w, 4], BF16, name="y_b", align_bytes=64, bufs=3)
-            copy = nc.vector.tensor_copy if round_on_vector else nc.scalar.copy
+            y_b[cc, o] = ring.tile([P, w, 4], BF16, name="y_b", align_bytes=64, bufs=4)
+            copy = nc.vector.tensor_copy if last_chunk else nc.scalar.copy
             copy(
                 out=y_b[cc, o][:].rearrange("p (c i) t -> p c t i", i=4),
                 in_=y[:].rearrange("p t (c i) -> p c t i", i=4),
             )
 
-        def y_planes(cc, o):
-            j0, w = chunks[cc]
-            y_c = ring.tile([P, w], I32, name="y_c", align_bytes=64, bufs=3)
-            quantise(y_c[:], y_s[:, o * S + j0 : o * S + j0 + w], y_b[cc, o][:].rearrange("p c t -> p (c t)"))
-            nc.sync.dma_start(
-                out=out_1[o, :, j0 : j0 + w, :].rearrange("p m t -> p (m t)").bitcast(I32), in_=y_c[:]
+        def quantise_y(cc, o):
+            j0, w = CHUNKS[cc]
+            if o == 0:
+                y_c[cc] = ring.tile([P, 2 * w], I32, name="y_c", align_bytes=64)
+            quantise(
+                y_c[cc][:, o * w : (o + 1) * w],
+                y_s[:, o * S + j0 : o * S + j0 + w],
+                y_b[cc, o][:].rearrange("p j t -> p (j t)"),
             )
+            if o == 1:
+                nc.sync.dma_start(
+                    out=out_1[:, :, j0 : j0 + w, :].rearrange("o p j t -> p o (j t)").bitcast(I32),
+                    in_=y_c[cc][:].rearrange("p (o j) -> p o j", o=2),
+                )
 
-        units = [(g, cc) for cc in range(len(chunks)) for g in range(2)]
-        later = {}
+        blends = [(g, cc) for cc in range(len(CHUNKS)) for g in range(2)]
 
-        def after(step, work):
-            later.setdefault(step, []).append(work)
+        def product_step(cc, o):
+            return max(2 * cc + 2 + o, SKIN_PARTS.index((1, o)) + QUANTISE_LAG)
 
-        def weight_steps(step, g, o):
-            box = []
-            after(step, lambda: box.append(round_weight(skin_raw[g, o])))
-            after(step + 1, lambda: quantise(skin_c[g][o][:], skin_s[g][o][:], box[0][:]))
-
-        for s, (g, cc) in enumerate(units):
-            after(s + 1, lambda g=g, cc=cc: quantise_h(g, cc))
-        after(0, lambda: quantise(w1_c[1][:], w1_s[1][:], w1_b[:]))
-        after(0, lambda: load_skin(1, 1, "slot6"))
-        weight_steps(0, 0, 0)
-        after(0, lambda: load_phase(0, 2, "slot2"))
-        weight_steps(1, 1, 0)
-        after(1, lambda: load_phase(1, 2, "slot3"))
-        weight_steps(2, 0, 1)
-        weight_steps(3, 1, 1)
-        for cc in range(len(chunks)):
-            for o in range(2):
-                step = max(2 * cc + 2 + o, 2 + 2 * o)
-                tail = cc == len(chunks) - 1
-                after(step, lambda cc=cc, o=o, tail=tail: skin_product(cc, o, tail, tail))
-                after(step + 2, lambda cc=cc, o=o: y_planes(cc, o))
-        for s in range(len(units) + 4):
+        for s in range(product_step(len(CHUNKS) - 1, 1) + QUANTISE_LAG + 1):
+            if s < len(blends):
+                blend_terms(*blends[s], 0)
+            if 1 <= s <= len(blends):
+                blend_sum(*blends[s - 1])
+            if s < len(blends):
+                blend_terms(*blends[s], 1)
+            if 1 <= s <= len(blends):
+                quantise_h(*blends[s - 1])
             if s == 0:
-                blend_terms(*units[s], lambda: None)
-            elif s < len(units):
-                blend_terms(*units[s], lambda: blend_sum(*units[s - 1]))
-            elif s == len(units):
-                blend_sum(*units[s - 1])
-            for work in later.get(s, []):
-                work()
+                quantise(w1_c[1][:], w1_s[1][:], w1_b1[:])
+                load_phase(0, 2, 6)
+            if s == 1:
+                load_phase(1, 2, 1)
+            if 0 <= s - QUANTISE_LAG < len(SKIN_PARTS):
+                g, o = SKIN_PARTS[s - QUANTISE_LAG]
+                quantise(skin_c[g][o][:], skin_s[g][o][:], skin_b[g, o][:])
+            if s < len(SKIN_PARTS):
+                skin_b[SKIN_PARTS[s]] = round_and_deal(skin_raw[SKIN_PARTS[s]])
+            if s == 0:
+                load_skin(1, 1, 2)
+            for cc in range(len(CHUNKS)):
+                for o in range(2):
+                    if s == product_step(cc, o):
+                        skin_product(cc, o)
+                    if s == product_step(cc, o) + QUANTISE_LAG:
+                        quantise_y(cc, o)
 
         for q in range(4):
-            nc.sync.dma_start(
-                out=out_2[:, 4 * q : 4 * q + 4, :].bitcast(I32).rearrange("g r m -> r g m"),
-                in_=y_s[32 * q : 32 * q + 4, :].bitcast(I32).rearrange("r (g m) -> r g m", g=2),
+            queue = nc.sync if q % 2 == 0 else nc.scalar
+            queue.dma_start(
+                out=out_2[:, 4 * q : 4 * q + 4, :].bitcast(I32).rearrange("o i j -> i o j"),
+                in_=y_s[32 * q : 32 * q + 4, :].bitcast(I32).rearrange("i (o j) -> i o j", o=2),
             )

@@ -81,10 +81,10 @@ def tile_list_keyframe_blend_skinning_kernel(
             nc.sync.dma_start(out=tile[:], in_=words.rearrange("p t i -> p (t i)").bitcast(I32))
 
         def load_planes(tile, scales):
-            for q in range(4):
+            for i in range(4):
                 nc.sync.dma_start(
-                    out=tile[32 * q : 32 * q + 4, :].bitcast(I32).rearrange("i (a c) -> i a c", a=scales.shape[0]),
-                    in_=scales[:, 4 * q : 4 * q + 4, :].bitcast(I32).rearrange("a i c -> i a c"),
+                    out=tile[i:P:32, :].bitcast(I32).rearrange("q (a c) -> q a c", a=scales.shape[0]),
+                    in_=scales[:, i:16:4, :].bitcast(I32).rearrange("a q c -> q a c"),
                 )
 
         def load_phase(g, part, area):
@@ -108,10 +108,10 @@ def tile_list_keyframe_blend_skinning_kernel(
             nc.vector.quantize_mx(out=codes.bitcast(FP8X4), scales=scales, in_=values)
 
         nc.sync.dma_start(idx[:], offs)
-        for q in range(4):
+        for i in range(4):
             nc.sync.dma_start(
-                out=tab_s[32 * q : 32 * q + 8, :].bitcast(I32),
-                in_=tab_scales[:, 4 * q : 4 * q + 4, :].bitcast(I32),
+                out=tab_s[i:P:16, :].bitcast(I32),
+                in_=tab_scales[:, i:16:4, :].bitcast(I32).rearrange("a q c -> q a c"),
             )
         nc.sync.dma_start(idx2[:], offs2)
         nc.sync.dma_start(
@@ -128,10 +128,10 @@ def tile_list_keyframe_blend_skinning_kernel(
         nc.sync.dma_start(out=rest_cols[:], in_=rest.rearrange("(o p t) -> p o t", o=2, t=4))
 
         nc.vector.tensor_copy(v_s[0][:], tab_s[:].indirect(idx[:]))
-        for q in range(4):
+        for i in range(4):
             nc.scalar.dma_start(
-                out=v_s[1][32 * q : 32 * q + 4, :].bitcast(I32),
-                in_=v_s[0][32 * q + 4 : 32 * q + 8, :].bitcast(I32),
+                out=v_s[1][i:P:32, :].bitcast(I32),
+                in_=v_s[0][16 + i : P : 32, :].bitcast(I32),
             )
         nc.vector.tensor_copy(
             out=w4_c[:].bitcast(U16).rearrange("p (run t m) -> p run t m", run=4, t=4),
@@ -308,9 +308,9 @@ def tile_list_keyframe_blend_skinning_kernel(
                     if s == product_step(cc, o) + QUANTISE_LAG:
                         quantise_y(cc, o)
 
-        for q in range(4):
-            queue = nc.sync if q % 2 == 0 else nc.scalar
+        for i in range(4):
+            queue = nc.sync if i % 2 == 0 else nc.scalar
             queue.dma_start(
-                out=out_2[:, 4 * q : 4 * q + 4, :].bitcast(I32).rearrange("o i j -> i o j"),
-                in_=y_s[32 * q : 32 * q + 4, :].bitcast(I32).rearrange("i (o j) -> i o j", o=2),
+                out=out_2[:, i:16:4, :].bitcast(I32).rearrange("o q j -> q o j"),
+                in_=y_s[i:P:32, :].bitcast(I32).rearrange("q (o j) -> q o j", o=2),
             )

@@ -22,7 +22,7 @@ BANK = 512
 W4_COLS = 128
 
 CHUNKS = [(0, 256), (256, 256), (512, 256), (768, 128), (896, 128)]
-PHASE_PARTS = [(0, 256), (256, 512), (512, 1024)]
+PHASE_PARTS = [(0, 256), (256, 512), (512, 768), (768, 1024)]
 SKIN_PARTS = [(0, 0), (1, 0), (0, 1), (1, 1)]
 QUANTISE_LAG = 2
 
@@ -161,19 +161,11 @@ def tile_list_keyframe_blend_skinning_kernel(
         w1_b1 = round_and_deal(w1_raw[1])
         load_skin(0, 1, 0)
 
-        def blend_terms(g, cc, u):
+        def b_product(g, cc, t0, nt):
             j0, w = CHUNKS[cc]
-            part = min(cc, len(PHASE_PARTS) - 1)
-            p0 = j0 - PHASE_PARTS[part][0]
-            if u == 0:
-                b_term = ring.tile([P, 2, w, 2], F32, name="b_term")
-                a_term = ring.tile([P, 2, w, 2], F32, name="a_term")
-                terms[g, cc] = (b_term, a_term)
-            b_term, a_term = terms[g, cc]
-            a_ps = psum.tile([P, 2, w], F32, name="a_ps")
-            b_ps = psum.tile([P, 2, w], F32, name="b_ps")
-            for e in range(2):
-                m0 = (2 * u + e) * P
+            b_ps = psum.tile([P, nt, w], F32, name="b_ps")
+            for e in range(nt):
+                m0 = (t0 + e) * P
                 nc.tensor.matmul_mx(
                     out=b_ps[:, e, :],
                     lhsT=w1_c[g][:, m0 : m0 + P].bitcast(FP8X4),
@@ -183,13 +175,19 @@ def tile_list_keyframe_blend_skinning_kernel(
                     start=True,
                     stop=True,
                 )
-            for e in range(2):
-                for n0 in range(0, w, W4_COLS):
-                    cols = slice(j0 + n0, j0 + n0 + W4_COLS)
+            return b_ps
+
+        def a_product(g, cc, t0, nt):
+            j0, w = CHUNKS[cc]
+            a_ps = psum.tile([P, nt, w], F32, name="a_ps")
+            step = BANK if w == BANK else W4_COLS
+            for e in range(nt):
+                for n0 in range(0, w, step):
+                    cols = slice(j0 + n0, j0 + n0 + step)
                     for a in range(2):
-                        m0 = a * H + g * GROUP + (2 * u + e) * P
+                        m0 = a * H + g * GROUP + (t0 + e) * P
                         nc.tensor.matmul_mx(
-                            out=a_ps[:, e, n0 : n0 + W4_COLS],
+                            out=a_ps[:, e, n0 : n0 + step],
                             lhsT=w4_c[:, 2 * m0 : 2 * (m0 + P)].bitcast(FP4X4),
                             lhsT_scale=w4_s[:, m0 : m0 + P],
                             rhs=v_c[a][:, cols].bitcast(FP8X4),
@@ -197,20 +195,37 @@ def tile_list_keyframe_blend_skinning_kernel(
                             start=(a == 0),
                             stop=(a == 1),
                         )
-            phase_pair = phase_raw[g, part][:, 2 * u : 2 * u + 2, p0 : p0 + w].rearrange("p e j -> p j e")
-            nc.vector.tensor_tensor(b_term[:, u], b_ps[:].rearrange("p e j -> p j e"), phase_pair, MULT)
-            nc.vector.scalar_tensor_tensor(
-                a_term[:, u], phase_pair, 1.0, a_ps[:].rearrange("p e j -> p j e"), SUB, MULT
-            )
+            return a_ps
+
+        def blend_terms(g, cc, half):
+            j0, w = CHUNKS[cc]
+            part = min(cc, len(PHASE_PARTS) - 1)
+            p0 = j0 - PHASE_PARTS[part][0]
+            if half == 0:
+                b_term = ring.tile([P, 4, w], F32, name="b_term")
+                a_term = ring.tile([P, 4, w], F32, name="a_term")
+                terms[g, cc] = (b_term, a_term)
+            b_term, a_term = terms[g, cc]
+            nt = BANK // w
+            jobs = [(kind, t0) for t0 in range(0, 4, nt) for kind in "ba"]
+            for kind, t0 in jobs[half * len(jobs) // 2 : (half + 1) * len(jobs) // 2]:
+                rows = slice(t0, t0 + nt)
+                ph = phase_raw[g, part][:, rows, p0 : p0 + w]
+                if kind == "b":
+                    nc.vector.tensor_tensor(b_term[:, rows, :], b_product(g, cc, t0, nt)[:], ph, MULT)
+                else:
+                    nc.vector.scalar_tensor_tensor(
+                        a_term[:, rows, :], ph, 1.0, a_product(g, cc, t0, nt)[:], SUB, MULT
+                    )
 
         def blend_sum(g, cc):
             w = CHUNKS[cc][1]
-            h_b[g, cc] = ring.tile([P, w, 2, 2], BF16, name="h_b", align_bytes=64)
+            h_b[g, cc] = ring.tile([P, w, 4], BF16, name="h_b", align_bytes=64)
             b_term, a_term = terms[g, cc]
             nc.vector.tensor_tensor(
-                h_b[g, cc][:],
-                b_term[:].rearrange("p u j e -> p j u e"),
-                a_term[:].rearrange("p u j e -> p j u e"),
+                h_b[g, cc][:].rearrange("p (c i) t -> p c t i", i=4),
+                b_term[:].rearrange("p t (c i) -> p c t i", i=4),
+                a_term[:].rearrange("p t (c i) -> p c t i", i=4),
                 SUB,
             )
 
@@ -218,7 +233,7 @@ def tile_list_keyframe_blend_skinning_kernel(
             w = CHUNKS[cc][1]
             h_c[g, cc] = held([P, w], U32, "h_c%d%d" % (g, cc))
             h_s[g, cc] = held([P, w], U8, "h_s%d%d" % (g, cc))
-            quantise(h_c[g, cc][:], h_s[g, cc][:], h_b[g, cc][:].rearrange("p j u e -> p (j u e)"))
+            quantise(h_c[g, cc][:], h_s[g, cc][:], h_b[g, cc][:].rearrange("p j t -> p (j t)"))
 
         def skin_product(cc, o):
             j0, w = CHUNKS[cc]
@@ -292,8 +307,6 @@ def tile_list_keyframe_blend_skinning_kernel(
             if s == 0:
                 quantise(w1_c[1][:], w1_s[1][:], w1_b1[:])
                 load_phase(0, 2, 6)
-            if s == 1:
-                load_phase(1, 2, 1)
             if 0 <= s - QUANTISE_LAG < len(SKIN_PARTS):
                 g, o = SKIN_PARTS[s - QUANTISE_LAG]
                 quantise(skin_c[g][o][:], skin_s[g][o][:], skin_b[g, o][:])
@@ -301,6 +314,11 @@ def tile_list_keyframe_blend_skinning_kernel(
                 skin_b[SKIN_PARTS[s]] = round_and_deal(skin_raw[SKIN_PARTS[s]])
             if s == 0:
                 load_skin(1, 1, 2)
+            if s == 1:
+                load_phase(1, 2, 1)
+            if s == 2:
+                load_phase(0, 3, 3)
+                load_phase(1, 3, 4)
             for cc in range(len(CHUNKS)):
                 for o in range(2):
                     if s == product_step(cc, o):

@@ -25,6 +25,7 @@ CHUNKS = [(0, 256), (256, 256), (512, 256), (768, 128), (896, 128)]
 PHASE_PARTS = [(0, 256), (256, 512), (512, 768), (768, 1024)]
 SKIN_PARTS = [(0, 0), (1, 0), (0, 1), (1, 1)]
 QUANTISE_LAG = 2
+SKIN_LAG = 1
 
 FLOPS = 2 * S * (K * H + K2 * H + H * N)
 
@@ -47,7 +48,7 @@ def tile_list_keyframe_blend_skinning_kernel(
 
         idx = held([P, S // 16], U16, "idx")
         idx2 = held([P, S // 16], U16, "idx2")
-        tab_s = held([P, T], U8, "tab_s")
+        tab_s = staged([P, T], U8, "tab_s", 7)
         w4_s_raw = held([P, 2 * H], U8, "w4_s_raw")
         w4_raw = staged([P, 4 * H], U8, "w4_raw", 0)
         tab_w = [staged([P, T], I32, "tab_w0", 1), staged([P, T], I32, "tab_w1", 5)]
@@ -64,7 +65,6 @@ def tile_list_keyframe_blend_skinning_kernel(
         w1_s = [held([P, GROUP], U8, "w1_s%d" % g) for g in range(2)]
         skin_c = [[held([P, GROUP], U32, "skin_c%d%d" % (g, o)) for o in range(2)] for g in range(2)]
         skin_s = [[held([P, GROUP], U8, "skin_s%d%d" % (g, o)) for o in range(2)] for g in range(2)]
-        rest_cols = held([P, 2, 4], F32, "rest_cols")
         y_s = held([P, 2 * S], U8, "y_s")
         phase_raw, skin_raw, skin_b = {}, {}, {}
         terms, h_b, h_c, h_s, y_b, y_c = {}, {}, {}, {}, {}, {}
@@ -75,32 +75,32 @@ def tile_list_keyframe_blend_skinning_kernel(
         nc.gpsimd.memset(v_s[1][:].bitcast(I32), 0)
 
         def load_rows(tile, rows):
-            nc.sync.dma_start(out=tile[:], in_=rows.rearrange("(p t) c -> p t c", t=4))
+            nc.sync.dma_start(out=tile, in_=rows.rearrange("(p t) c -> p t c", t=4))
 
         def load_words(tile, words):
             nc.sync.dma_start(out=tile[:], in_=words.rearrange("p t i -> p (t i)").bitcast(I32))
 
-        def load_planes(tile, scales):
-            for i in range(4):
+        def load_planes(tile, scales, rows):
+            for i in rows:
                 nc.sync.dma_start(
                     out=tile[i:P:32, :].bitcast(I32).rearrange("q (a c) -> q a c", a=scales.shape[0]),
                     in_=scales[:, i:16:4, :].bitcast(I32).rearrange("a q c -> q a c"),
                 )
 
-        def load_phase(g, part, area):
+        def load_phase(g, part, place):
             j0, j1 = PHASE_PARTS[part]
-            phase_raw[g, part] = staged([P, 4, j1 - j0], F32, "phase_raw%d%d" % (g, part), area)
-            load_rows(phase_raw[g, part], phase[g * GROUP : (g + 1) * GROUP, j0:j1])
+            phase_raw[g, part] = place
+            load_rows(place, phase[g * GROUP : (g + 1) * GROUP, j0:j1])
 
-        def load_skin(g, o, area):
-            skin_raw[g, o] = staged([P, 4, GROUP], F32, "skin_raw%d%d" % (g, o), area)
-            load_rows(skin_raw[g, o], skin[g * GROUP : (g + 1) * GROUP, o * GROUP : (o + 1) * GROUP])
+        def load_skin(g, o, place):
+            skin_raw[g, o] = place
+            load_rows(place, skin[g * GROUP : (g + 1) * GROUP, o * GROUP : (o + 1) * GROUP])
 
         def round_and_deal(raw):
             dealt = ring.tile([P, 4 * GROUP], BF16, name="dealt", align_bytes=64)
             nc.scalar.copy(
-                out=dealt[:].rearrange("p (t m i) -> p m t i", t=4, i=4),
-                in_=raw[:].rearrange("p i (m t) -> p m t i", t=4),
+                out=dealt[:].rearrange("p (u e m i) -> p m u i e", u=2, e=2, i=4),
+                in_=raw.rearrange("p i (m u e) -> p m u i e", u=2, e=2),
             )
             return dealt
 
@@ -108,42 +108,64 @@ def tile_list_keyframe_blend_skinning_kernel(
             nc.vector.quantize_mx(out=codes.bitcast(FP8X4), scales=scales, in_=values)
 
         nc.sync.dma_start(idx[:], offs)
+        nc.sync.dma_start(
+            out=w4_raw[:].bitcast(I32).rearrange("p (a c) -> p a c", a=2),
+            in_=w4_words.bitcast(I32).rearrange("a p c -> p a c"),
+        )
         for i in range(4):
             nc.sync.dma_start(
                 out=tab_s[i:P:16, :].bitcast(I32),
                 in_=tab_scales[:, i:16:4, :].bitcast(I32).rearrange("a q c -> q a c"),
             )
-        nc.sync.dma_start(idx2[:], offs2)
-        nc.sync.dma_start(
-            out=w4_raw[:].bitcast(I32).rearrange("p (a c) -> p a c", a=2),
-            in_=w4_words.bitcast(I32).rearrange("a p c -> p a c"),
-        )
         load_words(tab_w[0], tab_words[0])
-        load_planes(tab2_s, tab2_scales)
-        load_rows(w1_raw[0], w1[:, 0:GROUP])
-        load_planes(w4_s_raw, w4_scales)
+        nc.sync.dma_start(idx2[:], offs2)
+        load_planes(tab2_s, tab2_scales, range(0, 2))
+        load_rows(w1_raw[0][:], w1[:, 0:GROUP])
+        load_planes(tab2_s, tab2_scales, range(2, 4))
+        load_planes(w4_s_raw, w4_scales, range(0, 1))
         load_words(tab2_w, tab2_words[0])
+        load_planes(w4_s_raw, w4_scales, range(1, 4))
         load_words(tab_w[1], tab_words[1])
-        load_phase(0, 0, 6)
-        nc.sync.dma_start(out=rest_cols[:], in_=rest.rearrange("(o p t) -> p o t", o=2, t=4))
 
-        nc.vector.tensor_copy(v_s[0][:], tab_s[:].indirect(idx[:]))
-        for i in range(4):
-            nc.scalar.dma_start(
-                out=v_s[1][i:P:32, :].bitcast(I32),
-                in_=v_s[0][16 + i : P : 32, :].bitcast(I32),
-            )
         nc.vector.tensor_copy(
             out=w4_c[:].bitcast(U16).rearrange("p (run t m) -> p run t m", run=4, t=4),
             in_=w4_raw[:].bitcast(U16).rearrange("p (run m t) -> p run t m", run=4, t=4),
         )
+        nc.vector.tensor_copy(v_s[0][:], tab_s[:].indirect(idx[:]))
+        for i in range(4):
+            nc.sync.dma_start(
+                out=v_s[1][i:P:32, :].bitcast(I32),
+                in_=v_s[0][16 + i : P : 32, :].bitcast(I32),
+            )
+        late = staged([P, 5 * 4 * GROUP + 6 * 4 * 256 + 8], F32, "late", 7)
+        used = [0]
+
+        def late_rows(width):
+            first = used[0]
+            used[0] = first + 4 * width
+            return late[:, first : first + 4 * width].rearrange("p (t c) -> p t c", t=4)
+
+        load_phase(0, 0, late_rows(256))
+        w1_raw1 = late_rows(GROUP)
+        load_rows(w1_raw1, w1[:, GROUP : 2 * GROUP])
+        load_phase(1, 0, late_rows(256))
+        load_skin(0, 0, late_rows(GROUP))
+        rest_cols = late_rows(2).rearrange("p t c -> p (t c)").rearrange("p (o t) -> p o t", o=2)
+        nc.sync.dma_start(out=rest_cols, in_=rest.rearrange("(o p t) -> p o t", o=2, t=4))
+        load_skin(1, 0, late_rows(GROUP))
+        load_phase(0, 1, late_rows(256))
+        load_skin(0, 1, late_rows(GROUP))
+        load_phase(1, 1, late_rows(256))
+        load_skin(1, 1, late_rows(GROUP))
+        load_phase(0, 2, late_rows(256))
+        load_phase(1, 2, late_rows(256))
+        nc.vector.tensor_copy(v_c[0][:], tab_w[0][:].bitcast(U32).indirect(idx[:]))
         nc.vector.tensor_copy(v2_s[:], tab2_s[:].indirect(idx2[:]))
+        quantise(w1_c[0][:], w1_s[0][:], round_and_deal(w1_raw[0][:])[:])
         nc.vector.tensor_copy(
             out=w4_s[:].rearrange("p (run t m) -> p run t m", run=4, t=4),
             in_=w4_s_raw[:].rearrange("p (run m t) -> p run t m", run=4, t=4),
         )
-        quantise(w1_c[0][:], w1_s[0][:], round_and_deal(w1_raw[0])[:])
-        nc.vector.tensor_copy(v_c[0][:], tab_w[0][:].bitcast(U32).indirect(idx[:]))
         nc.vector.tensor_copy(v2_c[:], tab2_w[:].bitcast(U32).indirect(idx2[:]))
         for j0 in range(0, S, S // 2):
             nc.vector.tensor_copy(
@@ -151,15 +173,9 @@ def tile_list_keyframe_blend_skinning_kernel(
                 tab_w[1][:].bitcast(U32).indirect(idx[:, j0 // 16 : (j0 + S // 2) // 16]),
             )
 
-        w1_raw.append(staged([P, 4, GROUP], F32, "w1_raw1", 0))
-        load_rows(w1_raw[1], w1[:, GROUP : 2 * GROUP])
-        load_phase(1, 0, 1)
-        load_skin(0, 0, 2)
-        load_phase(0, 1, 3)
-        load_skin(1, 0, 4)
-        load_phase(1, 1, 5)
-        w1_b1 = round_and_deal(w1_raw[1])
-        load_skin(0, 1, 0)
+        load_phase(0, 3, staged([P, 4, 256], F32, "phase_last0", 1)[:])
+        load_phase(1, 3, staged([P, 4, 256], F32, "phase_last1", 5)[:])
+        w1_b1 = round_and_deal(w1_raw1)
 
         def b_product(g, cc, t0, nt):
             j0, w = CHUNKS[cc]
@@ -199,7 +215,7 @@ def tile_list_keyframe_blend_skinning_kernel(
 
         def blend_terms(g, cc, half):
             j0, w = CHUNKS[cc]
-            part = min(cc, len(PHASE_PARTS) - 1)
+            part = j0 // 256
             p0 = j0 - PHASE_PARTS[part][0]
             if half == 0:
                 b_term = ring.tile([P, 4, w], F32, name="b_term")
@@ -293,7 +309,7 @@ def tile_list_keyframe_blend_skinning_kernel(
         blends = [(g, cc) for cc in range(len(CHUNKS)) for g in range(2)]
 
         def product_step(cc, o):
-            return max(2 * cc + 2 + o, SKIN_PARTS.index((1, o)) + QUANTISE_LAG)
+            return max(2 * cc + 2 + o, SKIN_PARTS.index((1, o)) + SKIN_LAG)
 
         for s in range(product_step(len(CHUNKS) - 1, 1) + QUANTISE_LAG + 1):
             if s < len(blends):
@@ -306,19 +322,11 @@ def tile_list_keyframe_blend_skinning_kernel(
                 quantise_h(*blends[s - 1])
             if s == 0:
                 quantise(w1_c[1][:], w1_s[1][:], w1_b1[:])
-                load_phase(0, 2, 6)
-            if 0 <= s - QUANTISE_LAG < len(SKIN_PARTS):
-                g, o = SKIN_PARTS[s - QUANTISE_LAG]
+            if 0 <= s - SKIN_LAG < len(SKIN_PARTS):
+                g, o = SKIN_PARTS[s - SKIN_LAG]
                 quantise(skin_c[g][o][:], skin_s[g][o][:], skin_b[g, o][:])
             if s < len(SKIN_PARTS):
                 skin_b[SKIN_PARTS[s]] = round_and_deal(skin_raw[SKIN_PARTS[s]])
-            if s == 0:
-                load_skin(1, 1, 2)
-            if s == 1:
-                load_phase(1, 2, 1)
-            if s == 2:
-                load_phase(0, 3, 3)
-                load_phase(1, 3, 4)
             for cc in range(len(CHUNKS)):
                 for o in range(2):
                     if s == product_step(cc, o):

@@ -22,10 +22,10 @@ BANK = 512
 W4_COLS = 128
 
 CHUNKS = [(0, 256), (256, 256), (512, 256), (768, 128), (896, 128)]
-PHASE_PARTS = [(0, 256), (256, 512), (512, 768), (768, 1024)]
+PHASE_COLS = 256
 SKIN_PARTS = [(0, 0), (1, 0), (0, 1), (1, 1)]
-QUANTISE_LAG = 2
 SKIN_LAG = 1
+Y_LAG = 2
 
 FLOPS = 2 * S * (K * H + K2 * H + H * N)
 
@@ -44,17 +44,17 @@ def tile_list_keyframe_blend_skinning_kernel(
             return keep.tile(shape, dtype, name=name, align_bytes=64)
 
         def staged(shape, dtype, name, area):
-            return keep.tile(shape, dtype, name=name, tag="area%d" % area, align_bytes=64)
+            return keep.tile(shape, dtype, name=name, tag=area, align_bytes=64)
 
         idx = held([P, S // 16], U16, "idx")
         idx2 = held([P, S // 16], U16, "idx2")
-        tab_s = staged([P, T], U8, "tab_s", 7)
+        tab_s = staged([P, T], U8, "tab_s", "late_area")
         w4_s_raw = held([P, 2 * H], U8, "w4_s_raw")
-        w4_raw = staged([P, 4 * H], U8, "w4_raw", 0)
-        tab_w = [staged([P, T], I32, "tab_w0", 1), staged([P, T], I32, "tab_w1", 5)]
-        tab2_s = staged([P, T2], U8, "tab2_s", 2)
-        w1_raw = [staged([P, 4, GROUP], F32, "w1_raw0", 3)]
-        tab2_w = staged([P, T2], I32, "tab2_w", 4)
+        w4_raw = held([P, 4 * H], U8, "w4_raw")
+        tab_w = [staged([P, T], I32, "tab_w%d" % a, "tab_area%d" % a) for a in range(2)]
+        tab2_s = held([P, T2], U8, "tab2_s")
+        w1_raw0 = held([P, 4, GROUP], F32, "w1_raw0")
+        tab2_w = held([P, T2], I32, "tab2_w")
         w4_c = held([P, 4 * H], U8, "w4_c")
         w4_s = held([P, 2 * H], U8, "w4_s")
         v_s = [held([P, S], U8, "v_s%d" % a) for a in range(2)]
@@ -67,30 +67,29 @@ def tile_list_keyframe_blend_skinning_kernel(
         skin_s = [[held([P, GROUP], U8, "skin_s%d%d" % (g, o)) for o in range(2)] for g in range(2)]
         y_s = held([P, 2 * S], U8, "y_s")
         phase_raw, skin_raw, skin_b = {}, {}, {}
-        terms, h_b, h_c, h_s, y_b, y_c = {}, {}, {}, {}, {}, {}
+        terms, h_b, h_c, h_s, y_b, y_c, last_ps = {}, {}, {}, {}, {}, {}, {}
 
         nc.gpsimd.memset(tab_s[:].bitcast(I32), 0)
         nc.vector.memset(tab2_s[:].bitcast(I32), 0)
         nc.gpsimd.memset(w4_s_raw[:].bitcast(I32), 0)
         nc.gpsimd.memset(v_s[1][:].bitcast(I32), 0)
 
-        def load_rows(tile, rows):
-            nc.sync.dma_start(out=tile, in_=rows.rearrange("(p t) c -> p t c", t=4))
+        def load_rows(place, rows):
+            nc.sync.dma_start(out=place, in_=rows.rearrange("(p t) c -> p t c", t=4))
 
         def load_words(tile, words):
             nc.sync.dma_start(out=tile[:], in_=words.rearrange("p t i -> p (t i)").bitcast(I32))
 
-        def load_planes(tile, scales, rows):
-            for i in rows:
+        def load_planes(tile, scales, live_rows):
+            for i in live_rows:
                 nc.sync.dma_start(
                     out=tile[i:P:32, :].bitcast(I32).rearrange("q (a c) -> q a c", a=scales.shape[0]),
                     in_=scales[:, i:16:4, :].bitcast(I32).rearrange("a q c -> q a c"),
                 )
 
         def load_phase(g, part, place):
-            j0, j1 = PHASE_PARTS[part]
             phase_raw[g, part] = place
-            load_rows(place, phase[g * GROUP : (g + 1) * GROUP, j0:j1])
+            load_rows(place, phase[g * GROUP : (g + 1) * GROUP, part * PHASE_COLS : (part + 1) * PHASE_COLS])
 
         def load_skin(g, o, place):
             skin_raw[g, o] = place
@@ -120,7 +119,7 @@ def tile_list_keyframe_blend_skinning_kernel(
         load_words(tab_w[0], tab_words[0])
         nc.sync.dma_start(idx2[:], offs2)
         load_planes(tab2_s, tab2_scales, range(0, 2))
-        load_rows(w1_raw[0][:], w1[:, 0:GROUP])
+        load_rows(w1_raw0[:], w1[:, 0:GROUP])
         load_planes(tab2_s, tab2_scales, range(2, 4))
         load_planes(w4_s_raw, w4_scales, range(0, 1))
         load_words(tab2_w, tab2_words[0])
@@ -137,31 +136,36 @@ def tile_list_keyframe_blend_skinning_kernel(
                 out=v_s[1][i:P:32, :].bitcast(I32),
                 in_=v_s[0][16 + i : P : 32, :].bitcast(I32),
             )
-        late = staged([P, 5 * 4 * GROUP + 6 * 4 * 256 + 8], F32, "late", 7)
-        used = [0]
+
+        late = staged([P, 4 * (5 * GROUP + 6 * PHASE_COLS + 2)], F32, "late", "late_area")
+        late_places = []
+
+        def late_place(width):
+            first = 4 * sum(late_places)
+            late_places.append(width)
+            return late[:, first : first + 4 * width]
 
         def late_rows(width):
-            first = used[0]
-            used[0] = first + 4 * width
-            return late[:, first : first + 4 * width].rearrange("p (t c) -> p t c", t=4)
+            return late_place(width).rearrange("p (t c) -> p t c", t=4)
 
-        load_phase(0, 0, late_rows(256))
+        load_phase(0, 0, late_rows(PHASE_COLS))
         w1_raw1 = late_rows(GROUP)
         load_rows(w1_raw1, w1[:, GROUP : 2 * GROUP])
-        load_phase(1, 0, late_rows(256))
+        load_phase(1, 0, late_rows(PHASE_COLS))
         load_skin(0, 0, late_rows(GROUP))
-        rest_cols = late_rows(2).rearrange("p t c -> p (t c)").rearrange("p (o t) -> p o t", o=2)
+        rest_cols = late_place(2).rearrange("p (o t) -> p o t", o=2)
         nc.sync.dma_start(out=rest_cols, in_=rest.rearrange("(o p t) -> p o t", o=2, t=4))
         load_skin(1, 0, late_rows(GROUP))
-        load_phase(0, 1, late_rows(256))
+        load_phase(0, 1, late_rows(PHASE_COLS))
         load_skin(0, 1, late_rows(GROUP))
-        load_phase(1, 1, late_rows(256))
+        load_phase(1, 1, late_rows(PHASE_COLS))
         load_skin(1, 1, late_rows(GROUP))
-        load_phase(0, 2, late_rows(256))
-        load_phase(1, 2, late_rows(256))
+        load_phase(0, 2, late_rows(PHASE_COLS))
+        load_phase(1, 2, late_rows(PHASE_COLS))
+
         nc.vector.tensor_copy(v_c[0][:], tab_w[0][:].bitcast(U32).indirect(idx[:]))
         nc.vector.tensor_copy(v2_s[:], tab2_s[:].indirect(idx2[:]))
-        quantise(w1_c[0][:], w1_s[0][:], round_and_deal(w1_raw[0][:])[:])
+        quantise(w1_c[0][:], w1_s[0][:], round_and_deal(w1_raw0[:])[:])
         nc.vector.tensor_copy(
             out=w4_s[:].rearrange("p (run t m) -> p run t m", run=4, t=4),
             in_=w4_s_raw[:].rearrange("p (run m t) -> p run t m", run=4, t=4),
@@ -173,8 +177,8 @@ def tile_list_keyframe_blend_skinning_kernel(
                 tab_w[1][:].bitcast(U32).indirect(idx[:, j0 // 16 : (j0 + S // 2) // 16]),
             )
 
-        load_phase(0, 3, staged([P, 4, 256], F32, "phase_last0", 1)[:])
-        load_phase(1, 3, staged([P, 4, 256], F32, "phase_last1", 5)[:])
+        for g in range(2):
+            load_phase(g, 3, staged([P, 4, PHASE_COLS], F32, "phase_last%d" % g, "tab_area%d" % g)[:])
         w1_b1 = round_and_deal(w1_raw1)
 
         def b_product(g, cc, t0, nt):
@@ -196,14 +200,13 @@ def tile_list_keyframe_blend_skinning_kernel(
         def a_product(g, cc, t0, nt):
             j0, w = CHUNKS[cc]
             a_ps = psum.tile([P, nt, w], F32, name="a_ps")
-            step = BANK if w == BANK else W4_COLS
             for e in range(nt):
-                for n0 in range(0, w, step):
-                    cols = slice(j0 + n0, j0 + n0 + step)
+                for n0 in range(0, w, W4_COLS):
+                    cols = slice(j0 + n0, j0 + n0 + W4_COLS)
                     for a in range(2):
                         m0 = a * H + g * GROUP + (t0 + e) * P
                         nc.tensor.matmul_mx(
-                            out=a_ps[:, e, n0 : n0 + step],
+                            out=a_ps[:, e, n0 : n0 + W4_COLS],
                             lhsT=w4_c[:, 2 * m0 : 2 * (m0 + P)].bitcast(FP4X4),
                             lhsT_scale=w4_s[:, m0 : m0 + P],
                             rhs=v_c[a][:, cols].bitcast(FP8X4),
@@ -215,8 +218,7 @@ def tile_list_keyframe_blend_skinning_kernel(
 
         def blend_terms(g, cc, half):
             j0, w = CHUNKS[cc]
-            part = j0 // 256
-            p0 = j0 - PHASE_PARTS[part][0]
+            part, p0 = divmod(j0, PHASE_COLS)
             if half == 0:
                 b_term = ring.tile([P, 4, w], F32, name="b_term")
                 a_term = ring.tile([P, 4, w], F32, name="a_term")
@@ -251,25 +253,38 @@ def tile_list_keyframe_blend_skinning_kernel(
             h_s[g, cc] = held([P, w], U8, "h_s%d%d" % (g, cc))
             quantise(h_c[g, cc][:], h_s[g, cc][:], h_b[g, cc][:].rearrange("p j t -> p (j t)"))
 
+        def y_pass(y_ps, cc, o, g, t, k, start, stop):
+            nc.tensor.matmul_mx(
+                out=y_ps[:, k, :],
+                lhsT=skin_c[g][o][:, t * P : (t + 1) * P].bitcast(FP8X4),
+                lhsT_scale=skin_s[g][o][:, t * P : (t + 1) * P],
+                rhs=h_c[g, cc][:].bitcast(FP8X4),
+                rhs_scale=h_s[g, cc][:],
+                start=start,
+                stop=stop,
+            )
+
+        def last_y_passes(o, g):
+            cc = len(CHUNKS) - 1
+            if g == 0:
+                last_ps[o] = psum.tile([P, 4, CHUNKS[cc][1]], F32, name=("b_ps", "a_ps")[o])
+            for t in range(4):
+                y_pass(last_ps[o], cc, o, g, t, t, g == 0 and t == 0, g == 1 and t == 3)
+
         def skin_product(cc, o):
             j0, w = CHUNKS[cc]
             last_chunk = cc == len(CHUNKS) - 1
             per_bank = BANK // w
             y = ring.tile([P, 4, w], F32, name="y", bufs=4)
             for t0 in range(0, 4, per_bank):
-                y_ps = psum.tile([P, per_bank, w], F32, name="y_ps", bufs=4)
-                for k in range(per_bank):
-                    m0 = (t0 + k) * P
-                    for g in range(2):
-                        nc.tensor.matmul_mx(
-                            out=y_ps[:, k, :],
-                            lhsT=skin_c[g][o][:, m0 : m0 + P].bitcast(FP8X4),
-                            lhsT_scale=skin_s[g][o][:, m0 : m0 + P],
-                            rhs=h_c[g, cc][:].bitcast(FP8X4),
-                            rhs_scale=h_s[g, cc][:],
-                            start=(g == 0),
-                            stop=(g == 1),
-                        )
+                if last_chunk:
+                    last_y_passes(o, 1)
+                    y_ps = last_ps[o]
+                else:
+                    y_ps = psum.tile([P, per_bank, w], F32, name="y_ps", bufs=4)
+                    for k in range(per_bank):
+                        for g in range(2):
+                            y_pass(y_ps, cc, o, g, t0 + k, k, g == 0, g == 1)
                 if last_chunk and o == 1:
                     nc.vector.tensor_tensor(
                         y[:, t0 : t0 + per_bank, :],
@@ -311,7 +326,7 @@ def tile_list_keyframe_blend_skinning_kernel(
         def product_step(cc, o):
             return max(2 * cc + 2 + o, SKIN_PARTS.index((1, o)) + SKIN_LAG)
 
-        for s in range(product_step(len(CHUNKS) - 1, 1) + QUANTISE_LAG + 1):
+        for s in range(product_step(len(CHUNKS) - 1, 1) + Y_LAG + 1):
             if s < len(blends):
                 blend_terms(*blends[s], 0)
             if 1 <= s <= len(blends):
@@ -320,6 +335,9 @@ def tile_list_keyframe_blend_skinning_kernel(
                 blend_terms(*blends[s], 1)
             if 1 <= s <= len(blends):
                 quantise_h(*blends[s - 1])
+            if s == len(blends) - 1:
+                for o in range(2):
+                    last_y_passes(o, 0)
             if s == 0:
                 quantise(w1_c[1][:], w1_s[1][:], w1_b1[:])
             if 0 <= s - SKIN_LAG < len(SKIN_PARTS):
@@ -331,7 +349,7 @@ def tile_list_keyframe_blend_skinning_kernel(
                 for o in range(2):
                     if s == product_step(cc, o):
                         skin_product(cc, o)
-                    if s == product_step(cc, o) + QUANTISE_LAG:
+                    if s == product_step(cc, o) + Y_LAG:
                         quantise_y(cc, o)
 
         for i in range(4):

@@ -26,6 +26,7 @@ PHASE_COLS = 256
 SKIN_PARTS = [(0, 0), (1, 0), (0, 1), (1, 1)]
 SKIN_LAG = 1
 Y_LAG = 2
+POOL_COLS = 192
 
 FLOPS = 2 * S * (K * H + K2 * H + H * N)
 
@@ -39,6 +40,7 @@ def tile_list_keyframe_blend_skinning_kernel(
         keep = ctx.enter_context(tc.tile_pool(name="keep", bufs=1))
         ring = ctx.enter_context(tc.tile_pool(name="ring", bufs=3))
         psum = ctx.enter_context(tc.psum_pool(name="psum", bufs=2))
+        late = ctx.enter_context(tc.tile_pool(name="late", bufs=1))
 
         def held(shape, dtype, name):
             return keep.tile(shape, dtype, name=name, align_bytes=64)
@@ -48,7 +50,9 @@ def tile_list_keyframe_blend_skinning_kernel(
 
         idx = held([P, S // 16], U16, "idx")
         idx2 = held([P, S // 16], U16, "idx2")
-        tab_s = staged([P, T], U8, "tab_s", "late_area")
+        late_bytes = 16 * (5 * GROUP + 6 * PHASE_COLS + 4)
+        tab_s_area = late.tile([P, late_bytes], U8, name="tab_s_area", align_bytes=64, offset=0)
+        tab_s = tab_s_area[:, 0:T]
         w4_s_raw = held([P, 2 * H], U8, "w4_s_raw")
         w4_raw = held([P, 4 * H], U8, "w4_raw")
         tab_w = [staged([P, T], I32, "tab_w%d" % a, "tab_area%d" % a) for a in range(2)]
@@ -69,7 +73,7 @@ def tile_list_keyframe_blend_skinning_kernel(
         phase_raw, skin_raw, skin_b = {}, {}, {}
         terms, h_b, h_c, h_s, y_b, y_c, last_ps = {}, {}, {}, {}, {}, {}, {}
 
-        nc.gpsimd.memset(tab_s[:].bitcast(I32), 0)
+        nc.gpsimd.memset(tab_s.bitcast(I32), 0)
         nc.vector.memset(tab2_s[:].bitcast(I32), 0)
         nc.gpsimd.memset(w4_s_raw[:].bitcast(I32), 0)
         nc.gpsimd.memset(v_s[1][:].bitcast(I32), 0)
@@ -113,7 +117,7 @@ def tile_list_keyframe_blend_skinning_kernel(
         )
         for i in range(4):
             nc.sync.dma_start(
-                out=tab_s[i:P:16, :].bitcast(I32),
+                out=tab_s_area[i:P:16, 0:T].bitcast(I32),
                 in_=tab_scales[:, i:16:4, :].bitcast(I32).rearrange("a q c -> q a c"),
             )
         load_words(tab_w[0], tab_words[0])
@@ -130,38 +134,40 @@ def tile_list_keyframe_blend_skinning_kernel(
             out=w4_c[:].bitcast(U16).rearrange("p (run t m) -> p run t m", run=4, t=4),
             in_=w4_raw[:].bitcast(U16).rearrange("p (run m t) -> p run t m", run=4, t=4),
         )
-        nc.vector.tensor_copy(v_s[0][:], tab_s[:].indirect(idx[:]))
+        nc.vector.tensor_copy(v_s[0][:], tab_s.indirect(idx[:]))
         for i in range(4):
             nc.sync.dma_start(
                 out=v_s[1][i:P:32, :].bitcast(I32),
                 in_=v_s[0][16 + i : P : 32, :].bitcast(I32),
             )
 
-        late = staged([P, 4 * (5 * GROUP + 6 * PHASE_COLS + 2)], F32, "late", "late_area")
         late_places = []
-
-        def late_place(width):
-            first = 4 * sum(late_places)
-            late_places.append(width)
-            return late[:, first : first + 4 * width]
+        phase_offset = {}
 
         def late_rows(width):
-            return late_place(width).rearrange("p (t c) -> p t c", t=4)
+            first = 16 * sum(late_places)
+            late_places.append(width)
+            place = late.tile([P, 4, width], F32, name="late%d" % len(late_places), align_bytes=64, offset=first)
+            return place[:]
 
-        load_phase(0, 0, late_rows(PHASE_COLS))
+        def load_late_phase(g, part):
+            phase_offset[g, part] = 16 * sum(late_places)
+            load_phase(g, part, late_rows(PHASE_COLS))
+
+        load_late_phase(0, 0)
         w1_raw1 = late_rows(GROUP)
         load_rows(w1_raw1, w1[:, GROUP : 2 * GROUP])
-        load_phase(1, 0, late_rows(PHASE_COLS))
+        load_late_phase(1, 0)
         load_skin(0, 0, late_rows(GROUP))
-        rest_cols = late_place(2).rearrange("p (o t) -> p o t", o=2)
+        rest_cols = late_rows(4).rearrange("p a b -> p (a b)")[:, 0:8].rearrange("p (o t) -> p o t", o=2)
         nc.sync.dma_start(out=rest_cols, in_=rest.rearrange("(o p t) -> p o t", o=2, t=4))
         load_skin(1, 0, late_rows(GROUP))
-        load_phase(0, 1, late_rows(PHASE_COLS))
+        load_late_phase(0, 1)
         load_skin(0, 1, late_rows(GROUP))
-        load_phase(1, 1, late_rows(PHASE_COLS))
+        load_late_phase(1, 1)
         load_skin(1, 1, late_rows(GROUP))
-        load_phase(0, 2, late_rows(PHASE_COLS))
-        load_phase(1, 2, late_rows(PHASE_COLS))
+        load_late_phase(0, 2)
+        load_late_phase(1, 2)
 
         nc.vector.tensor_copy(v_c[0][:], tab_w[0][:].bitcast(U32).indirect(idx[:]))
         nc.vector.tensor_copy(v2_s[:], tab2_s[:].indirect(idx2[:]))
@@ -220,36 +226,59 @@ def tile_list_keyframe_blend_skinning_kernel(
             j0, w = CHUNKS[cc]
             part, p0 = divmod(j0, PHASE_COLS)
             if half == 0:
-                b_term = ring.tile([P, 4, w], F32, name="b_term")
-                a_term = ring.tile([P, 4, w], F32, name="a_term")
+                b_term = ring.tile([P, 4 * w], F32, name="b_term")
+                a_term = ring.tile([P, 4 * w], F32, name="a_term")
                 terms[g, cc] = (b_term, a_term)
             b_term, a_term = terms[g, cc]
             nt = BANK // w
+            order = "p t j -> p j t" if nt == 2 else "p t j -> p t j"
             jobs = [(kind, t0) for t0 in range(0, 4, nt) for kind in "ba"]
             for kind, t0 in jobs[half * len(jobs) // 2 : (half + 1) * len(jobs) // 2]:
                 rows = slice(t0, t0 + nt)
-                ph = phase_raw[g, part][:, rows, p0 : p0 + w]
+                cols = slice(t0 * w, (t0 + nt) * w)
+                ph = phase_raw[g, part][:, rows, p0 : p0 + w].rearrange(order)
+                inner = 2 if nt == 2 else w
                 if kind == "b":
-                    nc.vector.tensor_tensor(b_term[:, rows, :], b_product(g, cc, t0, nt)[:], ph, MULT)
+                    nc.vector.tensor_tensor(
+                        b_term[:, cols].rearrange("p (x y) -> p x y", y=inner),
+                        b_product(g, cc, t0, nt)[:].rearrange(order), ph, MULT,
+                    )
                 else:
                     nc.vector.scalar_tensor_tensor(
-                        a_term[:, rows, :], ph, 1.0, a_product(g, cc, t0, nt)[:], SUB, MULT
+                        a_term[:, cols].rearrange("p (x y) -> p x y", y=inner),
+                        ph, 1.0, a_product(g, cc, t0, nt)[:].rearrange(order), SUB, MULT,
                     )
 
         def blend_sum(g, cc):
             w = CHUNKS[cc][1]
-            h_b[g, cc] = ring.tile([P, w, 4], BF16, name="h_b", align_bytes=64)
             b_term, a_term = terms[g, cc]
+            if BANK // w == 2:
+                h_b[g, cc] = ring.tile([P, w, 4], BF16, name="h_wide", align_bytes=64, bufs=1)
+                for engine, cols in ((nc.gpsimd, slice(0, POOL_COLS)), (nc.vector, slice(POOL_COLS, w))):
+                    engine.tensor_tensor(
+                        h_b[g, cc][:, cols, :].rearrange("p j (u e) -> p j u e", e=2),
+                        b_term[:].rearrange("p (u j e) -> p j u e", u=2, e=2)[:, cols],
+                        a_term[:].rearrange("p (u j e) -> p j u e", u=2, e=2)[:, cols],
+                        SUB,
+                    )
+                return
+            h_b[g, cc] = ring.tile([P, w, 4], BF16, name="h_b", align_bytes=64)
             nc.vector.tensor_tensor(
                 h_b[g, cc][:].rearrange("p (c i) t -> p c t i", i=4),
-                b_term[:].rearrange("p t (c i) -> p c t i", i=4),
-                a_term[:].rearrange("p t (c i) -> p c t i", i=4),
+                b_term[:].rearrange("p (t c i) -> p c t i", t=4, i=4),
+                a_term[:].rearrange("p (t c i) -> p c t i", t=4, i=4),
                 SUB,
             )
 
         def quantise_h(g, cc):
             w = CHUNKS[cc][1]
-            h_c[g, cc] = held([P, w], U32, "h_c%d%d" % (g, cc))
+            following = (1 - g, cc + g)
+            if following in phase_offset:
+                h_c[g, cc] = late.tile(
+                    [P, w], U32, name="h_c%d%d" % (g, cc), align_bytes=64, offset=phase_offset[following]
+                )
+            else:
+                h_c[g, cc] = held([P, w], U32, "h_c%d%d" % (g, cc))
             h_s[g, cc] = held([P, w], U8, "h_s%d%d" % (g, cc))
             quantise(h_c[g, cc][:], h_s[g, cc][:], h_b[g, cc][:].rearrange("p j t -> p (j t)"))
 
@@ -326,31 +355,41 @@ def tile_list_keyframe_blend_skinning_kernel(
         def product_step(cc, o):
             return max(2 * cc + 2 + o, SKIN_PARTS.index((1, o)) + SKIN_LAG)
 
-        for s in range(product_step(len(CHUNKS) - 1, 1) + Y_LAG + 1):
-            if s < len(blends):
-                blend_terms(*blends[s], 0)
-            if 1 <= s <= len(blends):
-                blend_sum(*blends[s - 1])
-            if s < len(blends):
-                blend_terms(*blends[s], 1)
-            if 1 <= s <= len(blends):
-                quantise_h(*blends[s - 1])
-            if s == len(blends) - 1:
-                for o in range(2):
-                    last_y_passes(o, 0)
+        def other_quantisers(s):
             if s == 0:
                 quantise(w1_c[1][:], w1_s[1][:], w1_b1[:])
             if 0 <= s - SKIN_LAG < len(SKIN_PARTS):
                 g, o = SKIN_PARTS[s - SKIN_LAG]
                 quantise(skin_c[g][o][:], skin_s[g][o][:], skin_b[g, o][:])
+            for cc in range(len(CHUNKS)):
+                for o in range(2):
+                    if s == product_step(cc, o) + Y_LAG:
+                        quantise_y(cc, o)
+
+        for s in range(product_step(len(CHUNKS) - 1, 1) + Y_LAG + 1):
+            shared = 1 <= s <= len(blends) and CHUNKS[blends[s - 1][1]][1] > POOL_COLS
+            if s < len(blends):
+                blend_terms(*blends[s], 0)
+            if 1 <= s <= len(blends) and not shared:
+                blend_sum(*blends[s - 1])
+            if s < len(blends):
+                blend_terms(*blends[s], 1)
+            if shared:
+                blend_sum(*blends[s - 1])
+                other_quantisers(s)
+            if 1 <= s <= len(blends):
+                quantise_h(*blends[s - 1])
+            if s == len(blends) - 1:
+                for o in range(2):
+                    last_y_passes(o, 0)
+            if not shared:
+                other_quantisers(s)
             if s < len(SKIN_PARTS):
                 skin_b[SKIN_PARTS[s]] = round_and_deal(skin_raw[SKIN_PARTS[s]])
             for cc in range(len(CHUNKS)):
                 for o in range(2):
                     if s == product_step(cc, o):
                         skin_product(cc, o)
-                    if s == product_step(cc, o) + Y_LAG:
-                        quantise_y(cc, o)
 
         for i in range(4):
             queue = nc.sync if i % 2 == 0 else nc.scalar

@@ -25,8 +25,12 @@ CHUNKS = [(0, 256), (256, 256), (512, 256), (768, 128), (896, 128)]
 PHASE_COLS = 256
 SKIN_PARTS = [(0, 0), (1, 0), (0, 1), (1, 1)]
 SKIN_LAG = 1
-Y_LAG = 2
+Y_LAG = 3
+VECTOR_ROUNDS_FROM = 2
+SKIN_FIRST = 1
 POOL_COLS = 192
+POOL_COLS_LAST = 96
+BLENDS = [(g, j0, 256) for j0 in (0, 256, 512) for g in range(2)] + [(0, 768, 256), (1, 768, 128), (1, 896, 128)]
 
 FLOPS = 2 * S * (K * H + K2 * H + H * N)
 
@@ -67,10 +71,10 @@ def tile_list_keyframe_blend_skinning_kernel(
         v2_c = held([P, S], U32, "v2_c")
         w1_c = [held([P, GROUP], U32, "w1_c%d" % g) for g in range(2)]
         w1_s = [held([P, GROUP], U8, "w1_s%d" % g) for g in range(2)]
-        skin_c = [[held([P, GROUP], U32, "skin_c%d%d" % (g, o)) for o in range(2)] for g in range(2)]
+        skin_c = [[None, None], [None, None]]
         skin_s = [[held([P, GROUP], U8, "skin_s%d%d" % (g, o)) for o in range(2)] for g in range(2)]
         y_s = held([P, 2 * S], U8, "y_s")
-        phase_raw, skin_raw, skin_b = {}, {}, {}
+        phase_raw, skin_raw, skin_b, y_f = {}, {}, {}, {}
         terms, h_b, h_c, h_s, y_b, y_c, last_ps = {}, {}, {}, {}, {}, {}, {}
 
         nc.gpsimd.memset(tab_s.bitcast(I32), 0)
@@ -161,12 +165,12 @@ def tile_list_keyframe_blend_skinning_kernel(
         load_skin(0, 0, late_rows(GROUP))
         rest_cols = late_rows(4).rearrange("p a b -> p (a b)")[:, 0:8].rearrange("p (o t) -> p o t", o=2)
         nc.sync.dma_start(out=rest_cols, in_=rest.rearrange("(o p t) -> p o t", o=2, t=4))
-        load_skin(1, 0, late_rows(GROUP))
         load_late_phase(0, 1)
-        load_skin(0, 1, late_rows(GROUP))
+        load_skin(1, 0, late_rows(GROUP))
         load_late_phase(1, 1)
-        load_skin(1, 1, late_rows(GROUP))
+        load_skin(0, 1, late_rows(GROUP))
         load_late_phase(0, 2)
+        load_skin(1, 1, late_rows(GROUP))
         load_late_phase(1, 2)
 
         nc.vector.tensor_copy(v_c[0][:], tab_w[0][:].bitcast(U32).indirect(idx[:]))
@@ -187,8 +191,7 @@ def tile_list_keyframe_blend_skinning_kernel(
             load_phase(g, 3, staged([P, 4, PHASE_COLS], F32, "phase_last%d" % g, "tab_area%d" % g)[:])
         w1_b1 = round_and_deal(w1_raw1)
 
-        def b_product(g, cc, t0, nt):
-            j0, w = CHUNKS[cc]
+        def b_product(g, j0, w, t0, nt):
             b_ps = psum.tile([P, nt, w], F32, name="b_ps")
             for e in range(nt):
                 m0 = (t0 + e) * P
@@ -203,8 +206,7 @@ def tile_list_keyframe_blend_skinning_kernel(
                 )
             return b_ps
 
-        def a_product(g, cc, t0, nt):
-            j0, w = CHUNKS[cc]
+        def a_product(g, j0, w, t0, nt):
             a_ps = psum.tile([P, nt, w], F32, name="a_ps")
             for e in range(nt):
                 for n0 in range(0, w, W4_COLS):
@@ -222,14 +224,13 @@ def tile_list_keyframe_blend_skinning_kernel(
                         )
             return a_ps
 
-        def blend_terms(g, cc, half):
-            j0, w = CHUNKS[cc]
+        def blend_terms(g, j0, w, half):
             part, p0 = divmod(j0, PHASE_COLS)
             if half == 0:
                 b_term = ring.tile([P, 4 * w], F32, name="b_term")
                 a_term = ring.tile([P, 4 * w], F32, name="a_term")
-                terms[g, cc] = (b_term, a_term)
-            b_term, a_term = terms[g, cc]
+                terms[g, j0] = (b_term, a_term)
+            b_term, a_term = terms[g, j0]
             nt = BANK // w
             order = "p t j -> p j t" if nt == 2 else "p t j -> p t j"
             jobs = [(kind, t0) for t0 in range(0, 4, nt) for kind in "ba"]
@@ -241,54 +242,58 @@ def tile_list_keyframe_blend_skinning_kernel(
                 if kind == "b":
                     nc.vector.tensor_tensor(
                         b_term[:, cols].rearrange("p (x y) -> p x y", y=inner),
-                        b_product(g, cc, t0, nt)[:].rearrange(order), ph, MULT,
+                        b_product(g, j0, w, t0, nt)[:].rearrange(order), ph, MULT,
                     )
                 else:
                     nc.vector.scalar_tensor_tensor(
                         a_term[:, cols].rearrange("p (x y) -> p x y", y=inner),
-                        ph, 1.0, a_product(g, cc, t0, nt)[:].rearrange(order), SUB, MULT,
+                        ph, 1.0, a_product(g, j0, w, t0, nt)[:].rearrange(order), SUB, MULT,
                     )
 
-        def blend_sum(g, cc):
-            w = CHUNKS[cc][1]
-            b_term, a_term = terms[g, cc]
+        def blend_sum(g, j0, w):
+            b_term, a_term = terms[g, j0]
             if BANK // w == 2:
-                h_b[g, cc] = ring.tile([P, w, 4], BF16, name="h_wide", align_bytes=64, bufs=1)
-                for engine, cols in ((nc.gpsimd, slice(0, POOL_COLS)), (nc.vector, slice(POOL_COLS, w))):
+                h_b[g, j0] = ring.tile([P, w, 4], BF16, name="h_wide", align_bytes=64, bufs=1)
+                share = POOL_COLS_LAST if j0 + w == S else POOL_COLS
+                for engine, cols in ((nc.gpsimd, slice(0, share)), (nc.vector, slice(share, w))):
                     engine.tensor_tensor(
-                        h_b[g, cc][:, cols, :].rearrange("p j (u e) -> p j u e", e=2),
+                        h_b[g, j0][:, cols, :].rearrange("p j (u e) -> p j u e", e=2),
                         b_term[:].rearrange("p (u j e) -> p j u e", u=2, e=2)[:, cols],
                         a_term[:].rearrange("p (u j e) -> p j u e", u=2, e=2)[:, cols],
                         SUB,
                     )
                 return
-            h_b[g, cc] = ring.tile([P, w, 4], BF16, name="h_b", align_bytes=64)
+            h_b[g, j0] = ring.tile([P, w, 4], BF16, name="h_b", align_bytes=64)
             nc.vector.tensor_tensor(
-                h_b[g, cc][:].rearrange("p (c i) t -> p c t i", i=4),
+                h_b[g, j0][:].rearrange("p (c i) t -> p c t i", i=4),
                 b_term[:].rearrange("p (t c i) -> p c t i", t=4, i=4),
                 a_term[:].rearrange("p (t c i) -> p c t i", t=4, i=4),
                 SUB,
             )
 
-        def quantise_h(g, cc):
-            w = CHUNKS[cc][1]
-            following = (1 - g, cc + g)
+        def quantise_h(g, j0, w):
+            following = (1 - g, j0 // PHASE_COLS + g)
+            name = "h_c%d_%d" % (g, j0)
             if following in phase_offset:
-                h_c[g, cc] = late.tile(
-                    [P, w], U32, name="h_c%d%d" % (g, cc), align_bytes=64, offset=phase_offset[following]
-                )
+                codes = late.tile([P, w], U32, name=name, align_bytes=64, offset=phase_offset[following])
+            elif following == (0, 3):
+                codes = staged([P, w], U32, name, "tab_area0")
             else:
-                h_c[g, cc] = held([P, w], U32, "h_c%d%d" % (g, cc))
-            h_s[g, cc] = held([P, w], U8, "h_s%d%d" % (g, cc))
-            quantise(h_c[g, cc][:], h_s[g, cc][:], h_b[g, cc][:].rearrange("p j t -> p (j t)"))
+                codes = held([P, w], U32, name)
+            scales = held([P, w], U8, "h_s%d_%d" % (g, j0))
+            quantise(codes[:], scales[:], h_b[g, j0][:].rearrange("p j t -> p (j t)"))
+            for cc, (first, width) in enumerate(CHUNKS):
+                if j0 <= first < j0 + w:
+                    h_c[g, cc] = codes[:, first - j0 : first - j0 + width]
+                    h_s[g, cc] = scales[:, first - j0 : first - j0 + width]
 
         def y_pass(y_ps, cc, o, g, t, k, start, stop):
             nc.tensor.matmul_mx(
                 out=y_ps[:, k, :],
                 lhsT=skin_c[g][o][:, t * P : (t + 1) * P].bitcast(FP8X4),
                 lhsT_scale=skin_s[g][o][:, t * P : (t + 1) * P],
-                rhs=h_c[g, cc][:].bitcast(FP8X4),
-                rhs_scale=h_s[g, cc][:],
+                rhs=h_c[g, cc].bitcast(FP8X4),
+                rhs_scale=h_s[g, cc],
                 start=start,
                 stop=stop,
             )
@@ -304,7 +309,7 @@ def tile_list_keyframe_blend_skinning_kernel(
             j0, w = CHUNKS[cc]
             last_chunk = cc == len(CHUNKS) - 1
             per_bank = BANK // w
-            y = ring.tile([P, 4, w], F32, name="y", bufs=4)
+            y = ring.tile([P, 4, w], F32, name="y", bufs=5)
             for t0 in range(0, 4, per_bank):
                 if last_chunk:
                     last_y_passes(o, 1)
@@ -328,8 +333,16 @@ def tile_list_keyframe_blend_skinning_kernel(
             nc.sync.dma_start(
                 out=out_0[o * GROUP : (o + 1) * GROUP, j0 : j0 + w].rearrange("(p t) j -> p t j", t=4), in_=y[:]
             )
-            y_b[cc, o] = ring.tile([P, w, 4], BF16, name="y_b", align_bytes=64, bufs=4)
-            copy = nc.vector.tensor_copy if last_chunk else nc.scalar.copy
+            y_f[cc, o] = y
+            if cc < VECTOR_ROUNDS_FROM:
+                round_y(cc, o, nc.scalar.copy)
+            elif last_chunk:
+                round_y(cc, o, nc.vector.tensor_copy)
+
+        def round_y(cc, o, copy):
+            w = CHUNKS[cc][1]
+            y = y_f[cc, o]
+            y_b[cc, o] = ring.tile([P, w, 4], BF16, name="y_b", align_bytes=64, bufs=6)
             copy(
                 out=y_b[cc, o][:].rearrange("p (c i) t -> p c t i", i=4),
                 in_=y[:].rearrange("p t (c i) -> p c t i", i=4),
@@ -338,7 +351,7 @@ def tile_list_keyframe_blend_skinning_kernel(
         def quantise_y(cc, o):
             j0, w = CHUNKS[cc]
             if o == 0:
-                y_c[cc] = ring.tile([P, 2 * w], I32, name="y_c", align_bytes=64)
+                y_c[cc] = ring.tile([P, 2 * w], I32, name="y_c", align_bytes=64, bufs=4)
             quantise(
                 y_c[cc][:, o * w : (o + 1) * w],
                 y_s[:, o * S + j0 : o * S + j0 + w],
@@ -350,24 +363,33 @@ def tile_list_keyframe_blend_skinning_kernel(
                     in_=y_c[cc][:].rearrange("p (o j) -> p o j", o=2),
                 )
 
-        blends = [(g, cc) for cc in range(len(CHUNKS)) for g in range(2)]
+        blends = BLENDS
 
         def product_step(cc, o):
-            return max(2 * cc + 2 + o, SKIN_PARTS.index((1, o)) + SKIN_LAG)
+            return max(blends.index((1,) + CHUNKS[cc]) + 1 + o, SKIN_PARTS.index((1, o)) + SKIN_FIRST + SKIN_LAG)
 
         def other_quantisers(s):
             if s == 0:
                 quantise(w1_c[1][:], w1_s[1][:], w1_b1[:])
-            if 0 <= s - SKIN_LAG < len(SKIN_PARTS):
-                g, o = SKIN_PARTS[s - SKIN_LAG]
+            if 0 <= s - SKIN_FIRST - SKIN_LAG < len(SKIN_PARTS):
+                g, o = SKIN_PARTS[s - SKIN_FIRST - SKIN_LAG]
+                part = (blends[s][0], blends[s][1] // PHASE_COLS)
+                skin_c[g][o] = late.tile(
+                    [P, GROUP], U32, name="skin_c%d%d" % (g, o), align_bytes=64,
+                    offset=phase_offset[part] + 4 * PHASE_COLS,
+                )
                 quantise(skin_c[g][o][:], skin_s[g][o][:], skin_b[g, o][:])
+            for cc in range(VECTOR_ROUNDS_FROM, len(CHUNKS) - 1):
+                for o in range(2):
+                    if s == product_step(cc, o) + Y_LAG - 1:
+                        round_y(cc, o, nc.vector.tensor_copy)
             for cc in range(len(CHUNKS)):
                 for o in range(2):
                     if s == product_step(cc, o) + Y_LAG:
                         quantise_y(cc, o)
 
         for s in range(product_step(len(CHUNKS) - 1, 1) + Y_LAG + 1):
-            shared = 1 <= s <= len(blends) and CHUNKS[blends[s - 1][1]][1] > POOL_COLS
+            shared = 1 <= s <= len(blends) and blends[s - 1][2] > POOL_COLS
             if s < len(blends):
                 blend_terms(*blends[s], 0)
             if 1 <= s <= len(blends) and not shared:
@@ -384,8 +406,8 @@ def tile_list_keyframe_blend_skinning_kernel(
                     last_y_passes(o, 0)
             if not shared:
                 other_quantisers(s)
-            if s < len(SKIN_PARTS):
-                skin_b[SKIN_PARTS[s]] = round_and_deal(skin_raw[SKIN_PARTS[s]])
+            if 0 <= s - SKIN_FIRST < len(SKIN_PARTS):
+                skin_b[SKIN_PARTS[s - SKIN_FIRST]] = round_and_deal(skin_raw[SKIN_PARTS[s - SKIN_FIRST]])
             for cc in range(len(CHUNKS)):
                 for o in range(2):
                     if s == product_step(cc, o):

@@ -21,16 +21,17 @@ GROUP = 512
 BANK = 512
 W4_COLS = 128
 
-CHUNKS = [(0, 256), (256, 256), (512, 256), (768, 128), (896, 128)]
+CHUNKS = [(0, 512), (512, 256), (768, 128), (896, 128)]
 PHASE_COLS = 256
 SKIN_PARTS = [(0, 0), (1, 0), (0, 1), (1, 1)]
-SKIN_LAG = 1
-Y_LAG = 3
-VECTOR_ROUNDS_FROM = 2
-SKIN_FIRST = 1
+PROMPT = 8
+W1_STEP = 1
+SKIN_STEP = 3
+SCALAR_ROUNDS = 3
 POOL_COLS = 192
 POOL_COLS_LAST = 96
-BLENDS = [(g, j0, 256) for j0 in (0, 256, 512) for g in range(2)] + [(0, 768, 256), (1, 768, 128), (1, 896, 128)]
+BLENDS = [(g, j0, 256) for g in range(2) for j0 in (0, 256)]
+BLENDS = BLENDS + [(0, 512, 256), (1, 512, 256), (0, 768, 256), (1, 768, 128), (1, 896, 128)]
 
 FLOPS = 2 * S * (K * H + K2 * H + H * N)
 
@@ -44,37 +45,39 @@ def tile_list_keyframe_blend_skinning_kernel(
         keep = ctx.enter_context(tc.tile_pool(name="keep", bufs=1))
         ring = ctx.enter_context(tc.tile_pool(name="ring", bufs=3))
         psum = ctx.enter_context(tc.psum_pool(name="psum", bufs=2))
-        late = ctx.enter_context(tc.tile_pool(name="late", bufs=1))
+        shared = ctx.enter_context(tc.tile_pool(name="shared", bufs=1))
 
         def held(shape, dtype, name):
             return keep.tile(shape, dtype, name=name, align_bytes=64)
 
-        def staged(shape, dtype, name, area):
-            return keep.tile(shape, dtype, name=name, tag=area, align_bytes=64)
+        def placed(shape, dtype, name, offset):
+            return shared.tile(shape, dtype, name=name, align_bytes=64, offset=offset)
 
         idx = held([P, S // 16], U16, "idx")
         idx2 = held([P, S // 16], U16, "idx2")
         late_bytes = 16 * (5 * GROUP + 6 * PHASE_COLS + 4)
-        tab_s_area = late.tile([P, late_bytes], U8, name="tab_s_area", align_bytes=64, offset=0)
+        tab_s_area = placed([P, late_bytes], U8, "tab_s_area", 0)
         tab_s = tab_s_area[:, 0:T]
+        tab_at = late_bytes
+        tab_w = [placed([P, T], I32, "tab_w%d" % a, tab_at + 4 * T * a) for a in range(2)]
+        early_at = tab_at + 8 * T
+        tab2_w = placed([P, T2], I32, "tab2_w", early_at)
+        w1_raw0 = placed([P, 4, GROUP], F32, "w1_raw0", early_at + 4 * T2)
+        tab2_s = placed([P, T2], U8, "tab2_s", early_at + 4 * T2 + 16 * GROUP)
+        w4_raw = placed([P, 4 * H], U8, "w4_raw", early_at + 5 * T2 + 16 * GROUP)
         w4_s_raw = held([P, 2 * H], U8, "w4_s_raw")
-        w4_raw = held([P, 4 * H], U8, "w4_raw")
-        tab_w = [staged([P, T], I32, "tab_w%d" % a, "tab_area%d" % a) for a in range(2)]
-        tab2_s = held([P, T2], U8, "tab2_s")
-        w1_raw0 = held([P, 4, GROUP], F32, "w1_raw0")
-        tab2_w = held([P, T2], I32, "tab2_w")
         w4_c = held([P, 4 * H], U8, "w4_c")
         w4_s = held([P, 2 * H], U8, "w4_s")
         v_s = [held([P, S], U8, "v_s%d" % a) for a in range(2)]
         v2_s = held([P, S], U8, "v2_s")
         v_c = [held([P, S], U32, "v_c%d" % a) for a in range(2)]
         v2_c = held([P, S], U32, "v2_c")
-        w1_c = [held([P, GROUP], U32, "w1_c%d" % g) for g in range(2)]
+        w1_c = [held([P, GROUP], U32, "w1_c0"), None]
         w1_s = [held([P, GROUP], U8, "w1_s%d" % g) for g in range(2)]
         skin_c = [[None, None], [None, None]]
         skin_s = [[held([P, GROUP], U8, "skin_s%d%d" % (g, o)) for o in range(2)] for g in range(2)]
         y_s = held([P, 2 * S], U8, "y_s")
-        phase_raw, skin_raw, skin_b, y_f = {}, {}, {}, {}
+        phase_raw, skin_raw, skin_b, y_f, y_r = {}, {}, {}, {}, {}
         terms, h_b, h_c, h_s, y_b, y_c, last_ps = {}, {}, {}, {}, {}, {}, {}
 
         nc.gpsimd.memset(tab_s.bitcast(I32), 0)
@@ -95,17 +98,18 @@ def tile_list_keyframe_blend_skinning_kernel(
                     in_=scales[:, i:16:4, :].bitcast(I32).rearrange("a q c -> q a c"),
                 )
 
-        def load_phase(g, part, place):
-            phase_raw[g, part] = place
-            load_rows(place, phase[g * GROUP : (g + 1) * GROUP, part * PHASE_COLS : (part + 1) * PHASE_COLS])
+        def load_phase(g, j0, w, place):
+            phase_raw[g, j0] = place
+            load_rows(place, phase[g * GROUP : (g + 1) * GROUP, j0 : j0 + w])
 
         def load_skin(g, o, place):
             skin_raw[g, o] = place
             load_rows(place, skin[g * GROUP : (g + 1) * GROUP, o * GROUP : (o + 1) * GROUP])
 
-        def round_and_deal(raw):
-            dealt = ring.tile([P, 4 * GROUP], BF16, name="dealt", align_bytes=64)
-            nc.scalar.copy(
+        def round_and_deal(raw, copy=nc.scalar.copy, dealt=None):
+            if dealt is None:
+                dealt = ring.tile([P, 4 * GROUP], BF16, name="dealt", align_bytes=64)
+            copy(
                 out=dealt[:].rearrange("p (u e m i) -> p m u i e", u=2, e=2, i=4),
                 in_=raw.rearrange("p i (m u e) -> p m u i e", u=2, e=2),
             )
@@ -129,9 +133,8 @@ def tile_list_keyframe_blend_skinning_kernel(
         load_planes(tab2_s, tab2_scales, range(0, 2))
         load_rows(w1_raw0[:], w1[:, 0:GROUP])
         load_planes(tab2_s, tab2_scales, range(2, 4))
-        load_planes(w4_s_raw, w4_scales, range(0, 1))
+        load_planes(w4_s_raw, w4_scales, range(0, 4))
         load_words(tab2_w, tab2_words[0])
-        load_planes(w4_s_raw, w4_scales, range(1, 4))
         load_words(tab_w[1], tab_words[1])
 
         nc.vector.tensor_copy(
@@ -151,27 +154,27 @@ def tile_list_keyframe_blend_skinning_kernel(
         def late_rows(width):
             first = 16 * sum(late_places)
             late_places.append(width)
-            place = late.tile([P, 4, width], F32, name="late%d" % len(late_places), align_bytes=64, offset=first)
+            place = placed([P, 4, width], F32, "late%d" % len(late_places), first)
             return place[:]
 
         def load_late_phase(g, part):
-            phase_offset[g, part] = 16 * sum(late_places)
-            load_phase(g, part, late_rows(PHASE_COLS))
+            phase_offset[g, part * PHASE_COLS] = 16 * sum(late_places)
+            load_phase(g, part * PHASE_COLS, PHASE_COLS, late_rows(PHASE_COLS))
 
         load_late_phase(0, 0)
+        load_late_phase(0, 1)
         w1_raw1 = late_rows(GROUP)
         load_rows(w1_raw1, w1[:, GROUP : 2 * GROUP])
         load_late_phase(1, 0)
         load_skin(0, 0, late_rows(GROUP))
         rest_cols = late_rows(4).rearrange("p a b -> p (a b)")[:, 0:8].rearrange("p (o t) -> p o t", o=2)
         nc.sync.dma_start(out=rest_cols, in_=rest.rearrange("(o p t) -> p o t", o=2, t=4))
-        load_late_phase(0, 1)
-        load_skin(1, 0, late_rows(GROUP))
         load_late_phase(1, 1)
-        load_skin(0, 1, late_rows(GROUP))
+        load_skin(1, 0, late_rows(GROUP))
         load_late_phase(0, 2)
-        load_skin(1, 1, late_rows(GROUP))
+        load_skin(0, 1, late_rows(GROUP))
         load_late_phase(1, 2)
+        load_skin(1, 1, late_rows(GROUP))
 
         nc.vector.tensor_copy(v_c[0][:], tab_w[0][:].bitcast(U32).indirect(idx[:]))
         nc.vector.tensor_copy(v2_s[:], tab2_s[:].indirect(idx2[:]))
@@ -187,8 +190,9 @@ def tile_list_keyframe_blend_skinning_kernel(
                 tab_w[1][:].bitcast(U32).indirect(idx[:, j0 // 16 : (j0 + S // 2) // 16]),
             )
 
-        for g in range(2):
-            load_phase(g, 3, staged([P, 4, PHASE_COLS], F32, "phase_last%d" % g, "tab_area%d" % g)[:])
+        for n, (g, j0, w) in enumerate(BLENDS[-3:]):
+            phase_offset[g, j0] = tab_at + (0, 4 * T, 6 * T)[n]
+            load_phase(g, j0, w, placed([P, 4, w], F32, "phase_last%d" % n, phase_offset[g, j0])[:])
         w1_b1 = round_and_deal(w1_raw1)
 
         def b_product(g, j0, w, t0, nt):
@@ -225,7 +229,6 @@ def tile_list_keyframe_blend_skinning_kernel(
             return a_ps
 
         def blend_terms(g, j0, w, half):
-            part, p0 = divmod(j0, PHASE_COLS)
             if half == 0:
                 b_term = ring.tile([P, 4 * w], F32, name="b_term")
                 a_term = ring.tile([P, 4 * w], F32, name="a_term")
@@ -237,7 +240,7 @@ def tile_list_keyframe_blend_skinning_kernel(
             for kind, t0 in jobs[half * len(jobs) // 2 : (half + 1) * len(jobs) // 2]:
                 rows = slice(t0, t0 + nt)
                 cols = slice(t0 * w, (t0 + nt) * w)
-                ph = phase_raw[g, part][:, rows, p0 : p0 + w].rearrange(order)
+                ph = phase_raw[g, j0][:, rows, :].rearrange(order)
                 inner = 2 if nt == 2 else w
                 if kind == "b":
                     nc.vector.tensor_tensor(
@@ -253,9 +256,14 @@ def tile_list_keyframe_blend_skinning_kernel(
         def blend_sum(g, j0, w):
             b_term, a_term = terms[g, j0]
             if BANK // w == 2:
-                h_b[g, j0] = ring.tile([P, w, 4], BF16, name="h_wide", align_bytes=64, bufs=1)
+                if (g, j0, w) != BLENDS[PROMPT]:
+                    h_b[g, j0] = ring.tile([P, w, 4], BF16, name="h_wide", align_bytes=64, bufs=1)
                 share = POOL_COLS_LAST if j0 + w == S else POOL_COLS
-                for engine, cols in ((nc.gpsimd, slice(0, share)), (nc.vector, slice(share, w))):
+                shares = ((nc.gpsimd, slice(0, share)), (nc.vector, slice(share, w)))
+                if (g, j0, w) == BLENDS[PROMPT]:
+                    h_b[g, j0] = held([P, w, 4], BF16, "h_prompt")
+                    shares = ((nc.vector, slice(0, w)),)
+                for engine, cols in shares:
                     engine.tensor_tensor(
                         h_b[g, j0][:, cols, :].rearrange("p j (u e) -> p j u e", e=2),
                         b_term[:].rearrange("p (u j e) -> p j u e", u=2, e=2)[:, cols],
@@ -271,29 +279,30 @@ def tile_list_keyframe_blend_skinning_kernel(
                 SUB,
             )
 
-        def quantise_h(g, j0, w):
-            following = (1 - g, j0 // PHASE_COLS + g)
+        def behind_terms(s, name, width, at):
+            g, j0, w = BLENDS[s]
+            return placed([P, width], U32, name, phase_offset[g, j0] + at)
+
+        def quantise_h(s):
+            g, j0, w = BLENDS[s]
             name = "h_c%d_%d" % (g, j0)
-            if following in phase_offset:
-                codes = late.tile([P, w], U32, name=name, align_bytes=64, offset=phase_offset[following])
-            elif following == (0, 3):
-                codes = staged([P, w], U32, name, "tab_area0")
+            if s + 1 < len(BLENDS):
+                codes = behind_terms(s + 1, name, w, 0)
             else:
                 codes = held([P, w], U32, name)
             scales = held([P, w], U8, "h_s%d_%d" % (g, j0))
             quantise(codes[:], scales[:], h_b[g, j0][:].rearrange("p j t -> p (j t)"))
-            for cc, (first, width) in enumerate(CHUNKS):
-                if j0 <= first < j0 + w:
-                    h_c[g, cc] = codes[:, first - j0 : first - j0 + width]
-                    h_s[g, cc] = scales[:, first - j0 : first - j0 + width]
+            for first in range(j0, j0 + w, P):
+                h_c[g, first] = (codes, scales, first - j0)
 
-        def y_pass(y_ps, cc, o, g, t, k, start, stop):
+        def y_pass(place, j0, w, o, g, t, start, stop):
+            codes, scales, c0 = h_c[g, j0]
             nc.tensor.matmul_mx(
-                out=y_ps[:, k, :],
+                out=place,
                 lhsT=skin_c[g][o][:, t * P : (t + 1) * P].bitcast(FP8X4),
                 lhsT_scale=skin_s[g][o][:, t * P : (t + 1) * P],
-                rhs=h_c[g, cc].bitcast(FP8X4),
-                rhs_scale=h_s[g, cc],
+                rhs=codes[:, c0 : c0 + w].bitcast(FP8X4),
+                rhs_scale=scales[:, c0 : c0 + w],
                 start=start,
                 stop=stop,
             )
@@ -303,13 +312,13 @@ def tile_list_keyframe_blend_skinning_kernel(
             if g == 0:
                 last_ps[o] = psum.tile([P, 4, CHUNKS[cc][1]], F32, name=("b_ps", "a_ps")[o])
             for t in range(4):
-                y_pass(last_ps[o], cc, o, g, t, t, g == 0 and t == 0, g == 1 and t == 3)
+                y_pass(last_ps[o][:, t, :], *CHUNKS[cc], o, g, t, g == 0 and t == 0, g == 1 and t == 3)
 
         def skin_product(cc, o):
             j0, w = CHUNKS[cc]
             last_chunk = cc == len(CHUNKS) - 1
             per_bank = BANK // w
-            y = ring.tile([P, 4, w], F32, name="y", bufs=5)
+            y = placed([P, 4, w], F32, "y%d%d" % (cc, o), early_at + 16 * (2 * j0 + o * w))
             for t0 in range(0, 4, per_bank):
                 if last_chunk:
                     last_y_passes(o, 1)
@@ -317,8 +326,10 @@ def tile_list_keyframe_blend_skinning_kernel(
                 else:
                     y_ps = psum.tile([P, per_bank, w], F32, name="y_ps", bufs=4)
                     for k in range(per_bank):
-                        for g in range(2):
-                            y_pass(y_ps, cc, o, g, t0 + k, k, g == 0, g == 1)
+                        for c0 in range(0, w, PHASE_COLS):
+                            n = min(w, PHASE_COLS)
+                            for g in range(2):
+                                y_pass(y_ps[:, k, c0 : c0 + n], j0 + c0, n, o, g, t0 + k, g == 0, g == 1)
                 if last_chunk and o == 1:
                     nc.vector.tensor_tensor(
                         y[:, t0 : t0 + per_bank, :],
@@ -330,88 +341,128 @@ def tile_list_keyframe_blend_skinning_kernel(
                     for k in range(per_bank):
                         t = t0 + k
                         nc.scalar.activation(y[:, t, :], y_ps[:, k, :], IDENT, bias=rest_cols[:, o, t : t + 1])
-            nc.sync.dma_start(
-                out=out_0[o * GROUP : (o + 1) * GROUP, j0 : j0 + w].rearrange("(p t) j -> p t j", t=4), in_=y[:]
-            )
+            rows = out_0[o * GROUP : (o + 1) * GROUP, j0 : j0 + w].rearrange("(p t) j -> p t j", t=4)
+            per_store = 2 if (cc, o) == (0, 1) else 4
+            for t0 in range(0, 4, per_store):
+                nc.sync.dma_start(out=rows[:, t0 : t0 + per_store, :], in_=y[:, t0 : t0 + per_store, :])
             y_f[cc, o] = y
-            if cc < VECTOR_ROUNDS_FROM:
-                round_y(cc, o, nc.scalar.copy)
-            elif last_chunk:
-                round_y(cc, o, nc.vector.tensor_copy)
 
-        def round_y(cc, o, copy):
-            w = CHUNKS[cc][1]
-            y = y_f[cc, o]
-            y_b[cc, o] = ring.tile([P, w, 4], BF16, name="y_b", align_bytes=64, bufs=6)
+        def round_y(cc, o, c0, copy, place=None):
+            w = min(CHUNKS[cc][1], PHASE_COLS)
+            if place is None:
+                if c0 == 0:
+                    y_b[cc, o] = held([P, CHUNKS[cc][1], 4], BF16, "y_b%d%d" % (cc, o))
+                place = y_b[cc, o][:, c0 : c0 + w, :]
+            y_r[cc, o, c0] = place
             copy(
-                out=y_b[cc, o][:].rearrange("p (c i) t -> p c t i", i=4),
-                in_=y[:].rearrange("p t (c i) -> p c t i", i=4),
+                out=place.rearrange("p (c i) t -> p c t i", i=4),
+                in_=y_f[cc, o][:, :, c0 : c0 + w].rearrange("p t (c i) -> p c t i", i=4),
             )
 
-        def quantise_y(cc, o):
+        def quantise_y(cc, o, c0, n, values):
             j0, w = CHUNKS[cc]
-            if o == 0:
-                y_c[cc] = ring.tile([P, 2 * w], I32, name="y_c", align_bytes=64, bufs=4)
+            half, at = divmod(j0 + c0, GROUP)
+            if half not in y_c:
+                y_c[half] = held([P, 2, GROUP], I32, "y_c%d" % half)
             quantise(
-                y_c[cc][:, o * w : (o + 1) * w],
-                y_s[:, o * S + j0 : o * S + j0 + w],
-                y_b[cc, o][:].rearrange("p j t -> p (j t)"),
+                y_c[half][:, o, at : at + n],
+                y_s[:, o * S + j0 + c0 : o * S + j0 + c0 + n],
+                values.rearrange("p j t -> p (j t)"),
             )
-            if o == 1:
-                nc.sync.dma_start(
-                    out=out_1[:, :, j0 : j0 + w, :].rearrange("o p j t -> p o (j t)").bitcast(I32),
-                    in_=y_c[cc][:].rearrange("p (o j) -> p o j", o=2),
-                )
+            words = out_1[:, :, half * GROUP : (half + 1) * GROUP, :].rearrange("o p j t -> p o (j t)").bitcast(I32)
+            if half == 0 and at + n == GROUP:
+                nc.sync.dma_start(out=words[:, o, :], in_=y_c[half][:, o, :])
+            elif at + n == GROUP and o == 1:
+                nc.sync.dma_start(out=words, in_=y_c[half][:])
 
-        blends = BLENDS
+        def terms_of(s):
+            for half in range(2):
+                blend_terms(*BLENDS[s], half)
 
-        def product_step(cc, o):
-            return max(blends.index((1,) + CHUNKS[cc]) + 1 + o, SKIN_PARTS.index((1, o)) + SKIN_FIRST + SKIN_LAG)
+        def round_skin(g, o, copy=nc.scalar.copy):
+            skin_b[g, o] = round_and_deal(skin_raw[g, o], copy)
 
-        def other_quantisers(s):
-            if s == 0:
-                quantise(w1_c[1][:], w1_s[1][:], w1_b1[:])
-            if 0 <= s - SKIN_FIRST - SKIN_LAG < len(SKIN_PARTS):
-                g, o = SKIN_PARTS[s - SKIN_FIRST - SKIN_LAG]
-                part = (blends[s][0], blends[s][1] // PHASE_COLS)
-                skin_c[g][o] = late.tile(
-                    [P, GROUP], U32, name="skin_c%d%d" % (g, o), align_bytes=64,
-                    offset=phase_offset[part] + 4 * PHASE_COLS,
-                )
-                quantise(skin_c[g][o][:], skin_s[g][o][:], skin_b[g, o][:])
-            for cc in range(VECTOR_ROUNDS_FROM, len(CHUNKS) - 1):
-                for o in range(2):
-                    if s == product_step(cc, o) + Y_LAG - 1:
-                        round_y(cc, o, nc.vector.tensor_copy)
-            for cc in range(len(CHUNKS)):
-                for o in range(2):
-                    if s == product_step(cc, o) + Y_LAG:
-                        quantise_y(cc, o)
+        def quantise_skin(g, o, s):
+            if s is None:
+                skin_c[g][o] = held([P, GROUP], U32, "skin_c%d%d" % (g, o))
+            else:
+                skin_c[g][o] = behind_terms(s, "skin_c%d%d" % (g, o), GROUP, 4 * PHASE_COLS)
+            quantise(skin_c[g][o][:], skin_s[g][o][:], skin_b[g, o][:])
 
-        for s in range(product_step(len(CHUNKS) - 1, 1) + Y_LAG + 1):
-            shared = 1 <= s <= len(blends) and blends[s - 1][2] > POOL_COLS
-            if s < len(blends):
-                blend_terms(*blends[s], 0)
-            if 1 <= s <= len(blends) and not shared:
-                blend_sum(*blends[s - 1])
-            if s < len(blends):
-                blend_terms(*blends[s], 1)
-            if shared:
-                blend_sum(*blends[s - 1])
-                other_quantisers(s)
-            if 1 <= s <= len(blends):
-                quantise_h(*blends[s - 1])
-            if s == len(blends) - 1:
-                for o in range(2):
-                    last_y_passes(o, 0)
-            if not shared:
-                other_quantisers(s)
-            if 0 <= s - SKIN_FIRST < len(SKIN_PARTS):
-                skin_b[SKIN_PARTS[s - SKIN_FIRST]] = round_and_deal(skin_raw[SKIN_PARTS[s - SKIN_FIRST]])
-            for cc in range(len(CHUNKS)):
-                for o in range(2):
-                    if s == product_step(cc, o):
-                        skin_product(cc, o)
+        terms_of(0)
+        terms_of(1)
+        blend_sum(*BLENDS[0])
+        w1_c[1] = behind_terms(1, "w1_c1", GROUP, 4 * PHASE_COLS)
+        quantise(w1_c[1][:], w1_s[1][:], w1_b1[:])
+        quantise_h(0)
+        round_skin(0, 0)
+
+        terms_of(2)
+        blend_sum(*BLENDS[1])
+        quantise_h(1)
+        round_skin(1, 0)
+
+        terms_of(3)
+        blend_sum(*BLENDS[2])
+        quantise_skin(0, 0, 3)
+        quantise_h(2)
+        round_skin(0, 1)
+
+        terms_of(4)
+        blend_sum(*BLENDS[3])
+        quantise_skin(1, 0, 4)
+        quantise_h(3)
+        skin_product(0, 0)
+
+        terms_of(5)
+        blend_sum(*BLENDS[4])
+        round_skin(1, 1, nc.vector.tensor_copy)
+        quantise_skin(0, 1, 5)
+        quantise_h(4)
+        quantise_skin(1, 1, None)
+        round_y(0, 0, 0, nc.scalar.copy)
+        round_y(0, 0, 256, nc.scalar.copy)
+        skin_product(0, 1)
+
+        terms_of(6)
+        blend_sum(*BLENDS[5])
+        quantise_y(0, 0, 0, 512, y_b[0, 0][:])
+        quantise_h(5)
+        round_y(0, 1, 0, nc.scalar.copy)
+        skin_product(1, 0)
+        skin_product(1, 1)
+
+        terms_of(7)
+        blend_sum(*BLENDS[6])
+        quantise_h(6)
+        round_y(0, 1, 256, nc.scalar.copy, behind_terms(6, "y_late", 512, 0)[:].bitcast(BF16).rearrange("p (j t) -> p j t", t=4))
+
+        blend_terms(*BLENDS[8], 0)
+        blend_sum(*BLENDS[7])
+        blend_terms(*BLENDS[8], 1)
+        quantise_h(7)
+        for o in range(2):
+            last_y_passes(o, 0)
+        skin_product(2, 0)
+        skin_product(2, 1)
+
+        blend_sum(*BLENDS[8])
+        quantise_y(0, 1, 0, 256, y_r[0, 1, 0])
+        quantise_h(8)
+        skin_product(3, 0)
+        quantise_y(0, 1, 256, 256, y_r[0, 1, 256])
+        round_y(1, 0, 0, nc.vector.tensor_copy)
+        skin_product(3, 1)
+        round_y(1, 1, 0, nc.vector.tensor_copy)
+        round_y(2, 0, 0, nc.scalar.copy)
+        round_y(2, 1, 0, nc.scalar.copy)
+        for o in range(2):
+            quantise_y(1, o, 0, 256, y_r[1, o, 0])
+        for o in range(2):
+            round_y(3, o, 0, nc.vector.tensor_copy)
+        for cc in (2, 3):
+            for o in range(2):
+                quantise_y(cc, o, 0, 128, y_r[cc, o, 0])
 
         for i in range(4):
             queue = nc.sync if i % 2 == 0 else nc.scalar

@@ -28,7 +28,7 @@ PROMPT = 8
 W1_STEP = 1
 SKIN_STEP = 3
 SCALAR_ROUNDS = 3
-POOL_COLS = 192
+POOL_COLS = 160
 POOL_COLS_LAST = 96
 BLENDS = [(g, j0, 256) for g in range(2) for j0 in (0, 256)]
 BLENDS = BLENDS + [(0, 512, 256), (1, 512, 256), (0, 768, 256), (1, 768, 128), (1, 896, 128)]
@@ -68,8 +68,10 @@ def tile_list_keyframe_blend_skinning_kernel(
         w4_s_raw = held([P, 2 * H], U8, "w4_s_raw")
         w4_c = held([P, 4 * H], U8, "w4_c")
         w4_s = held([P, 2 * H], U8, "w4_s")
-        v_s = [held([P, S], U8, "v_s%d" % a) for a in range(2)]
-        v2_s = held([P, S], U8, "v2_s")
+        picked_s = held([P, 2 * S], U8, "picked_s")
+        moved_s = held([P, 2 * S], U8, "moved_s")
+        v_s = [picked_s[:, 0:S], moved_s[:, 0:S]]
+        v2_s = moved_s[:, S : 2 * S]
         v_c = [held([P, S], U32, "v_c%d" % a) for a in range(2)]
         v2_c = held([P, S], U32, "v2_c")
         w1_c = [held([P, GROUP], U32, "w1_c0"), None]
@@ -83,7 +85,7 @@ def tile_list_keyframe_blend_skinning_kernel(
         nc.gpsimd.memset(tab_s.bitcast(I32), 0)
         nc.vector.memset(tab2_s[:].bitcast(I32), 0)
         nc.gpsimd.memset(w4_s_raw[:].bitcast(I32), 0)
-        nc.gpsimd.memset(v_s[1][:].bitcast(I32), 0)
+        nc.gpsimd.memset(moved_s[:].bitcast(I32), 0)
 
         def load_rows(place, rows):
             nc.sync.dma_start(out=place, in_=rows.rearrange("(p t) c -> p t c", t=4))
@@ -123,16 +125,12 @@ def tile_list_keyframe_blend_skinning_kernel(
             out=w4_raw[:].bitcast(I32).rearrange("p (a c) -> p a c", a=2),
             in_=w4_words.bitcast(I32).rearrange("a p c -> p a c"),
         )
-        for i in range(4):
-            nc.sync.dma_start(
-                out=tab_s_area[i:P:16, 0:T].bitcast(I32),
-                in_=tab_scales[:, i:16:4, :].bitcast(I32).rearrange("a q c -> q a c"),
-            )
+        nc.sync.dma_start(out=tab_s_area[4:P:8, 0:T].bitcast(I32), in_=tab_scales[1].bitcast(I32))
+        load_planes(tab_s, tab_scales[0:1], range(4))
         load_words(tab_w[0], tab_words[0])
         nc.sync.dma_start(idx2[:], offs2)
-        load_planes(tab2_s, tab2_scales, range(0, 2))
+        nc.sync.dma_start(out=tab2_s[4:P:8, :].bitcast(I32), in_=tab2_scales[0].bitcast(I32))
         load_rows(w1_raw0[:], w1[:, 0:GROUP])
-        load_planes(tab2_s, tab2_scales, range(2, 4))
         load_planes(w4_s_raw, w4_scales, range(0, 4))
         load_words(tab2_w, tab2_words[0])
         load_words(tab_w[1], tab_words[1])
@@ -141,11 +139,12 @@ def tile_list_keyframe_blend_skinning_kernel(
             out=w4_c[:].bitcast(U16).rearrange("p (run t m) -> p run t m", run=4, t=4),
             in_=w4_raw[:].bitcast(U16).rearrange("p (run m t) -> p run t m", run=4, t=4),
         )
-        nc.vector.tensor_copy(v_s[0][:], tab_s.indirect(idx[:]))
+        nc.vector.tensor_copy(picked_s[:, 0:S], tab_s.indirect(idx[:]))
+        nc.vector.tensor_copy(picked_s[:, S : 2 * S], tab2_s[:].indirect(idx2[:]))
         for i in range(4):
             nc.sync.dma_start(
-                out=v_s[1][i:P:32, :].bitcast(I32),
-                in_=v_s[0][16 + i : P : 32, :].bitcast(I32),
+                out=moved_s[i:P:32, :].bitcast(I32),
+                in_=picked_s[4 + 8 * i : P : 32, :].bitcast(I32),
             )
 
         late_places = []
@@ -177,7 +176,6 @@ def tile_list_keyframe_blend_skinning_kernel(
         load_skin(1, 1, late_rows(GROUP))
 
         nc.vector.tensor_copy(v_c[0][:], tab_w[0][:].bitcast(U32).indirect(idx[:]))
-        nc.vector.tensor_copy(v2_s[:], tab2_s[:].indirect(idx2[:]))
         quantise(w1_c[0][:], w1_s[0][:], round_and_deal(w1_raw0[:])[:])
         nc.vector.tensor_copy(
             out=w4_s[:].rearrange("p (run t m) -> p run t m", run=4, t=4),

@@ -21,17 +21,14 @@ GROUP = 512
 BANK = 512
 W4_COLS = 128
 
+WIDE = 256
+NARROW = 128
+
+BLENDS = [(g, j0, WIDE) for g in range(2) for j0 in (0, 256)]
+BLENDS = BLENDS + [(0, 512, WIDE), (1, 512, WIDE), (0, 768, WIDE), (1, 768, NARROW), (1, 896, NARROW)]
 CHUNKS = [(0, 512), (512, 256), (768, 128), (896, 128)]
-PHASE_COLS = 256
-SKIN_PARTS = [(0, 0), (1, 0), (0, 1), (1, 1)]
-PROMPT = 8
-W1_STEP = 1
-SKIN_STEP = 3
-SCALAR_ROUNDS = 3
 POOL_COLS = 160
 POOL_COLS_LAST = 96
-BLENDS = [(g, j0, 256) for g in range(2) for j0 in (0, 256)]
-BLENDS = BLENDS + [(0, 512, 256), (1, 512, 256), (0, 768, 256), (1, 768, 128), (1, 896, 128)]
 
 FLOPS = 2 * S * (K * H + K2 * H + H * N)
 
@@ -55,7 +52,7 @@ def tile_list_keyframe_blend_skinning_kernel(
 
         idx = held([P, S // 16], U16, "idx")
         idx2 = held([P, S // 16], U16, "idx2")
-        late_bytes = 16 * (5 * GROUP + 6 * PHASE_COLS + 4)
+        late_bytes = 16 * (5 * GROUP + 6 * WIDE + 4)
         tab_s_area = placed([P, late_bytes], U8, "tab_s_area", 0)
         tab_s = tab_s_area[:, 0:T]
         tab_at = late_bytes
@@ -80,7 +77,7 @@ def tile_list_keyframe_blend_skinning_kernel(
         skin_s = [[held([P, GROUP], U8, "skin_s%d%d" % (g, o)) for o in range(2)] for g in range(2)]
         y_s = held([P, 2 * S], U8, "y_s")
         phase_raw, skin_raw, skin_b, y_f, y_r = {}, {}, {}, {}, {}
-        terms, h_b, h_c, h_s, y_b, y_c, last_ps = {}, {}, {}, {}, {}, {}, {}
+        terms, h_b, h_q, y_b, y_c, last_ps = {}, {}, {}, {}, {}, {}
 
         nc.gpsimd.memset(tab_s.bitcast(I32), 0)
         nc.vector.memset(tab2_s[:].bitcast(I32), 0)
@@ -93,28 +90,30 @@ def tile_list_keyframe_blend_skinning_kernel(
         def load_words(tile, words):
             nc.sync.dma_start(out=tile[:], in_=words.rearrange("p t i -> p (t i)").bitcast(I32))
 
-        def load_planes(tile, scales, live_rows):
-            for i in live_rows:
+        def load_planes(tile, scales):
+            for i in range(4):
                 nc.sync.dma_start(
                     out=tile[i:P:32, :].bitcast(I32).rearrange("q (a c) -> q a c", a=scales.shape[0]),
                     in_=scales[:, i:16:4, :].bitcast(I32).rearrange("a q c -> q a c"),
                 )
 
+        def load_spread(tile, rows):
+            nc.sync.dma_start(out=tile[4:P:8, :].bitcast(I32), in_=rows.bitcast(I32))
+
         def load_phase(g, j0, w, place):
             phase_raw[g, j0] = place
             load_rows(place, phase[g * GROUP : (g + 1) * GROUP, j0 : j0 + w])
 
-        def load_skin(g, o, place):
-            skin_raw[g, o] = place
-            load_rows(place, skin[g * GROUP : (g + 1) * GROUP, o * GROUP : (o + 1) * GROUP])
-
-        def round_and_deal(raw, copy=nc.scalar.copy, dealt=None):
+        def round_and_deal(raws, copy, dealt=None):
             if dealt is None:
                 dealt = ring.tile([P, 4 * GROUP], BF16, name="dealt", align_bytes=64)
-            copy(
-                out=dealt[:].rearrange("p (u e m i) -> p m u i e", u=2, e=2, i=4),
-                in_=raw.rearrange("p i (m u e) -> p m u i e", u=2, e=2),
-            )
+            places = dealt[:].rearrange("p (u e m i) -> p m u i e", u=2, e=2, i=4)
+            count = P // len(raws)
+            for n, raw in enumerate(raws):
+                copy(
+                    out=places[:, n * count : (n + 1) * count],
+                    in_=raw.rearrange("p i (m u e) -> p m u i e", u=2, e=2),
+                )
             return dealt
 
         def quantise(codes, scales, values):
@@ -125,13 +124,13 @@ def tile_list_keyframe_blend_skinning_kernel(
             out=w4_raw[:].bitcast(I32).rearrange("p (a c) -> p a c", a=2),
             in_=w4_words.bitcast(I32).rearrange("a p c -> p a c"),
         )
-        nc.sync.dma_start(out=tab_s_area[4:P:8, 0:T].bitcast(I32), in_=tab_scales[1].bitcast(I32))
-        load_planes(tab_s, tab_scales[0:1], range(4))
+        load_spread(tab_s, tab_scales[1])
+        load_planes(tab_s, tab_scales[0:1])
         load_words(tab_w[0], tab_words[0])
         nc.sync.dma_start(idx2[:], offs2)
-        nc.sync.dma_start(out=tab2_s[4:P:8, :].bitcast(I32), in_=tab2_scales[0].bitcast(I32))
+        load_spread(tab2_s, tab2_scales[0])
         load_rows(w1_raw0[:], w1[:, 0:GROUP])
-        load_planes(w4_s_raw, w4_scales, range(0, 4))
+        load_planes(w4_s_raw, w4_scales)
         load_words(tab2_w, tab2_words[0])
         load_words(tab_w[1], tab_words[1])
 
@@ -157,26 +156,35 @@ def tile_list_keyframe_blend_skinning_kernel(
             return place[:]
 
         def load_late_phase(g, part):
-            phase_offset[g, part * PHASE_COLS] = 16 * sum(late_places)
-            load_phase(g, part * PHASE_COLS, PHASE_COLS, late_rows(PHASE_COLS))
+            phase_offset[g, part * WIDE] = 16 * sum(late_places)
+            load_phase(g, part * WIDE, WIDE, late_rows(WIDE))
+
+        def load_late_group(rows, parts):
+            width = GROUP // parts
+            raws = [late_rows(width) for n in range(parts)]
+            for n, raw in enumerate(raws):
+                load_rows(raw, rows[:, n * width : (n + 1) * width])
+            return raws
+
+        def load_skin(g, o, parts):
+            skin_raw[g, o] = load_late_group(skin[g * GROUP : (g + 1) * GROUP, o * GROUP : (o + 1) * GROUP], parts)
 
         load_late_phase(0, 0)
         load_late_phase(0, 1)
-        w1_raw1 = late_rows(GROUP)
-        load_rows(w1_raw1, w1[:, GROUP : 2 * GROUP])
+        w1_raw1 = load_late_group(w1[:, GROUP : 2 * GROUP], 2)
         load_late_phase(1, 0)
-        load_skin(0, 0, late_rows(GROUP))
+        load_skin(0, 0, 1)
+        load_late_phase(1, 1)
+        load_skin(1, 0, 1)
+        load_late_phase(0, 2)
         rest_cols = late_rows(4).rearrange("p a b -> p (a b)")[:, 0:8].rearrange("p (o t) -> p o t", o=2)
         nc.sync.dma_start(out=rest_cols, in_=rest.rearrange("(o p t) -> p o t", o=2, t=4))
-        load_late_phase(1, 1)
-        load_skin(1, 0, late_rows(GROUP))
-        load_late_phase(0, 2)
-        load_skin(0, 1, late_rows(GROUP))
+        load_skin(0, 1, 2)
         load_late_phase(1, 2)
-        load_skin(1, 1, late_rows(GROUP))
+        load_skin(1, 1, 2)
 
         nc.vector.tensor_copy(v_c[0][:], tab_w[0][:].bitcast(U32).indirect(idx[:]))
-        quantise(w1_c[0][:], w1_s[0][:], round_and_deal(w1_raw0[:])[:])
+        quantise(w1_c[0][:], w1_s[0][:], round_and_deal([w1_raw0[:]], nc.scalar.copy)[:])
         nc.vector.tensor_copy(
             out=w4_s[:].rearrange("p (run t m) -> p run t m", run=4, t=4),
             in_=w4_s_raw[:].rearrange("p (run m t) -> p run t m", run=4, t=4),
@@ -191,7 +199,7 @@ def tile_list_keyframe_blend_skinning_kernel(
         for n, (g, j0, w) in enumerate(BLENDS[-3:]):
             phase_offset[g, j0] = tab_at + (0, 4 * T, 6 * T)[n]
             load_phase(g, j0, w, placed([P, 4, w], F32, "phase_last%d" % n, phase_offset[g, j0])[:])
-        w1_b1 = round_and_deal(w1_raw1)
+        w1_b1 = round_and_deal(w1_raw1, nc.scalar.copy)
 
         def b_product(g, j0, w, t0, nt):
             b_ps = psum.tile([P, nt, w], F32, name="b_ps")
@@ -233,13 +241,13 @@ def tile_list_keyframe_blend_skinning_kernel(
                 terms[g, j0] = (b_term, a_term)
             b_term, a_term = terms[g, j0]
             nt = BANK // w
-            order = "p t j -> p j t" if nt == 2 else "p t j -> p t j"
+            order = "p t j -> p j t" if w == WIDE else "p t j -> p t j"
             jobs = [(kind, t0) for t0 in range(0, 4, nt) for kind in "ba"]
             for kind, t0 in jobs[half * len(jobs) // 2 : (half + 1) * len(jobs) // 2]:
                 rows = slice(t0, t0 + nt)
                 cols = slice(t0 * w, (t0 + nt) * w)
                 ph = phase_raw[g, j0][:, rows, :].rearrange(order)
-                inner = 2 if nt == 2 else w
+                inner = nt if w == WIDE else w
                 if kind == "b":
                     nc.vector.tensor_tensor(
                         b_term[:, cols].rearrange("p (x y) -> p x y", y=inner),
@@ -253,14 +261,10 @@ def tile_list_keyframe_blend_skinning_kernel(
 
         def blend_sum(g, j0, w):
             b_term, a_term = terms[g, j0]
-            if BANK // w == 2:
-                if (g, j0, w) != BLENDS[PROMPT]:
-                    h_b[g, j0] = ring.tile([P, w, 4], BF16, name="h_wide", align_bytes=64, bufs=1)
+            if w == WIDE:
+                h_b[g, j0] = ring.tile([P, w, 4], BF16, name="h_wide", align_bytes=64, bufs=1)
                 share = POOL_COLS_LAST if j0 + w == S else POOL_COLS
                 shares = ((nc.gpsimd, slice(0, share)), (nc.vector, slice(share, w)))
-                if (g, j0, w) == BLENDS[PROMPT]:
-                    h_b[g, j0] = held([P, w, 4], BF16, "h_prompt")
-                    shares = ((nc.vector, slice(0, w)),)
                 for engine, cols in shares:
                     engine.tensor_tensor(
                         h_b[g, j0][:, cols, :].rearrange("p j (u e) -> p j u e", e=2),
@@ -285,16 +289,16 @@ def tile_list_keyframe_blend_skinning_kernel(
             g, j0, w = BLENDS[s]
             name = "h_c%d_%d" % (g, j0)
             if s + 1 < len(BLENDS):
-                codes = behind_terms(s + 1, name, w, 0)
+                codes = behind_terms(s + 1, name, w, h_at)
             else:
                 codes = held([P, w], U32, name)
             scales = held([P, w], U8, "h_s%d_%d" % (g, j0))
             quantise(codes[:], scales[:], h_b[g, j0][:].rearrange("p j t -> p (j t)"))
             for first in range(j0, j0 + w, P):
-                h_c[g, first] = (codes, scales, first - j0)
+                h_q[g, first] = (codes, scales, first - j0)
 
         def y_pass(place, j0, w, o, g, t, start, stop):
-            codes, scales, c0 = h_c[g, j0]
+            codes, scales, c0 = h_q[g, j0]
             nc.tensor.matmul_mx(
                 out=place,
                 lhsT=skin_c[g][o][:, t * P : (t + 1) * P].bitcast(FP8X4),
@@ -324,8 +328,8 @@ def tile_list_keyframe_blend_skinning_kernel(
                 else:
                     y_ps = psum.tile([P, per_bank, w], F32, name="y_ps", bufs=4)
                     for k in range(per_bank):
-                        for c0 in range(0, w, PHASE_COLS):
-                            n = min(w, PHASE_COLS)
+                        for c0 in range(0, w, WIDE):
+                            n = min(w, WIDE)
                             for g in range(2):
                                 y_pass(y_ps[:, k, c0 : c0 + n], j0 + c0, n, o, g, t0 + k, g == 0, g == 1)
                 if last_chunk and o == 1:
@@ -346,7 +350,7 @@ def tile_list_keyframe_blend_skinning_kernel(
             y_f[cc, o] = y
 
         def round_y(cc, o, c0, copy, place=None):
-            w = min(CHUNKS[cc][1], PHASE_COLS)
+            w = min(CHUNKS[cc][1], WIDE)
             if place is None:
                 if c0 == 0:
                     y_b[cc, o] = held([P, CHUNKS[cc][1], 4], BF16, "y_b%d%d" % (cc, o))
@@ -377,20 +381,22 @@ def tile_list_keyframe_blend_skinning_kernel(
             for half in range(2):
                 blend_terms(*BLENDS[s], half)
 
-        def round_skin(g, o, copy=nc.scalar.copy):
-            skin_b[g, o] = round_and_deal(skin_raw[g, o], copy)
+        def round_skin(g, o):
+            skin_b[g, o] = round_and_deal(skin_raw[g, o], nc.scalar.copy)
 
         def quantise_skin(g, o, s):
             if s is None:
                 skin_c[g][o] = held([P, GROUP], U32, "skin_c%d%d" % (g, o))
             else:
-                skin_c[g][o] = behind_terms(s, "skin_c%d%d" % (g, o), GROUP, 4 * PHASE_COLS)
+                skin_c[g][o] = behind_terms(s, "skin_c%d%d" % (g, o), GROUP, after_h)
             quantise(skin_c[g][o][:], skin_s[g][o][:], skin_b[g, o][:])
 
+        h_at = 4 * WIDE
+        after_h = 8 * WIDE
         terms_of(0)
         terms_of(1)
         blend_sum(*BLENDS[0])
-        w1_c[1] = behind_terms(1, "w1_c1", GROUP, 4 * PHASE_COLS)
+        w1_c[1] = behind_terms(1, "w1_c1", GROUP, after_h)
         quantise(w1_c[1][:], w1_s[1][:], w1_b1[:])
         quantise_h(0)
         round_skin(0, 0)
@@ -414,17 +420,18 @@ def tile_list_keyframe_blend_skinning_kernel(
 
         terms_of(5)
         blend_sum(*BLENDS[4])
-        round_skin(1, 1, nc.vector.tensor_copy)
         quantise_skin(0, 1, 5)
+        last_b = placed([P, 4 * GROUP], BF16, "last_b", phase_offset[1, 2 * WIDE] + h_at - 8 * GROUP)
+        skin_b[1, 1] = round_and_deal(skin_raw[1, 1], nc.vector.tensor_copy, last_b)
         quantise_h(4)
         quantise_skin(1, 1, None)
         round_y(0, 0, 0, nc.scalar.copy)
-        round_y(0, 0, 256, nc.scalar.copy)
+        round_y(0, 0, WIDE, nc.scalar.copy)
         skin_product(0, 1)
 
         terms_of(6)
         blend_sum(*BLENDS[5])
-        quantise_y(0, 0, 0, 512, y_b[0, 0][:])
+        quantise_y(0, 0, 0, GROUP, y_b[0, 0][:])
         quantise_h(5)
         round_y(0, 1, 0, nc.scalar.copy)
         skin_product(1, 0)
@@ -433,7 +440,8 @@ def tile_list_keyframe_blend_skinning_kernel(
         terms_of(7)
         blend_sum(*BLENDS[6])
         quantise_h(6)
-        round_y(0, 1, 256, nc.scalar.copy, behind_terms(6, "y_late", 512, 0)[:].bitcast(BF16).rearrange("p (j t) -> p j t", t=4))
+        y_late = behind_terms(6, "y_late", GROUP, h_at)
+        round_y(0, 1, WIDE, nc.scalar.copy, y_late[:].bitcast(BF16).rearrange("p (j t) -> p j t", t=4))
 
         blend_terms(*BLENDS[8], 0)
         blend_sum(*BLENDS[7])
@@ -445,22 +453,22 @@ def tile_list_keyframe_blend_skinning_kernel(
         skin_product(2, 1)
 
         blend_sum(*BLENDS[8])
-        quantise_y(0, 1, 0, 256, y_r[0, 1, 0])
+        quantise_y(0, 1, 0, WIDE, y_r[0, 1, 0])
         quantise_h(8)
         skin_product(3, 0)
-        quantise_y(0, 1, 256, 256, y_r[0, 1, 256])
+        quantise_y(0, 1, WIDE, WIDE, y_r[0, 1, WIDE])
         round_y(1, 0, 0, nc.vector.tensor_copy)
         skin_product(3, 1)
         round_y(1, 1, 0, nc.vector.tensor_copy)
         round_y(2, 0, 0, nc.scalar.copy)
         round_y(2, 1, 0, nc.scalar.copy)
         for o in range(2):
-            quantise_y(1, o, 0, 256, y_r[1, o, 0])
+            quantise_y(1, o, 0, WIDE, y_r[1, o, 0])
         for o in range(2):
             round_y(3, o, 0, nc.vector.tensor_copy)
         for cc in (2, 3):
             for o in range(2):
-                quantise_y(cc, o, 0, 128, y_r[cc, o, 0])
+                quantise_y(cc, o, 0, NARROW, y_r[cc, o, 0])
 
         for i in range(4):
             queue = nc.sync if i % 2 == 0 else nc.scalar

@@ -19,8 +19,6 @@ K, K2, H, N, T, T2, S = 1024, 512, 1024, 1024, 2048, 4096, 1024
 P = 128
 GROUP = 512
 BANK = 512
-W4_COLS = 128
-
 WIDE = 256
 NARROW = 128
 
@@ -28,7 +26,6 @@ BLENDS = [(g, j0, WIDE) for g in range(2) for j0 in (0, 256)]
 BLENDS = BLENDS + [(0, 512, WIDE), (1, 512, WIDE), (0, 768, WIDE), (1, 768, NARROW), (1, 896, NARROW)]
 CHUNKS = [(0, 512), (512, 256), (768, 128), (896, 128)]
 POOL_COLS = 160
-POOL_COLS_LAST = 96
 
 FLOPS = 2 * S * (K * H + K2 * H + H * N)
 
@@ -52,16 +49,12 @@ def tile_list_keyframe_blend_skinning_kernel(
 
         idx = held([P, S // 16], U16, "idx")
         idx2 = held([P, S // 16], U16, "idx2")
-        late_bytes = 16 * (5 * GROUP + 6 * WIDE + 4)
-        tab_s_area = placed([P, late_bytes], U8, "tab_s_area", 0)
-        tab_s = tab_s_area[:, 0:T]
-        tab_at = late_bytes
-        tab_w = [placed([P, T], I32, "tab_w%d" % a, tab_at + 4 * T * a) for a in range(2)]
-        early_at = tab_at + 8 * T
-        tab2_w = placed([P, T2], I32, "tab2_w", early_at)
-        w1_raw0 = placed([P, 4, GROUP], F32, "w1_raw0", early_at + 4 * T2)
-        tab2_s = placed([P, T2], U8, "tab2_s", early_at + 4 * T2 + 16 * GROUP)
-        w4_raw = placed([P, 4 * H], U8, "w4_raw", early_at + 5 * T2 + 16 * GROUP)
+        tab_w = [placed([P, T], I32, "tab_w%d" % a, 4 * T * a) for a in range(2)]
+        tab2_w = placed([P, T2], I32, "tab2_w", 8 * T)
+        rows_at = 8 * T + 4 * T2
+        tab_s = held([P, T], U8, "tab_s")
+        tab2_s = held([P, T2], U8, "tab2_s")
+        w4_raw = held([P, 4 * H], U8, "w4_raw")
         w4_s_raw = held([P, 2 * H], U8, "w4_s_raw")
         w4_c = held([P, 4 * H], U8, "w4_c")
         w4_s = held([P, 2 * H], U8, "w4_s")
@@ -71,21 +64,14 @@ def tile_list_keyframe_blend_skinning_kernel(
         v2_s = moved_s[:, S : 2 * S]
         v_c = [held([P, S], U32, "v_c%d" % a) for a in range(2)]
         v2_c = held([P, S], U32, "v2_c")
-        w1_c = [held([P, GROUP], U32, "w1_c0"), None]
-        w1_s = [held([P, GROUP], U8, "w1_s%d" % g) for g in range(2)]
-        skin_c = [[None, None], [None, None]]
-        skin_s = [[held([P, GROUP], U8, "skin_s%d%d" % (g, o)) for o in range(2)] for g in range(2)]
+        w1_c, w1_s, skin_c, skin_s = {}, {}, {}, {}
         y_s = held([P, 2 * S], U8, "y_s")
-        phase_raw, skin_raw, skin_b, y_f, y_r = {}, {}, {}, {}, {}
+        raw, raw_at, dealt, y_f, y_r = {}, {}, {}, {}, {}
         terms, h_b, h_q, y_b, y_c, last_ps = {}, {}, {}, {}, {}, {}
+        used = []
 
-        nc.gpsimd.memset(tab_s.bitcast(I32), 0)
-        nc.vector.memset(tab2_s[:].bitcast(I32), 0)
-        nc.gpsimd.memset(w4_s_raw[:].bitcast(I32), 0)
-        nc.gpsimd.memset(moved_s[:].bitcast(I32), 0)
-
-        def load_rows(place, rows):
-            nc.sync.dma_start(out=place, in_=rows.rearrange("(p t) c -> p t c", t=4))
+        for plane in (tab2_s, tab_s, w4_s_raw, moved_s):
+            nc.vector.memset(plane[:].bitcast(I32), 0)
 
         def load_words(tile, words):
             nc.sync.dma_start(out=tile[:], in_=words.rearrange("p t i -> p (t i)").bitcast(I32))
@@ -100,200 +86,195 @@ def tile_list_keyframe_blend_skinning_kernel(
         def load_spread(tile, rows):
             nc.sync.dma_start(out=tile[4:P:8, :].bitcast(I32), in_=rows.bitcast(I32))
 
-        def load_phase(g, j0, w, place):
-            phase_raw[g, j0] = place
-            load_rows(place, phase[g * GROUP : (g + 1) * GROUP, j0 : j0 + w])
+        def load_rows(key, rows, first, width):
+            at = rows_at + 16 * sum(used)
+            used.append(width)
+            place = placed([P, 4, width], F32, "raw%d" % len(used), at)
+            nc.sync.dma_start(out=place[:], in_=rows[:, first : first + width].rearrange("(p t) c -> p t c", t=4))
+            raw.setdefault(key, []).append((first, width, place))
+            raw_at.setdefault(key, at)
 
-        def round_and_deal(raws, copy, dealt=None):
-            if dealt is None:
-                dealt = ring.tile([P, 4 * GROUP], BF16, name="dealt", align_bytes=64)
-            places = dealt[:].rearrange("p (u e m i) -> p m u i e", u=2, e=2, i=4)
-            count = P // len(raws)
-            for n, raw in enumerate(raws):
+        def load_phase(s):
+            g, j0, w = BLENDS[s]
+            load_rows(s, phase[g * GROUP : (g + 1) * GROUP, j0 : j0 + w], 0, w)
+
+        def load_weight(key, widths, skip=0):
+            if key[0] == "w1":
+                rows = w1[:, key[1] * GROUP : (key[1] + 1) * GROUP]
+            else:
+                rows = skin[key[1] * GROUP : (key[1] + 1) * GROUP, key[2] * GROUP : (key[2] + 1) * GROUP]
+            first = skip
+            for width in widths:
+                load_rows(key, rows, first, width)
+                first = first + width
+
+        def round_weight(key, copy, place=None):
+            if place is None:
+                place = ring.tile([P, 4 * GROUP], BF16, name="dealt", align_bytes=64)
+            dealt[key] = place
+            places = place[:].rearrange("p (u e m i) -> p m u i e", u=2, e=2, i=4)
+            for first, width, part in raw[key]:
                 copy(
-                    out=places[:, n * count : (n + 1) * count],
-                    in_=raw.rearrange("p i (m u e) -> p m u i e", u=2, e=2),
+                    out=places[:, first // 4 : (first + width) // 4],
+                    in_=part[:].rearrange("p i (m u e) -> p m u i e", u=2, e=2),
                 )
-            return dealt
 
         def quantise(codes, scales, values):
             nc.vector.quantize_mx(out=codes.bitcast(FP8X4), scales=scales, in_=values)
 
-        nc.sync.dma_start(idx[:], offs)
+        def gather(out, window, offsets):
+            nc.vector.tensor_copy(out, window.indirect(offsets))
+
+        nc.sync.dma_start(idx2[:], offs2)
         nc.sync.dma_start(
             out=w4_raw[:].bitcast(I32).rearrange("p (a c) -> p a c", a=2),
             in_=w4_words.bitcast(I32).rearrange("a p c -> p a c"),
         )
+        load_spread(tab2_s, tab2_scales[0])
+        nc.sync.dma_start(idx[:], offs)
+        load_words(tab_w[0], tab_words[0])
         load_spread(tab_s, tab_scales[1])
         load_planes(tab_s, tab_scales[0:1])
-        load_words(tab_w[0], tab_words[0])
-        nc.sync.dma_start(idx2[:], offs2)
-        load_spread(tab2_s, tab2_scales[0])
-        load_rows(w1_raw0[:], w1[:, 0:GROUP])
-        load_planes(w4_s_raw, w4_scales)
         load_words(tab2_w, tab2_words[0])
+        load_planes(w4_s_raw, w4_scales)
         load_words(tab_w[1], tab_words[1])
+        load_weight(("w1", 0), [256])
 
-        nc.vector.tensor_copy(
+        nc.scalar.copy(
             out=w4_c[:].bitcast(U16).rearrange("p (run t m) -> p run t m", run=4, t=4),
             in_=w4_raw[:].bitcast(U16).rearrange("p (run m t) -> p run t m", run=4, t=4),
         )
-        nc.vector.tensor_copy(picked_s[:, 0:S], tab_s.indirect(idx[:]))
-        nc.vector.tensor_copy(picked_s[:, S : 2 * S], tab2_s[:].indirect(idx2[:]))
+        gather(picked_s[:, S : 2 * S], tab2_s[:], idx2[:])
+        gather(v_c[0][:], tab_w[0][:].bitcast(U32), idx[:])
+        gather(picked_s[:, 0:S], tab_s[:], idx[:])
         for i in range(4):
             nc.sync.dma_start(
                 out=moved_s[i:P:32, :].bitcast(I32),
                 in_=picked_s[4 + 8 * i : P : 32, :].bitcast(I32),
             )
+        load_weight(("w1", 0), [128, 128], 256)
+        load_phase(0)
+        load_phase(1)
+        load_weight(("w1", 1), [256, 256])
+        load_phase(2)
+        load_weight(("skin", 0, 0), [512])
+        load_phase(3)
+        load_weight(("skin", 1, 0), [512])
+        load_phase(4)
+        rest_cols = held([P, 2, 4], F32, "rest_cols")
+        nc.sync.dma_start(out=rest_cols[:], in_=rest.rearrange("(o p t) -> p o t", o=2, t=4))
+        load_weight(("skin", 0, 1), [256, 256])
+        load_phase(5)
+        load_weight(("skin", 1, 1), [256, 256])
+        for s in range(6, len(BLENDS)):
+            load_phase(s)
 
-        late_places = []
-        phase_offset = {}
-
-        def late_rows(width):
-            first = 16 * sum(late_places)
-            late_places.append(width)
-            place = placed([P, 4, width], F32, "late%d" % len(late_places), first)
-            return place[:]
-
-        def load_late_phase(g, part):
-            phase_offset[g, part * WIDE] = 16 * sum(late_places)
-            load_phase(g, part * WIDE, WIDE, late_rows(WIDE))
-
-        def load_late_group(rows, parts):
-            width = GROUP // parts
-            raws = [late_rows(width) for n in range(parts)]
-            for n, raw in enumerate(raws):
-                load_rows(raw, rows[:, n * width : (n + 1) * width])
-            return raws
-
-        def load_skin(g, o, parts):
-            skin_raw[g, o] = load_late_group(skin[g * GROUP : (g + 1) * GROUP, o * GROUP : (o + 1) * GROUP], parts)
-
-        load_late_phase(0, 0)
-        load_late_phase(0, 1)
-        w1_raw1 = load_late_group(w1[:, GROUP : 2 * GROUP], 2)
-        load_late_phase(1, 0)
-        load_skin(0, 0, 1)
-        load_late_phase(1, 1)
-        load_skin(1, 0, 1)
-        load_late_phase(0, 2)
-        rest_cols = late_rows(4).rearrange("p a b -> p (a b)")[:, 0:8].rearrange("p (o t) -> p o t", o=2)
-        nc.sync.dma_start(out=rest_cols, in_=rest.rearrange("(o p t) -> p o t", o=2, t=4))
-        load_skin(0, 1, 2)
-        load_late_phase(1, 2)
-        load_skin(1, 1, 2)
-
-        nc.vector.tensor_copy(v_c[0][:], tab_w[0][:].bitcast(U32).indirect(idx[:]))
-        quantise(w1_c[0][:], w1_s[0][:], round_and_deal([w1_raw0[:]], nc.scalar.copy)[:])
         nc.vector.tensor_copy(
             out=w4_s[:].rearrange("p (run t m) -> p run t m", run=4, t=4),
             in_=w4_s_raw[:].rearrange("p (run m t) -> p run t m", run=4, t=4),
         )
-        nc.vector.tensor_copy(v2_c[:], tab2_w[:].bitcast(U32).indirect(idx2[:]))
-        for j0 in range(0, S, S // 2):
-            nc.vector.tensor_copy(
-                v_c[1][:, j0 : j0 + S // 2],
-                tab_w[1][:].bitcast(U32).indirect(idx[:, j0 // 16 : (j0 + S // 2) // 16]),
-            )
+        gather(v2_c[:], tab2_w[:].bitcast(U32), idx2[:])
+        gather(v_c[1][:], tab_w[1][:].bitcast(U32), idx[:])
 
-        for n, (g, j0, w) in enumerate(BLENDS[-3:]):
-            phase_offset[g, j0] = tab_at + (0, 4 * T, 6 * T)[n]
-            load_phase(g, j0, w, placed([P, 4, w], F32, "phase_last%d" % n, phase_offset[g, j0])[:])
-        w1_b1 = round_and_deal(w1_raw1, nc.scalar.copy)
+        def behind_terms(s, name, width, at):
+            return placed([P, width], U32, name, raw_at[s] + at)
 
-        def b_product(g, j0, w, t0, nt):
-            b_ps = psum.tile([P, nt, w], F32, name="b_ps")
+        h_at = 4 * WIDE
+        after_h = 8 * WIDE
+
+        def quantise_weight(key, s):
+            name = "_".join(str(x) for x in key)
+            if s is None:
+                codes = held([P, GROUP], U32, name + "_c")
+            else:
+                codes = behind_terms(s, name + "_c", GROUP, after_h)
+            scales = held([P, GROUP], U8, name + "_s")
+            quantise(codes[:], scales[:], dealt[key][:])
+            if key[0] == "w1":
+                w1_c[key[1]], w1_s[key[1]] = codes, scales
+            else:
+                skin_c[key[1:]], skin_s[key[1:]] = codes, scales
+
+        def product(kind, g, j0, w, t0, nt):
+            bank = psum.tile([P, nt, w], F32, name=kind + "_ps")
             for e in range(nt):
-                m0 = (t0 + e) * P
-                nc.tensor.matmul_mx(
-                    out=b_ps[:, e, :],
-                    lhsT=w1_c[g][:, m0 : m0 + P].bitcast(FP8X4),
-                    lhsT_scale=w1_s[g][:, m0 : m0 + P],
-                    rhs=v2_c[:, j0 : j0 + w].bitcast(FP8X4),
-                    rhs_scale=v2_s[:, j0 : j0 + w],
-                    start=True,
-                    stop=True,
-                )
-            return b_ps
-
-        def a_product(g, j0, w, t0, nt):
-            a_ps = psum.tile([P, nt, w], F32, name="a_ps")
-            for e in range(nt):
-                for n0 in range(0, w, W4_COLS):
-                    cols = slice(j0 + n0, j0 + n0 + W4_COLS)
+                if kind == "b":
+                    m0 = (t0 + e) * P
+                    nc.tensor.matmul_mx(
+                        out=bank[:, e, :],
+                        lhsT=w1_c[g][:, m0 : m0 + P].bitcast(FP8X4),
+                        lhsT_scale=w1_s[g][:, m0 : m0 + P],
+                        rhs=v2_c[:, j0 : j0 + w].bitcast(FP8X4),
+                        rhs_scale=v2_s[:, j0 : j0 + w],
+                        start=True,
+                        stop=True,
+                    )
+                else:
                     for a in range(2):
                         m0 = a * H + g * GROUP + (t0 + e) * P
                         nc.tensor.matmul_mx(
-                            out=a_ps[:, e, n0 : n0 + W4_COLS],
+                            out=bank[:, e, :],
                             lhsT=w4_c[:, 2 * m0 : 2 * (m0 + P)].bitcast(FP4X4),
                             lhsT_scale=w4_s[:, m0 : m0 + P],
-                            rhs=v_c[a][:, cols].bitcast(FP8X4),
-                            rhs_scale=v_s[a][:, cols],
+                            rhs=v_c[a][:, j0 : j0 + w].bitcast(FP8X4),
+                            rhs_scale=v_s[a][:, j0 : j0 + w],
                             start=(a == 0),
                             stop=(a == 1),
                         )
-            return a_ps
+            return bank
 
-        def blend_terms(g, j0, w, half):
-            if half == 0:
-                b_term = ring.tile([P, 4 * w], F32, name="b_term")
-                a_term = ring.tile([P, 4 * w], F32, name="a_term")
-                terms[g, j0] = (b_term, a_term)
-            b_term, a_term = terms[g, j0]
+        def term(s, kind, t0):
+            g, j0, w = BLENDS[s]
+            if (s, kind) not in terms:
+                terms[s, kind] = ring.tile([P, 4 * w], F32, name=kind + "_term")
             nt = BANK // w
             order = "p t j -> p j t" if w == WIDE else "p t j -> p t j"
-            jobs = [(kind, t0) for t0 in range(0, 4, nt) for kind in "ba"]
-            for kind, t0 in jobs[half * len(jobs) // 2 : (half + 1) * len(jobs) // 2]:
-                rows = slice(t0, t0 + nt)
-                cols = slice(t0 * w, (t0 + nt) * w)
-                ph = phase_raw[g, j0][:, rows, :].rearrange(order)
-                inner = nt if w == WIDE else w
-                if kind == "b":
-                    nc.vector.tensor_tensor(
-                        b_term[:, cols].rearrange("p (x y) -> p x y", y=inner),
-                        b_product(g, j0, w, t0, nt)[:].rearrange(order), ph, MULT,
-                    )
-                else:
-                    nc.vector.scalar_tensor_tensor(
-                        a_term[:, cols].rearrange("p (x y) -> p x y", y=inner),
-                        ph, 1.0, a_product(g, j0, w, t0, nt)[:].rearrange(order), SUB, MULT,
-                    )
+            ph = raw[s][0][2][:, t0 : t0 + nt, :].rearrange(order)
+            place = terms[s, kind][:, t0 * w : (t0 + nt) * w].rearrange("p (x y) -> p x y", y=nt if w == WIDE else w)
+            bank = product(kind, g, j0, w, t0, nt)[:].rearrange(order)
+            if kind == "b":
+                nc.vector.tensor_tensor(place, bank, ph, MULT)
+            else:
+                nc.vector.scalar_tensor_tensor(place, ph, 1.0, bank, SUB, MULT)
 
-        def blend_sum(g, j0, w):
-            b_term, a_term = terms[g, j0]
+        def terms_of(s):
+            for t0 in range(0, 4, BANK // BLENDS[s][2]):
+                for kind in "ab":
+                    term(s, kind, t0)
+
+        def blend_sum(s):
+            g, j0, w = BLENDS[s]
+            b_term, a_term = terms[s, "b"], terms[s, "a"]
             if w == WIDE:
-                h_b[g, j0] = ring.tile([P, w, 4], BF16, name="h_wide", align_bytes=64, bufs=1)
-                share = POOL_COLS_LAST if j0 + w == S else POOL_COLS
-                shares = ((nc.gpsimd, slice(0, share)), (nc.vector, slice(share, w)))
+                h_b[s] = ring.tile([P, w, 4], BF16, name="h_wide", align_bytes=64, bufs=1)
+                shares = [(nc.gpsimd, slice(0, POOL_COLS)), (nc.vector, slice(POOL_COLS, w))]
+                if j0 + w == S:
+                    shares = [(nc.vector, slice(0, w))]
                 for engine, cols in shares:
                     engine.tensor_tensor(
-                        h_b[g, j0][:, cols, :].rearrange("p j (u e) -> p j u e", e=2),
+                        h_b[s][:, cols, :].rearrange("p j (u e) -> p j u e", e=2),
                         b_term[:].rearrange("p (u j e) -> p j u e", u=2, e=2)[:, cols],
                         a_term[:].rearrange("p (u j e) -> p j u e", u=2, e=2)[:, cols],
                         SUB,
                     )
                 return
-            h_b[g, j0] = ring.tile([P, w, 4], BF16, name="h_b", align_bytes=64)
+            h_b[s] = ring.tile([P, w, 4], BF16, name="h_b", align_bytes=64)
             nc.vector.tensor_tensor(
-                h_b[g, j0][:].rearrange("p (c i) t -> p c t i", i=4),
+                h_b[s][:].rearrange("p (c i) t -> p c t i", i=4),
                 b_term[:].rearrange("p (t c i) -> p c t i", t=4, i=4),
                 a_term[:].rearrange("p (t c i) -> p c t i", t=4, i=4),
                 SUB,
             )
 
-        def behind_terms(s, name, width, at):
-            g, j0, w = BLENDS[s]
-            return placed([P, width], U32, name, phase_offset[g, j0] + at)
-
         def quantise_h(s):
             g, j0, w = BLENDS[s]
-            name = "h_c%d_%d" % (g, j0)
+            name = "h_c%d" % s
             if s + 1 < len(BLENDS):
                 codes = behind_terms(s + 1, name, w, h_at)
             else:
                 codes = held([P, w], U32, name)
-            scales = held([P, w], U8, "h_s%d_%d" % (g, j0))
-            quantise(codes[:], scales[:], h_b[g, j0][:].rearrange("p j t -> p (j t)"))
+            scales = held([P, w], U8, "h_s%d" % s)
+            quantise(codes[:], scales[:], h_b[s][:].rearrange("p j t -> p (j t)"))
             for first in range(j0, j0 + w, P):
                 h_q[g, first] = (codes, scales, first - j0)
 
@@ -301,8 +282,8 @@ def tile_list_keyframe_blend_skinning_kernel(
             codes, scales, c0 = h_q[g, j0]
             nc.tensor.matmul_mx(
                 out=place,
-                lhsT=skin_c[g][o][:, t * P : (t + 1) * P].bitcast(FP8X4),
-                lhsT_scale=skin_s[g][o][:, t * P : (t + 1) * P],
+                lhsT=skin_c[g, o][:, t * P : (t + 1) * P].bitcast(FP8X4),
+                lhsT_scale=skin_s[g, o][:, t * P : (t + 1) * P],
                 rhs=codes[:, c0 : c0 + w].bitcast(FP8X4),
                 rhs_scale=scales[:, c0 : c0 + w],
                 start=start,
@@ -320,7 +301,7 @@ def tile_list_keyframe_blend_skinning_kernel(
             j0, w = CHUNKS[cc]
             last_chunk = cc == len(CHUNKS) - 1
             per_bank = BANK // w
-            y = placed([P, 4, w], F32, "y%d%d" % (cc, o), early_at + 16 * (2 * j0 + o * w))
+            y = placed([P, 4, w], F32, "y%d%d" % (cc, o), 16 * (2 * j0 + o * w))
             for t0 in range(0, 4, per_bank):
                 if last_chunk:
                     last_y_passes(o, 1)
@@ -377,60 +358,46 @@ def tile_list_keyframe_blend_skinning_kernel(
             elif at + n == GROUP and o == 1:
                 nc.sync.dma_start(out=words, in_=y_c[half][:])
 
-        def terms_of(s):
-            for half in range(2):
-                blend_terms(*BLENDS[s], half)
-
-        def round_skin(g, o):
-            skin_b[g, o] = round_and_deal(skin_raw[g, o], nc.scalar.copy)
-
-        def quantise_skin(g, o, s):
-            if s is None:
-                skin_c[g][o] = held([P, GROUP], U32, "skin_c%d%d" % (g, o))
-            else:
-                skin_c[g][o] = behind_terms(s, "skin_c%d%d" % (g, o), GROUP, after_h)
-            quantise(skin_c[g][o][:], skin_s[g][o][:], skin_b[g, o][:])
-
-        h_at = 4 * WIDE
-        after_h = 8 * WIDE
+        round_weight(("w1", 0), nc.scalar.copy)
+        quantise_weight(("w1", 0), None)
+        round_weight(("w1", 1), nc.scalar.copy)
         terms_of(0)
         terms_of(1)
-        blend_sum(*BLENDS[0])
-        w1_c[1] = behind_terms(1, "w1_c1", GROUP, after_h)
-        quantise(w1_c[1][:], w1_s[1][:], w1_b1[:])
+        blend_sum(0)
+        quantise_weight(("w1", 1), 1)
         quantise_h(0)
-        round_skin(0, 0)
+        round_weight(("skin", 0, 0), nc.scalar.copy)
 
         terms_of(2)
-        blend_sum(*BLENDS[1])
+        blend_sum(1)
         quantise_h(1)
-        round_skin(1, 0)
+        round_weight(("skin", 1, 0), nc.scalar.copy)
 
         terms_of(3)
-        blend_sum(*BLENDS[2])
-        quantise_skin(0, 0, 3)
+        blend_sum(2)
+        quantise_weight(("skin", 0, 0), 3)
         quantise_h(2)
-        round_skin(0, 1)
+        round_weight(("skin", 0, 1), nc.scalar.copy)
 
         terms_of(4)
-        blend_sum(*BLENDS[3])
-        quantise_skin(1, 0, 4)
+        blend_sum(3)
+        quantise_weight(("skin", 1, 0), 4)
         quantise_h(3)
         skin_product(0, 0)
 
         terms_of(5)
-        blend_sum(*BLENDS[4])
-        quantise_skin(0, 1, 5)
-        last_b = placed([P, 4 * GROUP], BF16, "last_b", phase_offset[1, 2 * WIDE] + h_at - 8 * GROUP)
-        skin_b[1, 1] = round_and_deal(skin_raw[1, 1], nc.vector.tensor_copy, last_b)
+        blend_sum(4)
+        quantise_weight(("skin", 0, 1), 5)
+        last_b = placed([P, 4 * GROUP], BF16, "last_b", raw_at[5] + h_at - 8 * GROUP)
+        round_weight(("skin", 1, 1), nc.vector.tensor_copy, last_b)
         quantise_h(4)
-        quantise_skin(1, 1, None)
+        quantise_weight(("skin", 1, 1), None)
         round_y(0, 0, 0, nc.scalar.copy)
         round_y(0, 0, WIDE, nc.scalar.copy)
         skin_product(0, 1)
 
         terms_of(6)
-        blend_sum(*BLENDS[5])
+        blend_sum(5)
         quantise_y(0, 0, 0, GROUP, y_b[0, 0][:])
         quantise_h(5)
         round_y(0, 1, 0, nc.scalar.copy)
@@ -438,21 +405,21 @@ def tile_list_keyframe_blend_skinning_kernel(
         skin_product(1, 1)
 
         terms_of(7)
-        blend_sum(*BLENDS[6])
+        blend_sum(6)
         quantise_h(6)
         y_late = behind_terms(6, "y_late", GROUP, h_at)
         round_y(0, 1, WIDE, nc.scalar.copy, y_late[:].bitcast(BF16).rearrange("p (j t) -> p j t", t=4))
 
-        blend_terms(*BLENDS[8], 0)
-        blend_sum(*BLENDS[7])
-        blend_terms(*BLENDS[8], 1)
+        term(8, "a", 0)
+        blend_sum(7)
+        term(8, "b", 0)
         quantise_h(7)
         for o in range(2):
             last_y_passes(o, 0)
         skin_product(2, 0)
         skin_product(2, 1)
 
-        blend_sum(*BLENDS[8])
+        blend_sum(8)
         quantise_y(0, 1, 0, WIDE, y_r[0, 1, 0])
         quantise_h(8)
         skin_product(3, 0)

@@ -22,10 +22,11 @@ BANK = 512
 WIDE = 256
 NARROW = 128
 
-BLENDS = [(g, j0, WIDE) for g in range(2) for j0 in (0, 256)]
-BLENDS = BLENDS + [(0, 512, WIDE), (1, 512, WIDE), (0, 768, WIDE), (1, 768, NARROW), (1, 896, NARROW)]
+BLENDS = [[(g, j0, WIDE)] for g in range(2) for j0 in (0, 256)] + [[(g, 512, WIDE)] for g in range(2)]
+BLENDS = BLENDS + [[(g, j0, NARROW) for g in range(2)] for j0 in (768, 896)]
+WEIGHTS = [("w1", 0), ("w1", 1), ("skin", 0, 0), ("skin", 1, 0), ("skin", 0, 1), ("skin", 1, 1)]
 CHUNKS = [(0, 512), (512, 256), (768, 128), (896, 128)]
-POOL_COLS = 160
+POOL_COLS = 144
 
 FLOPS = 2 * S * (K * H + K2 * H + H * N)
 
@@ -54,9 +55,9 @@ def tile_list_keyframe_blend_skinning_kernel(
         rows_at = 8 * T + 4 * T2
         tab_s = held([P, T], U8, "tab_s")
         tab2_s = held([P, T2], U8, "tab2_s")
-        w4_raw = held([P, 4 * H], U8, "w4_raw")
+        w4_raw = [held([P, 2 * H], U8, "w4_raw%d" % g) for g in range(2)]
         w4_s_raw = held([P, 2 * H], U8, "w4_s_raw")
-        w4_c = held([P, 4 * H], U8, "w4_c")
+        w4_c = [held([P, 2 * H], U8, "w4_c%d" % g) for g in range(2)]
         w4_s = held([P, 2 * H], U8, "w4_s")
         picked_s = held([P, 2 * S], U8, "picked_s")
         moved_s = held([P, 2 * S], U8, "moved_s")
@@ -69,6 +70,11 @@ def tile_list_keyframe_blend_skinning_kernel(
         raw, raw_at, dealt, y_f, y_r = {}, {}, {}, {}, {}
         terms, h_b, h_q, y_b, y_c, last_ps = {}, {}, {}, {}, {}, {}
         used = []
+        done = set()
+        dealt_at = {}
+        h_codes_at = {}
+        h_codes = {}
+        made = []
 
         for plane in (tab2_s, tab_s, w4_s_raw, moved_s):
             nc.vector.memset(plane[:].bitcast(I32), 0)
@@ -95,8 +101,12 @@ def tile_list_keyframe_blend_skinning_kernel(
             raw_at.setdefault(key, at)
 
         def load_phase(s):
-            g, j0, w = BLENDS[s]
-            load_rows(s, phase[g * GROUP : (g + 1) * GROUP, j0 : j0 + w], 0, w)
+            at = rows_at + 16 * sum(used)
+            used.append(WIDE)
+            raw[s], raw_at[s] = placed([P, 4, WIDE], F32, "phase%d" % s, at), at
+            for n, (g, j0, w) in enumerate(BLENDS[s]):
+                rows = phase[g * GROUP : (g + 1) * GROUP, j0 : j0 + w]
+                nc.sync.dma_start(out=raw[s][:, :, n * w : (n + 1) * w], in_=rows.rearrange("(p t) c -> p t c", t=4))
 
         def load_weight(key, widths, skip=0):
             if key[0] == "w1":
@@ -108,16 +118,32 @@ def tile_list_keyframe_blend_skinning_kernel(
                 load_rows(key, rows, first, width)
                 first = first + width
 
-        def round_weight(key, copy, place=None):
-            if place is None:
-                place = ring.tile([P, 4 * GROUP], BF16, name="dealt", align_bytes=64)
-            dealt[key] = place
-            places = place[:].rearrange("p (u e m i) -> p m u i e", u=2, e=2, i=4)
-            for first, width, part in raw[key]:
+        def round_weight(key, copy, parts=slice(None)):
+            if key not in dealt:
+                before = WEIGHTS[WEIGHTS.index(key) - 1]
+                if key == WEIGHTS[0]:
+                    dealt[key] = held([P, 4 * GROUP], BF16, "dealt0")
+                else:
+                    dealt_at[key] = raw_at[before]
+                    dealt[key] = placed([P, 4 * GROUP], BF16, "dealt%d" % WEIGHTS.index(key), dealt_at[key])
+            places = dealt[key][:].rearrange("p (u e m i) -> p m u i e", u=2, e=2, i=4)
+            for first, width, part in raw[key][parts]:
                 copy(
                     out=places[:, first // 4 : (first + width) // 4],
                     in_=part[:].rearrange("p i (m u e) -> p m u i e", u=2, e=2),
                 )
+
+        def load_w4(g):
+            nc.sync.dma_start(
+                out=w4_raw[g][:].bitcast(I32).rearrange("p (a c) -> p a c", a=2),
+                in_=w4_words[:, :, g * H : (g + 1) * H].bitcast(I32).rearrange("a p c -> p a c"),
+            )
+
+        def deal_w4(g):
+            nc.scalar.copy(
+                out=w4_c[g][:].bitcast(U16).rearrange("p (a t m) -> p a t m", a=2, t=4),
+                in_=w4_raw[g][:].bitcast(U16).rearrange("p (a m t) -> p a t m", a=2, t=4),
+            )
 
         def quantise(codes, scales, values):
             nc.vector.quantize_mx(out=codes.bitcast(FP8X4), scales=scales, in_=values)
@@ -126,10 +152,7 @@ def tile_list_keyframe_blend_skinning_kernel(
             nc.vector.tensor_copy(out, window.indirect(offsets))
 
         nc.sync.dma_start(idx2[:], offs2)
-        nc.sync.dma_start(
-            out=w4_raw[:].bitcast(I32).rearrange("p (a c) -> p a c", a=2),
-            in_=w4_words.bitcast(I32).rearrange("a p c -> p a c"),
-        )
+        load_w4(0)
         load_spread(tab2_s, tab2_scales[0])
         nc.sync.dma_start(idx[:], offs)
         load_words(tab_w[0], tab_words[0])
@@ -140,10 +163,7 @@ def tile_list_keyframe_blend_skinning_kernel(
         load_words(tab_w[1], tab_words[1])
         load_weight(("w1", 0), [256])
 
-        nc.scalar.copy(
-            out=w4_c[:].bitcast(U16).rearrange("p (run t m) -> p run t m", run=4, t=4),
-            in_=w4_raw[:].bitcast(U16).rearrange("p (run m t) -> p run t m", run=4, t=4),
-        )
+        deal_w4(0)
         gather(picked_s[:, S : 2 * S], tab2_s[:], idx2[:])
         gather(v_c[0][:], tab_w[0][:].bitcast(U32), idx[:])
         gather(picked_s[:, 0:S], tab_s[:], idx[:])
@@ -154,8 +174,9 @@ def tile_list_keyframe_blend_skinning_kernel(
             )
         load_weight(("w1", 0), [128, 128], 256)
         load_phase(0)
+        load_w4(1)
         load_phase(1)
-        load_weight(("w1", 1), [256, 256])
+        load_weight(("w1", 1), [128, 128, 128, 128])
         load_phase(2)
         load_weight(("skin", 0, 0), [512])
         load_phase(3)
@@ -166,15 +187,16 @@ def tile_list_keyframe_blend_skinning_kernel(
         load_weight(("skin", 0, 1), [256, 256])
         load_phase(5)
         load_weight(("skin", 1, 1), [256, 256])
-        for s in range(6, len(BLENDS)):
-            load_phase(s)
+        load_phase(6)
+        load_phase(7)
 
         nc.vector.tensor_copy(
             out=w4_s[:].rearrange("p (run t m) -> p run t m", run=4, t=4),
             in_=w4_s_raw[:].rearrange("p (run m t) -> p run t m", run=4, t=4),
         )
         gather(v2_c[:], tab2_w[:].bitcast(U32), idx2[:])
-        gather(v_c[1][:], tab_w[1][:].bitcast(U32), idx[:])
+        for j0, j1 in ((0, WIDE), (WIDE, S)):
+            gather(v_c[1][:, j0:j1], tab_w[1][:].bitcast(U32), idx[:, j0 // 16 : j1 // 16])
 
         def behind_terms(s, name, width, at):
             return placed([P, width], U32, name, raw_at[s] + at)
@@ -195,88 +217,98 @@ def tile_list_keyframe_blend_skinning_kernel(
             else:
                 skin_c[key[1:]], skin_s[key[1:]] = codes, scales
 
-        def product(kind, g, j0, w, t0, nt):
-            bank = psum.tile([P, nt, w], F32, name=kind + "_ps")
-            for e in range(nt):
-                if kind == "b":
-                    m0 = (t0 + e) * P
-                    nc.tensor.matmul_mx(
-                        out=bank[:, e, :],
-                        lhsT=w1_c[g][:, m0 : m0 + P].bitcast(FP8X4),
-                        lhsT_scale=w1_s[g][:, m0 : m0 + P],
-                        rhs=v2_c[:, j0 : j0 + w].bitcast(FP8X4),
-                        rhs_scale=v2_s[:, j0 : j0 + w],
-                        start=True,
-                        stop=True,
-                    )
-                else:
-                    for a in range(2):
-                        m0 = a * H + g * GROUP + (t0 + e) * P
+        def product(kind, s, u):
+            pair, second = divmod(len(made), 2)
+            made.append(kind)
+            swap = (max(pair // 2, 1) + 1) % 2
+            bank = psum.tile([P, 2, WIDE], F32, name="ab%d" % (2 * (pair % 2) + (second + swap) % 2), bufs=1)
+            for n, (g, j0, w) in enumerate(BLENDS[s]):
+                for e in range(2):
+                    t = 2 * u + e
+                    place = bank[:, e, n * w : (n + 1) * w]
+                    if kind == "b":
                         nc.tensor.matmul_mx(
-                            out=bank[:, e, :],
-                            lhsT=w4_c[:, 2 * m0 : 2 * (m0 + P)].bitcast(FP4X4),
-                            lhsT_scale=w4_s[:, m0 : m0 + P],
-                            rhs=v_c[a][:, j0 : j0 + w].bitcast(FP8X4),
-                            rhs_scale=v_s[a][:, j0 : j0 + w],
-                            start=(a == 0),
-                            stop=(a == 1),
+                            out=place,
+                            lhsT=w1_c[g][:, t * P : (t + 1) * P].bitcast(FP8X4),
+                            lhsT_scale=w1_s[g][:, t * P : (t + 1) * P],
+                            rhs=v2_c[:, j0 : j0 + w].bitcast(FP8X4),
+                            rhs_scale=v2_s[:, j0 : j0 + w],
+                            start=True,
+                            stop=True,
                         )
+                    else:
+                        for a in range(2):
+                            m0 = a * H + g * GROUP + t * P
+                            c0 = a * GROUP + t * P
+                            nc.tensor.matmul_mx(
+                                out=place,
+                                lhsT=w4_c[g][:, 2 * c0 : 2 * (c0 + P)].bitcast(FP4X4),
+                                lhsT_scale=w4_s[:, m0 : m0 + P],
+                                rhs=v_c[a][:, j0 : j0 + w].bitcast(FP8X4),
+                                rhs_scale=v_s[a][:, j0 : j0 + w],
+                                start=(a == 0),
+                                stop=(a == 1),
+                            )
             return bank
 
-        def term(s, kind, t0):
-            g, j0, w = BLENDS[s]
+        def term(s, kind, u, bank):
             if (s, kind) not in terms:
-                terms[s, kind] = ring.tile([P, 4 * w], F32, name=kind + "_term")
-            nt = BANK // w
-            order = "p t j -> p j t" if w == WIDE else "p t j -> p t j"
-            ph = raw[s][0][2][:, t0 : t0 + nt, :].rearrange(order)
-            place = terms[s, kind][:, t0 * w : (t0 + nt) * w].rearrange("p (x y) -> p x y", y=nt if w == WIDE else w)
-            bank = product(kind, g, j0, w, t0, nt)[:].rearrange(order)
+                terms[s, kind] = ring.tile([P, 2, WIDE, 2], F32, name=kind + "_term")
+            ph = raw[s][:, 2 * u : 2 * u + 2, :].rearrange("p e j -> p j e")
             if kind == "b":
-                nc.vector.tensor_tensor(place, bank, ph, MULT)
+                nc.vector.tensor_tensor(terms[s, kind][:, u], bank[:].rearrange("p e j -> p j e"), ph, MULT)
             else:
-                nc.vector.scalar_tensor_tensor(place, ph, 1.0, bank, SUB, MULT)
+                nc.vector.scalar_tensor_tensor(terms[s, kind][:, u], ph, 1.0, bank[:].rearrange("p e j -> p j e"), SUB, MULT)
 
         def terms_of(s):
-            for t0 in range(0, 4, BANK // BLENDS[s][2]):
+            if s == 0:
                 for kind in "ab":
-                    term(s, kind, t0)
-
-        def blend_sum(s):
-            g, j0, w = BLENDS[s]
-            b_term, a_term = terms[s, "b"], terms[s, "a"]
-            if w == WIDE:
-                h_b[s] = ring.tile([P, w, 4], BF16, name="h_wide", align_bytes=64, bufs=1)
-                shares = [(nc.gpsimd, slice(0, POOL_COLS)), (nc.vector, slice(POOL_COLS, w))]
-                if j0 + w == S:
-                    shares = [(nc.vector, slice(0, w))]
-                for engine, cols in shares:
-                    engine.tensor_tensor(
-                        h_b[s][:, cols, :].rearrange("p j (u e) -> p j u e", e=2),
-                        b_term[:].rearrange("p (u j e) -> p j u e", u=2, e=2)[:, cols],
-                        a_term[:].rearrange("p (u j e) -> p j u e", u=2, e=2)[:, cols],
-                        SUB,
-                    )
+                    for u in range(2):
+                        term(s, kind, u, product(kind, s, u))
                 return
-            h_b[s] = ring.tile([P, w, 4], BF16, name="h_b", align_bytes=64)
-            nc.vector.tensor_tensor(
-                h_b[s][:].rearrange("p (c i) t -> p c t i", i=4),
-                b_term[:].rearrange("p (t c i) -> p c t i", t=4, i=4),
-                a_term[:].rearrange("p (t c i) -> p c t i", t=4, i=4),
+            for u in range(2):
+                banks = [(kind, product(kind, s, u)) for kind in "ab"]
+                for kind, bank in reversed(banks):
+                    term(s, kind, u, bank)
+
+        def subtract(s, engine, place, cols):
+            engine.tensor_tensor(
+                place.rearrange("p j (u e) -> p j u e", e=2),
+                terms[s, "b"][:].rearrange("p u j e -> p j u e")[:, cols],
+                terms[s, "a"][:].rearrange("p u j e -> p j u e")[:, cols],
                 SUB,
             )
 
-        def quantise_h(s):
-            g, j0, w = BLENDS[s]
-            name = "h_c%d" % s
-            if s + 1 < len(BLENDS):
-                codes = behind_terms(s + 1, name, w, h_at)
+        def blend_sum(s):
+            whole = ring.tile([P, WIDE, 4], BF16, name="h_wide", align_bytes=64, bufs=1)
+            if s == 0:
+                subtract(s, nc.gpsimd, whole[:, 0:NARROW, :], slice(0, NARROW))
+                own = placed([P, NARROW, 4], BF16, "h_own", raw_at[1])
+                h_b[s] = [(NARROW, NARROW, own[:]), (0, NARROW, whole[:, 0:NARROW, :])]
+            elif s == len(BLENDS) - 1:
+                h_b[s] = [(c0, NARROW, whole[:, c0 : c0 + NARROW, :]) for c0 in (0, NARROW)]
+                for c0, n, place in h_b[s]:
+                    subtract(s, nc.vector, place, slice(c0, c0 + n))
             else:
-                codes = held([P, w], U32, name)
-            scales = held([P, w], U8, "h_s%d" % s)
-            quantise(codes[:], scales[:], h_b[s][:].rearrange("p j t -> p (j t)"))
-            for first in range(j0, j0 + w, P):
-                h_q[g, first] = (codes, scales, first - j0)
+                subtract(s, nc.vector, whole[:, POOL_COLS:WIDE, :], slice(POOL_COLS, WIDE))
+                subtract(s, nc.gpsimd, whole[:, 0:POOL_COLS, :], slice(0, POOL_COLS))
+                h_b[s] = [(0, WIDE, whole[:])]
+
+        def quantise_h(s, after=None, parts=slice(None)):
+            if s not in h_codes:
+                if after is not None:
+                    h_codes_at[s] = dealt_at[after]
+                elif s + 1 < len(BLENDS):
+                    h_codes_at[s] = raw_at[s + 1] + h_at
+                else:
+                    h_codes_at[s] = raw_at[s]
+                h_codes[s] = (placed([P, WIDE], U32, "h_c%d" % s, h_codes_at[s]), held([P, WIDE], U8, "h_s%d" % s))
+            codes, scales = h_codes[s]
+            for c0, n, values in h_b[s][parts]:
+                quantise(codes[:, c0 : c0 + n], scales[:, c0 : c0 + n], values.rearrange("p j t -> p (j t)"))
+            for n, (g, j0, w) in enumerate(BLENDS[s]):
+                for first in range(0, w, P):
+                    h_q[g, j0 + first] = (codes, scales, n * w + first)
 
         def y_pass(place, j0, w, o, g, t, start, stop):
             codes, scales, c0 = h_q[g, j0]
@@ -293,7 +325,7 @@ def tile_list_keyframe_blend_skinning_kernel(
         def last_y_passes(o, g):
             cc = len(CHUNKS) - 1
             if g == 0:
-                last_ps[o] = psum.tile([P, 4, CHUNKS[cc][1]], F32, name=("b_ps", "a_ps")[o])
+                last_ps[o] = psum.tile([P, 4, CHUNKS[cc][1]], F32, name="ab%d" % o, bufs=1)
             for t in range(4):
                 y_pass(last_ps[o][:, t, :], *CHUNKS[cc], o, g, t, g == 0 and t == 0, g == 1 and t == 3)
 
@@ -330,12 +362,13 @@ def tile_list_keyframe_blend_skinning_kernel(
                 nc.sync.dma_start(out=rows[:, t0 : t0 + per_store, :], in_=y[:, t0 : t0 + per_store, :])
             y_f[cc, o] = y
 
-        def round_y(cc, o, c0, copy, place=None):
+        def round_y(cc, o, c0, copy, at=None):
             w = min(CHUNKS[cc][1], WIDE)
-            if place is None:
-                if c0 == 0:
-                    y_b[cc, o] = held([P, CHUNKS[cc][1], 4], BF16, "y_b%d%d" % (cc, o))
-                place = y_b[cc, o][:, c0 : c0 + w, :]
+            name = "y_b%d%d_%d" % (cc, o, c0)
+            if at is None:
+                place = held([P, w, 4], BF16, name)[:]
+            else:
+                place = placed([P, w, 4], BF16, name, at)[:]
             y_r[cc, o, c0] = place
             copy(
                 out=place.rearrange("p (c i) t -> p c t i", i=4),
@@ -353,86 +386,86 @@ def tile_list_keyframe_blend_skinning_kernel(
                 values.rearrange("p j t -> p (j t)"),
             )
             words = out_1[:, :, half * GROUP : (half + 1) * GROUP, :].rearrange("o p j t -> p o (j t)").bitcast(I32)
-            if half == 0 and at + n == GROUP:
+            done.add((o, j0 + c0))
+            if half == 0 and (o, 0) in done and (o, WIDE) in done:
                 nc.sync.dma_start(out=words[:, o, :], in_=y_c[half][:, o, :])
-            elif at + n == GROUP and o == 1:
-                nc.sync.dma_start(out=words, in_=y_c[half][:])
+            elif half == 1 and (at + n) % WIDE == 0 and o == 1:
+                cols = slice(at + n - WIDE, at + n)
+                nc.sync.dma_start(out=words[:, :, cols], in_=y_c[half][:, :, cols])
 
         round_weight(("w1", 0), nc.scalar.copy)
         quantise_weight(("w1", 0), None)
+        deal_w4(1)
         round_weight(("w1", 1), nc.scalar.copy)
         terms_of(0)
-        terms_of(1)
         blend_sum(0)
+        terms_of(1)
+        subtract(0, nc.vector, h_b[0][0][2], slice(NARROW, WIDE))
         quantise_weight(("w1", 1), 1)
-        quantise_h(0)
+        quantise_h(0, ("w1", 1))
         round_weight(("skin", 0, 0), nc.scalar.copy)
 
-        terms_of(2)
         blend_sum(1)
+        terms_of(2)
         quantise_h(1)
         round_weight(("skin", 1, 0), nc.scalar.copy)
 
-        terms_of(3)
         blend_sum(2)
+        terms_of(3)
         quantise_weight(("skin", 0, 0), 3)
-        quantise_h(2)
+        quantise_h(2, ("skin", 0, 0))
         round_weight(("skin", 0, 1), nc.scalar.copy)
 
-        terms_of(4)
         blend_sum(3)
+        terms_of(4)
         quantise_weight(("skin", 1, 0), 4)
-        quantise_h(3)
-        skin_product(0, 0)
+        quantise_h(3, ("skin", 1, 0))
 
-        terms_of(5)
         blend_sum(4)
+        terms_of(5)
+        round_weight(("skin", 1, 1), nc.scalar.copy, slice(0, 1))
+        skin_product(0, 0)
         quantise_weight(("skin", 0, 1), 5)
-        last_b = placed([P, 4 * GROUP], BF16, "last_b", raw_at[5] + h_at - 8 * GROUP)
-        round_weight(("skin", 1, 1), nc.vector.tensor_copy, last_b)
-        quantise_h(4)
+        round_weight(("skin", 1, 1), nc.vector.tensor_copy, slice(1, 2))
         quantise_weight(("skin", 1, 1), None)
+        quantise_h(4, ("skin", 1, 1))
         round_y(0, 0, 0, nc.scalar.copy)
-        round_y(0, 0, WIDE, nc.scalar.copy)
-        skin_product(0, 1)
 
-        terms_of(6)
         blend_sum(5)
-        quantise_y(0, 0, 0, GROUP, y_b[0, 0][:])
+        terms_of(6)
+        skin_product(0, 1)
+        round_y(0, 0, WIDE, nc.scalar.copy, h_codes_at[3])
         quantise_h(5)
-        round_y(0, 1, 0, nc.scalar.copy)
+
+        blend_sum(6)
+        terms_of(7)
         skin_product(1, 0)
         skin_product(1, 1)
-
-        terms_of(7)
-        blend_sum(6)
         quantise_h(6)
-        y_late = behind_terms(6, "y_late", GROUP, h_at)
-        round_y(0, 1, WIDE, nc.scalar.copy, y_late[:].bitcast(BF16).rearrange("p (j t) -> p j t", t=4))
-
-        term(8, "a", 0)
-        blend_sum(7)
-        term(8, "b", 0)
-        quantise_h(7)
-        for o in range(2):
-            last_y_passes(o, 0)
         skin_product(2, 0)
         skin_product(2, 1)
 
-        blend_sum(8)
-        quantise_y(0, 1, 0, WIDE, y_r[0, 1, 0])
-        quantise_h(8)
+        blend_sum(7)
+        quantise_h(7, None, slice(0, 1))
+        for o in range(2):
+            last_y_passes(o, 0)
+        quantise_y(0, 0, 0, WIDE, y_r[0, 0, 0])
+        quantise_h(7, None, slice(1, 2))
         skin_product(3, 0)
-        quantise_y(0, 1, WIDE, WIDE, y_r[0, 1, WIDE])
-        round_y(1, 0, 0, nc.vector.tensor_copy)
+        round_y(0, 1, 0, nc.scalar.copy, h_codes_at[7])
+        quantise_y(0, 0, WIDE, WIDE, y_r[0, 0, WIDE])
+        round_y(0, 1, WIDE, nc.vector.tensor_copy)
         skin_product(3, 1)
+        round_y(1, 0, 0, nc.vector.tensor_copy)
         round_y(1, 1, 0, nc.vector.tensor_copy)
+        quantise_y(0, 1, WIDE, WIDE, y_r[0, 1, WIDE])
         round_y(2, 0, 0, nc.scalar.copy)
         round_y(2, 1, 0, nc.scalar.copy)
+        round_y(3, 0, 0, nc.scalar.copy)
         for o in range(2):
             quantise_y(1, o, 0, WIDE, y_r[1, o, 0])
-        for o in range(2):
-            round_y(3, o, 0, nc.vector.tensor_copy)
+        quantise_y(0, 1, 0, WIDE, y_r[0, 1, 0])
+        round_y(3, 1, 0, nc.vector.tensor_copy)
         for cc in (2, 3):
             for o in range(2):
                 quantise_y(cc, o, 0, NARROW, y_r[cc, o, 0])

@@ -70,6 +70,7 @@ def tile_list_keyframe_blend_skinning_kernel(
         raw, raw_at, dealt, y_f, y_r = {}, {}, {}, {}, {}
         terms, h_b, h_q, y_b, y_c, last_ps = {}, {}, {}, {}, {}, {}
         used = []
+        term_tile = {}
         done = set()
         dealt_at = {}
         h_codes_at = {}
@@ -175,8 +176,9 @@ def tile_list_keyframe_blend_skinning_kernel(
         load_weight(("w1", 0), [128, 128], 256)
         load_phase(0)
         load_w4(1)
+        load_weight(("w1", 1), [256])
         load_phase(1)
-        load_weight(("w1", 1), [128, 128, 128, 128])
+        load_weight(("w1", 1), [128, 128], 256)
         load_phase(2)
         load_weight(("skin", 0, 0), [512])
         load_phase(3)
@@ -253,7 +255,8 @@ def tile_list_keyframe_blend_skinning_kernel(
 
         def term(s, kind, u, bank):
             if (s, kind) not in terms:
-                terms[s, kind] = ring.tile([P, 2, WIDE, 2], F32, name=kind + "_term")
+                term_tile[s, kind] = ring.tile([P, 4 * WIDE + 2 * POOL_COLS], F32, name=kind + "_term", align_bytes=64)
+                terms[s, kind] = term_tile[s, kind][:, 0 : 4 * WIDE].rearrange("p (u j e) -> p u j e", u=2, e=2)
             ph = raw[s][:, 2 * u : 2 * u + 2, :].rearrange("p e j -> p j e")
             if kind == "b":
                 nc.vector.tensor_tensor(terms[s, kind][:, u], bank[:].rearrange("p e j -> p j e"), ph, MULT)
@@ -274,34 +277,27 @@ def tile_list_keyframe_blend_skinning_kernel(
         def subtract(s, engine, place, cols):
             engine.tensor_tensor(
                 place.rearrange("p j (u e) -> p j u e", e=2),
-                terms[s, "b"][:].rearrange("p u j e -> p j u e")[:, cols],
-                terms[s, "a"][:].rearrange("p u j e -> p j u e")[:, cols],
+                terms[s, "b"].rearrange("p u j e -> p j u e")[:, cols],
+                terms[s, "a"].rearrange("p u j e -> p j u e")[:, cols],
                 SUB,
             )
 
         def blend_sum(s):
-            whole = ring.tile([P, WIDE, 4], BF16, name="h_wide", align_bytes=64, bufs=1)
-            if s == 0:
-                subtract(s, nc.gpsimd, whole[:, 0:NARROW, :], slice(0, NARROW))
-                own = placed([P, NARROW, 4], BF16, "h_own", raw_at[1])
-                h_b[s] = [(NARROW, NARROW, own[:]), (0, NARROW, whole[:, 0:NARROW, :])]
-            elif s == len(BLENDS) - 1:
+            if s == len(BLENDS) - 1:
+                whole = held([P, WIDE, 4], BF16, "h_last")
                 h_b[s] = [(c0, NARROW, whole[:, c0 : c0 + NARROW, :]) for c0 in (0, NARROW)]
                 for c0, n, place in h_b[s]:
                     subtract(s, nc.vector, place, slice(c0, c0 + n))
-            else:
-                subtract(s, nc.vector, whole[:, POOL_COLS:WIDE, :], slice(POOL_COLS, WIDE))
-                subtract(s, nc.gpsimd, whole[:, 0:POOL_COLS, :], slice(0, POOL_COLS))
-                h_b[s] = [(0, WIDE, whole[:])]
+                return
+            first = 2 * WIDE + 2 * POOL_COLS
+            whole = term_tile[s, "a"][:, first : first + 2 * WIDE].bitcast(BF16).rearrange("p (j t) -> p j t", t=4)
+            subtract(s, nc.vector, whole[:, POOL_COLS:WIDE, :], slice(POOL_COLS, WIDE))
+            subtract(s, nc.gpsimd, whole[:, 0:POOL_COLS, :], slice(0, POOL_COLS))
+            h_b[s] = [(0, WIDE, whole)]
 
-        def quantise_h(s, after=None, parts=slice(None)):
+        def quantise_h(s, parts=slice(None)):
             if s not in h_codes:
-                if after is not None:
-                    h_codes_at[s] = dealt_at[after]
-                elif s + 1 < len(BLENDS):
-                    h_codes_at[s] = raw_at[s + 1] + h_at
-                else:
-                    h_codes_at[s] = raw_at[s]
+                h_codes_at[s] = raw_at[s]
                 h_codes[s] = (placed([P, WIDE], U32, "h_c%d" % s, h_codes_at[s]), held([P, WIDE], U8, "h_s%d" % s))
             codes, scales = h_codes[s]
             for c0, n, values in h_b[s][parts]:
@@ -364,11 +360,12 @@ def tile_list_keyframe_blend_skinning_kernel(
 
         def round_y(cc, o, c0, copy, at=None):
             w = min(CHUNKS[cc][1], WIDE)
-            name = "y_b%d%d_%d" % (cc, o, c0)
-            if at is None:
-                place = held([P, w, 4], BF16, name)[:]
+            if at is not None:
+                place = placed([P, w, 4], BF16, "y_late", at)[:]
             else:
-                place = placed([P, w, 4], BF16, name, at)[:]
+                if (cc, o) not in y_b:
+                    y_b[cc, o] = held([P, CHUNKS[cc][1], 4], BF16, "y_b%d%d" % (cc, o))
+                place = y_b[cc, o][:, c0 : c0 + w, :]
             y_r[cc, o, c0] = place
             copy(
                 out=place.rearrange("p (c i) t -> p c t i", i=4),
@@ -378,20 +375,25 @@ def tile_list_keyframe_blend_skinning_kernel(
         def quantise_y(cc, o, c0, n, values):
             j0, w = CHUNKS[cc]
             half, at = divmod(j0 + c0, GROUP)
-            if half not in y_c:
-                y_c[half] = held([P, 2, GROUP], I32, "y_c%d" % half)
+            if half == 0:
+                if (0, o) not in y_c:
+                    y_c[0, o] = held([P, GROUP], I32, "y_c0%d" % o)
+                codes = y_c[0, o][:]
+            else:
+                if 1 not in y_c:
+                    y_c[1] = held([P, 2, GROUP], I32, "y_c1")
+                codes = y_c[1][:, o, :]
             quantise(
-                y_c[half][:, o, at : at + n],
+                codes[:, at : at + n],
                 y_s[:, o * S + j0 + c0 : o * S + j0 + c0 + n],
                 values.rearrange("p j t -> p (j t)"),
             )
             words = out_1[:, :, half * GROUP : (half + 1) * GROUP, :].rearrange("o p j t -> p o (j t)").bitcast(I32)
-            done.add((o, j0 + c0))
-            if half == 0 and (o, 0) in done and (o, WIDE) in done:
-                nc.sync.dma_start(out=words[:, o, :], in_=y_c[half][:, o, :])
+            if half == 0 and at + n == GROUP:
+                nc.sync.dma_start(out=words[:, o, :], in_=codes)
             elif half == 1 and (at + n) % WIDE == 0 and o == 1:
                 cols = slice(at + n - WIDE, at + n)
-                nc.sync.dma_start(out=words[:, :, cols], in_=y_c[half][:, :, cols])
+                nc.sync.dma_start(out=words[:, :, cols], in_=y_c[1][:, :, cols])
 
         round_weight(("w1", 0), nc.scalar.copy)
         quantise_weight(("w1", 0), None)
@@ -399,45 +401,48 @@ def tile_list_keyframe_blend_skinning_kernel(
         round_weight(("w1", 1), nc.scalar.copy)
         terms_of(0)
         blend_sum(0)
+
         terms_of(1)
-        subtract(0, nc.vector, h_b[0][0][2], slice(NARROW, WIDE))
+        quantise_h(0)
         quantise_weight(("w1", 1), 1)
-        quantise_h(0, ("w1", 1))
+        blend_sum(1)
         round_weight(("skin", 0, 0), nc.scalar.copy)
 
-        blend_sum(1)
         terms_of(2)
         quantise_h(1)
+        blend_sum(2)
         round_weight(("skin", 1, 0), nc.scalar.copy)
 
-        blend_sum(2)
         terms_of(3)
+        quantise_h(2)
         quantise_weight(("skin", 0, 0), 3)
-        quantise_h(2, ("skin", 0, 0))
+        blend_sum(3)
         round_weight(("skin", 0, 1), nc.scalar.copy)
 
-        blend_sum(3)
         terms_of(4)
+        quantise_h(3)
         quantise_weight(("skin", 1, 0), 4)
-        quantise_h(3, ("skin", 1, 0))
-
         blend_sum(4)
-        terms_of(5)
-        round_weight(("skin", 1, 1), nc.scalar.copy, slice(0, 1))
-        skin_product(0, 0)
-        quantise_weight(("skin", 0, 1), 5)
-        round_weight(("skin", 1, 1), nc.vector.tensor_copy, slice(1, 2))
-        quantise_weight(("skin", 1, 1), None)
-        quantise_h(4, ("skin", 1, 1))
-        round_y(0, 0, 0, nc.scalar.copy)
 
+        terms_of(5)
+        skin_product(0, 0)
+        quantise_h(4)
+        dealt["skin", 1, 1] = placed([P, 4 * GROUP], BF16, "last_b", raw_at[5] + 64 - 8 * GROUP)
+        round_weight(("skin", 1, 1), nc.vector.tensor_copy)
+        quantise_weight(("skin", 0, 1), 5)
+        quantise_weight(("skin", 1, 1), None)
         blend_sum(5)
+        round_y(0, 0, 0, nc.scalar.copy)
+        round_y(0, 0, WIDE, nc.scalar.copy)
+
         terms_of(6)
         skin_product(0, 1)
-        round_y(0, 0, WIDE, nc.scalar.copy, h_codes_at[3])
         quantise_h(5)
-
+        y_c[0, 0] = placed([P, GROUP], I32, "y_c00", raw_at[6] + after_h)
+        quantise_y(0, 0, 0, GROUP, y_b[0, 0][:])
         blend_sum(6)
+        round_y(0, 1, 0, nc.scalar.copy)
+
         terms_of(7)
         skin_product(1, 0)
         skin_product(1, 1)
@@ -446,29 +451,23 @@ def tile_list_keyframe_blend_skinning_kernel(
         skin_product(2, 1)
 
         blend_sum(7)
-        quantise_h(7, None, slice(0, 1))
+        quantise_h(7, slice(0, 1))
         for o in range(2):
             last_y_passes(o, 0)
-        quantise_y(0, 0, 0, WIDE, y_r[0, 0, 0])
-        quantise_h(7, None, slice(1, 2))
-        skin_product(3, 0)
-        round_y(0, 1, 0, nc.scalar.copy, h_codes_at[7])
-        quantise_y(0, 0, WIDE, WIDE, y_r[0, 0, WIDE])
-        round_y(0, 1, WIDE, nc.vector.tensor_copy)
-        skin_product(3, 1)
-        round_y(1, 0, 0, nc.vector.tensor_copy)
-        round_y(1, 1, 0, nc.vector.tensor_copy)
-        quantise_y(0, 1, WIDE, WIDE, y_r[0, 1, WIDE])
-        round_y(2, 0, 0, nc.scalar.copy)
-        round_y(2, 1, 0, nc.scalar.copy)
-        round_y(3, 0, 0, nc.scalar.copy)
-        for o in range(2):
-            quantise_y(1, o, 0, WIDE, y_r[1, o, 0])
         quantise_y(0, 1, 0, WIDE, y_r[0, 1, 0])
-        round_y(3, 1, 0, nc.vector.tensor_copy)
+        quantise_h(7, slice(1, 2))
+        skin_product(3, 0)
+        round_y(0, 1, WIDE, nc.vector.tensor_copy)
+        round_y(1, 0, 0, nc.vector.tensor_copy)
+        skin_product(3, 1)
+        round_y(1, 1, 0, nc.vector.tensor_copy)
         for cc in (2, 3):
             for o in range(2):
-                quantise_y(cc, o, 0, NARROW, y_r[cc, o, 0])
+                round_y(cc, o, 0, nc.scalar.copy)
+        quantise_y(0, 1, WIDE, WIDE, y_r[0, 1, WIDE])
+        for cc in (1, 2, 3):
+            for o in range(2):
+                quantise_y(cc, o, 0, CHUNKS[cc][1], y_r[cc, o, 0])
 
         for i in range(4):
             queue = nc.sync if i % 2 == 0 else nc.scalar

@@ -55,9 +55,9 @@ def tile_list_keyframe_blend_skinning_kernel(
         rows_at = 8 * T + 4 * T2
         tab_s = held([P, T], U8, "tab_s")
         tab2_s = held([P, T2], U8, "tab2_s")
-        w4_raw = [held([P, 2 * H], U8, "w4_raw%d" % g) for g in range(2)]
+        w4_raw = held([P, 4 * H], U8, "w4_raw")
         w4_s_raw = held([P, 2 * H], U8, "w4_s_raw")
-        w4_c = [held([P, 2 * H], U8, "w4_c%d" % g) for g in range(2)]
+        w4_c = held([P, 4 * H], U8, "w4_c")
         w4_s = held([P, 2 * H], U8, "w4_s")
         picked_s = held([P, 2 * S], U8, "picked_s")
         moved_s = held([P, 2 * S], U8, "moved_s")
@@ -134,16 +134,16 @@ def tile_list_keyframe_blend_skinning_kernel(
                     in_=part[:].rearrange("p i (m u e) -> p m u i e", u=2, e=2),
                 )
 
-        def load_w4(g):
+        def load_w4():
             nc.sync.dma_start(
-                out=w4_raw[g][:].bitcast(I32).rearrange("p (a c) -> p a c", a=2),
-                in_=w4_words[:, :, g * H : (g + 1) * H].bitcast(I32).rearrange("a p c -> p a c"),
+                out=w4_raw[:].bitcast(I32).rearrange("p (a c) -> p a c", a=2),
+                in_=w4_words.bitcast(I32).rearrange("a p c -> p a c"),
             )
 
-        def deal_w4(g):
+        def deal_w4():
             nc.scalar.copy(
-                out=w4_c[g][:].bitcast(U16).rearrange("p (a t m) -> p a t m", a=2, t=4),
-                in_=w4_raw[g][:].bitcast(U16).rearrange("p (a m t) -> p a t m", a=2, t=4),
+                out=w4_c[:].bitcast(U16).rearrange("p (run t m) -> p run t m", run=4, t=4),
+                in_=w4_raw[:].bitcast(U16).rearrange("p (run m t) -> p run t m", run=4, t=4),
             )
 
         def quantise(codes, scales, values):
@@ -153,7 +153,7 @@ def tile_list_keyframe_blend_skinning_kernel(
             nc.vector.tensor_copy(out, window.indirect(offsets))
 
         nc.sync.dma_start(idx2[:], offs2)
-        load_w4(0)
+        load_w4()
         load_spread(tab2_s, tab2_scales[0])
         nc.sync.dma_start(idx[:], offs)
         load_words(tab_w[0], tab_words[0])
@@ -164,7 +164,7 @@ def tile_list_keyframe_blend_skinning_kernel(
         load_words(tab_w[1], tab_words[1])
         load_weight(("w1", 0), [256])
 
-        deal_w4(0)
+        deal_w4()
         gather(picked_s[:, S : 2 * S], tab2_s[:], idx2[:])
         gather(v_c[0][:], tab_w[0][:].bitcast(U32), idx[:])
         gather(picked_s[:, 0:S], tab_s[:], idx[:])
@@ -175,10 +175,8 @@ def tile_list_keyframe_blend_skinning_kernel(
             )
         load_weight(("w1", 0), [128, 128], 256)
         load_phase(0)
-        load_w4(1)
-        load_weight(("w1", 1), [256])
         load_phase(1)
-        load_weight(("w1", 1), [128, 128], 256)
+        load_weight(("w1", 1), [256, 256])
         load_phase(2)
         load_weight(("skin", 0, 0), [512])
         load_phase(3)
@@ -241,10 +239,9 @@ def tile_list_keyframe_blend_skinning_kernel(
                     else:
                         for a in range(2):
                             m0 = a * H + g * GROUP + t * P
-                            c0 = a * GROUP + t * P
                             nc.tensor.matmul_mx(
                                 out=place,
-                                lhsT=w4_c[g][:, 2 * c0 : 2 * (c0 + P)].bitcast(FP4X4),
+                                lhsT=w4_c[:, 2 * m0 : 2 * (m0 + P)].bitcast(FP4X4),
                                 lhsT_scale=w4_s[:, m0 : m0 + P],
                                 rhs=v_c[a][:, j0 : j0 + w].bitcast(FP8X4),
                                 rhs_scale=v_s[a][:, j0 : j0 + w],
@@ -391,13 +388,11 @@ def tile_list_keyframe_blend_skinning_kernel(
             words = out_1[:, :, half * GROUP : (half + 1) * GROUP, :].rearrange("o p j t -> p o (j t)").bitcast(I32)
             if half == 0 and at + n == GROUP:
                 nc.sync.dma_start(out=words[:, o, :], in_=codes)
-            elif half == 1 and (at + n) % WIDE == 0 and o == 1:
-                cols = slice(at + n - WIDE, at + n)
-                nc.sync.dma_start(out=words[:, :, cols], in_=y_c[1][:, :, cols])
+            elif at + n == GROUP and o == 1:
+                nc.sync.dma_start(out=words, in_=y_c[1][:])
 
         round_weight(("w1", 0), nc.scalar.copy)
         quantise_weight(("w1", 0), None)
-        deal_w4(1)
         round_weight(("w1", 1), nc.scalar.copy)
         terms_of(0)
         blend_sum(0)

@@ -22,11 +22,11 @@ BANK = 512
 WIDE = 256
 NARROW = 128
 
-BLENDS = [[(g, j0, WIDE)] for g in range(2) for j0 in (0, 256)] + [[(g, 512, WIDE)] for g in range(2)]
-BLENDS = BLENDS + [[(g, j0, NARROW) for g in range(2)] for j0 in (768, 896)]
+BLENDS = [(g, j0) for g in range(2) for j0 in (0, 256)] + [(g, j0) for j0 in (512, 768) for g in range(2)]
+PIECES = [(0, 0, 256), (0, 256, 256), (1, 0, 512)] + [(g, j0, 256) for g, j0 in BLENDS[4:]]
 WEIGHTS = [("w1", 0), ("w1", 1), ("skin", 0, 0), ("skin", 1, 0), ("skin", 0, 1), ("skin", 1, 1)]
-CHUNKS = [(0, 512), (512, 256), (768, 128), (896, 128)]
-POOL_COLS = 144
+CHUNKS = [(0, 512), (512, 256), (768, 256)]
+POOL_COLS = 152
 
 FLOPS = 2 * S * (K * H + K2 * H + H * N)
 
@@ -101,13 +101,18 @@ def tile_list_keyframe_blend_skinning_kernel(
             raw.setdefault(key, []).append((first, width, place))
             raw_at.setdefault(key, at)
 
-        def load_phase(s):
-            at = rows_at + 16 * sum(used)
-            used.append(WIDE)
-            raw[s], raw_at[s] = placed([P, 4, WIDE], F32, "phase%d" % s, at), at
-            for n, (g, j0, w) in enumerate(BLENDS[s]):
-                rows = phase[g * GROUP : (g + 1) * GROUP, j0 : j0 + w]
-                nc.sync.dma_start(out=raw[s][:, :, n * w : (n + 1) * w], in_=rows.rearrange("(p t) c -> p t c", t=4))
+        def load_phase(n):
+            g, j0, w = PIECES[n]
+            load_rows(n, phase[g * GROUP : (g + 1) * GROUP, j0 : j0 + w], 0, w)
+
+        def piece_of(s):
+            g, j0 = BLENDS[s]
+            n = [n for n, (pg, pj, pw) in enumerate(PIECES) if pg == g and pj <= j0 < pj + pw][0]
+            return n, j0 - PIECES[n][1]
+
+        def phase_at(s):
+            n, first = piece_of(s)
+            return raw_at[n] + 16 * first
 
         def load_weight(key, widths, skip=0):
             if key[0] == "w1":
@@ -119,7 +124,7 @@ def tile_list_keyframe_blend_skinning_kernel(
                 load_rows(key, rows, first, width)
                 first = first + width
 
-        def round_weight(key, copy, parts=slice(None)):
+        def round_weight(key, copy, parts=slice(None), cols=None):
             if key not in dealt:
                 before = WEIGHTS[WEIGHTS.index(key) - 1]
                 if key == WEIGHTS[0]:
@@ -129,9 +134,10 @@ def tile_list_keyframe_blend_skinning_kernel(
                     dealt[key] = placed([P, 4 * GROUP], BF16, "dealt%d" % WEIGHTS.index(key), dealt_at[key])
             places = dealt[key][:].rearrange("p (u e m i) -> p m u i e", u=2, e=2, i=4)
             for first, width, part in raw[key][parts]:
+                c0, c1 = cols or (0, width)
                 copy(
-                    out=places[:, first // 4 : (first + width) // 4],
-                    in_=part[:].rearrange("p i (m u e) -> p m u i e", u=2, e=2),
+                    out=places[:, (first + c0) // 4 : (first + c1) // 4],
+                    in_=part[:, :, c0:c1].rearrange("p i (m u e) -> p m u i e", u=2, e=2),
                 )
 
         def load_w4():
@@ -162,7 +168,7 @@ def tile_list_keyframe_blend_skinning_kernel(
         load_words(tab2_w, tab2_words[0])
         load_planes(w4_s_raw, w4_scales)
         load_words(tab_w[1], tab_words[1])
-        load_weight(("w1", 0), [256])
+        load_weight(("w1", 0), [512])
 
         deal_w4()
         gather(picked_s[:, S : 2 * S], tab2_s[:], idx2[:])
@@ -173,22 +179,20 @@ def tile_list_keyframe_blend_skinning_kernel(
                 out=moved_s[i:P:32, :].bitcast(I32),
                 in_=picked_s[4 + 8 * i : P : 32, :].bitcast(I32),
             )
-        load_weight(("w1", 0), [128, 128], 256)
         load_phase(0)
         load_phase(1)
         load_weight(("w1", 1), [256, 256])
         load_phase(2)
         load_weight(("skin", 0, 0), [512])
-        load_phase(3)
         load_weight(("skin", 1, 0), [512])
-        load_phase(4)
+        load_phase(3)
         rest_cols = held([P, 2, 4], F32, "rest_cols")
         nc.sync.dma_start(out=rest_cols[:], in_=rest.rearrange("(o p t) -> p o t", o=2, t=4))
+        load_phase(4)
         load_weight(("skin", 0, 1), [256, 256])
         load_phase(5)
-        load_weight(("skin", 1, 1), [256, 256])
+        load_weight(("skin", 1, 1), [512])
         load_phase(6)
-        load_phase(7)
 
         nc.vector.tensor_copy(
             out=w4_s[:].rearrange("p (run t m) -> p run t m", run=4, t=4),
@@ -199,10 +203,10 @@ def tile_list_keyframe_blend_skinning_kernel(
             gather(v_c[1][:, j0:j1], tab_w[1][:].bitcast(U32), idx[:, j0 // 16 : j1 // 16])
 
         def behind_terms(s, name, width, at):
-            return placed([P, width], U32, name, raw_at[s] + at)
+            return placed([P, width], U32, name, phase_at(s) + at)
 
         h_at = 4 * WIDE
-        after_h = 8 * WIDE
+        after_h = 8 * WIDE - 64
 
         def quantise_weight(key, s):
             name = "_".join(str(x) for x in key)
@@ -222,10 +226,11 @@ def tile_list_keyframe_blend_skinning_kernel(
             made.append(kind)
             swap = (max(pair // 2, 1) + 1) % 2
             bank = psum.tile([P, 2, WIDE], F32, name="ab%d" % (2 * (pair % 2) + (second + swap) % 2), bufs=1)
-            for n, (g, j0, w) in enumerate(BLENDS[s]):
+            g, j0 = BLENDS[s]
+            for w in (WIDE,):
                 for e in range(2):
                     t = 2 * u + e
-                    place = bank[:, e, n * w : (n + 1) * w]
+                    place = bank[:, e, :]
                     if kind == "b":
                         nc.tensor.matmul_mx(
                             out=place,
@@ -254,7 +259,8 @@ def tile_list_keyframe_blend_skinning_kernel(
             if (s, kind) not in terms:
                 term_tile[s, kind] = ring.tile([P, 4 * WIDE + 2 * POOL_COLS], F32, name=kind + "_term", align_bytes=64)
                 terms[s, kind] = term_tile[s, kind][:, 0 : 4 * WIDE].rearrange("p (u j e) -> p u j e", u=2, e=2)
-            ph = raw[s][:, 2 * u : 2 * u + 2, :].rearrange("p e j -> p j e")
+            n, first = piece_of(s)
+            ph = raw[n][0][2][:, 2 * u : 2 * u + 2, first : first + WIDE].rearrange("p e j -> p j e")
             if kind == "b":
                 nc.vector.tensor_tensor(terms[s, kind][:, u], bank[:].rearrange("p e j -> p j e"), ph, MULT)
             else:
@@ -282,7 +288,7 @@ def tile_list_keyframe_blend_skinning_kernel(
         def blend_sum(s):
             if s == len(BLENDS) - 1:
                 whole = held([P, WIDE, 4], BF16, "h_last")
-                h_b[s] = [(c0, NARROW, whole[:, c0 : c0 + NARROW, :]) for c0 in (0, NARROW)]
+                h_b[s] = [(0, WIDE, whole[:])]
                 for c0, n, place in h_b[s]:
                     subtract(s, nc.vector, place, slice(c0, c0 + n))
                 return
@@ -294,14 +300,12 @@ def tile_list_keyframe_blend_skinning_kernel(
 
         def quantise_h(s, parts=slice(None)):
             if s not in h_codes:
-                h_codes_at[s] = raw_at[s]
+                h_codes_at[s] = phase_at(s)
                 h_codes[s] = (placed([P, WIDE], U32, "h_c%d" % s, h_codes_at[s]), held([P, WIDE], U8, "h_s%d" % s))
             codes, scales = h_codes[s]
             for c0, n, values in h_b[s][parts]:
                 quantise(codes[:, c0 : c0 + n], scales[:, c0 : c0 + n], values.rearrange("p j t -> p (j t)"))
-            for n, (g, j0, w) in enumerate(BLENDS[s]):
-                for first in range(0, w, P):
-                    h_q[g, j0 + first] = (codes, scales, n * w + first)
+            h_q[BLENDS[s]] = (codes, scales, 0)
 
         def y_pass(place, j0, w, o, g, t, start, stop):
             codes, scales, c0 = h_q[g, j0]
@@ -315,30 +319,30 @@ def tile_list_keyframe_blend_skinning_kernel(
                 stop=stop,
             )
 
-        def last_y_passes(o, g):
+        def last_y_passes(g):
             cc = len(CHUNKS) - 1
-            if g == 0:
-                last_ps[o] = psum.tile([P, 4, CHUNKS[cc][1]], F32, name="ab%d" % o, bufs=1)
-            for t in range(4):
-                y_pass(last_ps[o][:, t, :], *CHUNKS[cc], o, g, t, g == 0 and t == 0, g == 1 and t == 3)
+            for o in range(2):
+                for u in range(2):
+                    if g == 0:
+                        last_ps[o, u] = psum.tile([P, 2, WIDE], F32, name="ab%d" % (2 * o + u), bufs=1)
+                    for e in range(2):
+                        y_pass(last_ps[o, u][:, e, :], *CHUNKS[cc], o, g, 2 * u + e, g == 0 and e == 0, g == 1 and e == 1)
 
-        def skin_product(cc, o):
+        def skin_product(cc, o, by_vector=()):
             j0, w = CHUNKS[cc]
             last_chunk = cc == len(CHUNKS) - 1
             per_bank = BANK // w
             y = placed([P, 4, w], F32, "y%d%d" % (cc, o), 16 * (2 * j0 + o * w))
             for t0 in range(0, 4, per_bank):
                 if last_chunk:
-                    last_y_passes(o, 1)
-                    y_ps = last_ps[o]
+                    y_ps = last_ps[o, t0 // 2]
                 else:
                     y_ps = psum.tile([P, per_bank, w], F32, name="y_ps", bufs=4)
                     for k in range(per_bank):
                         for c0 in range(0, w, WIDE):
-                            n = min(w, WIDE)
                             for g in range(2):
-                                y_pass(y_ps[:, k, c0 : c0 + n], j0 + c0, n, o, g, t0 + k, g == 0, g == 1)
-                if last_chunk and o == 1:
+                                y_pass(y_ps[:, k, c0 : c0 + WIDE], j0 + c0, WIDE, o, g, t0 + k, g == 0, g == 1)
+                if t0 in by_vector:
                     nc.vector.tensor_tensor(
                         y[:, t0 : t0 + per_bank, :],
                         y_ps[:],
@@ -388,10 +392,11 @@ def tile_list_keyframe_blend_skinning_kernel(
             words = out_1[:, :, half * GROUP : (half + 1) * GROUP, :].rearrange("o p j t -> p o (j t)").bitcast(I32)
             if half == 0 and at + n == GROUP:
                 nc.sync.dma_start(out=words[:, o, :], in_=codes)
-            elif at + n == GROUP and o == 1:
+            elif at + n == GROUP and o == 0:
                 nc.sync.dma_start(out=words, in_=y_c[1][:])
 
-        round_weight(("w1", 0), nc.scalar.copy)
+        round_weight(("w1", 0), nc.scalar.copy, cols=(0, 192))
+        round_weight(("w1", 0), nc.vector.tensor_copy, cols=(192, GROUP))
         quantise_weight(("w1", 0), None)
         round_weight(("w1", 1), nc.scalar.copy)
         terms_of(0)
@@ -422,47 +427,43 @@ def tile_list_keyframe_blend_skinning_kernel(
         terms_of(5)
         skin_product(0, 0)
         quantise_h(4)
-        dealt["skin", 1, 1] = placed([P, 4 * GROUP], BF16, "last_b", raw_at[5] + 64 - 8 * GROUP)
-        round_weight(("skin", 1, 1), nc.vector.tensor_copy)
-        quantise_weight(("skin", 0, 1), 5)
-        quantise_weight(("skin", 1, 1), None)
         blend_sum(5)
+        dealt["skin", 1, 1] = placed([P, 4 * GROUP], BF16, "last_b", phase_at(5) + 16 * WIDE - 64)
+        round_weight(("skin", 1, 1), nc.scalar.copy, cols=(0, 192))
         round_y(0, 0, 0, nc.scalar.copy)
-        round_y(0, 0, WIDE, nc.scalar.copy)
 
         terms_of(6)
-        skin_product(0, 1)
         quantise_h(5)
-        y_c[0, 0] = placed([P, GROUP], I32, "y_c00", raw_at[6] + after_h)
-        quantise_y(0, 0, 0, GROUP, y_b[0, 0][:])
+        round_weight(("skin", 1, 1), nc.vector.tensor_copy, cols=(192, GROUP))
+        quantise_weight(("skin", 0, 1), 5)
+        quantise_weight(("skin", 1, 1), 6)
         blend_sum(6)
-        round_y(0, 1, 0, nc.scalar.copy)
+        skin_product(1, 0)
 
         terms_of(7)
-        skin_product(1, 0)
-        skin_product(1, 1)
+        skin_product(0, 1)
         quantise_h(6)
-        skin_product(2, 0)
-        skin_product(2, 1)
+        skin_product(1, 1)
+        last_y_passes(0)
 
         blend_sum(7)
-        quantise_h(7, slice(0, 1))
-        for o in range(2):
-            last_y_passes(o, 0)
-        quantise_y(0, 1, 0, WIDE, y_r[0, 1, 0])
-        quantise_h(7, slice(1, 2))
-        skin_product(3, 0)
-        round_y(0, 1, WIDE, nc.vector.tensor_copy)
+        round_y(0, 0, WIDE, nc.vector.tensor_copy)
+        quantise_h(7)
+        last_y_passes(1)
+        skin_product(2, 0)
         round_y(1, 0, 0, nc.vector.tensor_copy)
-        skin_product(3, 1)
-        round_y(1, 1, 0, nc.vector.tensor_copy)
-        for cc in (2, 3):
-            for o in range(2):
-                round_y(cc, o, 0, nc.scalar.copy)
-        quantise_y(0, 1, WIDE, WIDE, y_r[0, 1, WIDE])
-        for cc in (1, 2, 3):
-            for o in range(2):
-                quantise_y(cc, o, 0, CHUNKS[cc][1], y_r[cc, o, 0])
+        quantise_y(0, 0, 0, GROUP, y_b[0, 0][:])
+        round_y(0, 1, 0, nc.vector.tensor_copy)
+        skin_product(2, 1)
+        round_y(0, 1, WIDE, nc.vector.tensor_copy)
+        round_y(1, 1, 0, nc.scalar.copy)
+        round_y(2, 0, 0, nc.scalar.copy)
+        quantise_y(1, 0, 0, WIDE, y_r[1, 0, 0])
+        quantise_y(0, 1, 0, GROUP, y_b[0, 1][:])
+        round_y(2, 1, 0, nc.vector.tensor_copy)
+        quantise_y(1, 1, 0, WIDE, y_r[1, 1, 0])
+        for o in (1, 0):
+            quantise_y(2, o, 0, WIDE, y_r[2, o, 0])
 
         for i in range(4):
             queue = nc.sync if i % 2 == 0 else nc.scalar

@@ -180,16 +180,17 @@ def tile_list_keyframe_blend_skinning_kernel(
                 in_=picked_s[4 + 8 * i : P : 32, :].bitcast(I32),
             )
         load_phase(0)
+        load_weight(("w1", 1), [320])
         load_phase(1)
-        load_weight(("w1", 1), [256, 256])
+        load_weight(("w1", 1), [192], 320)
         load_phase(2)
         load_weight(("skin", 0, 0), [512])
         load_weight(("skin", 1, 0), [512])
         load_phase(3)
-        rest_cols = held([P, 2, 4], F32, "rest_cols")
-        nc.sync.dma_start(out=rest_cols[:], in_=rest.rearrange("(o p t) -> p o t", o=2, t=4))
         load_phase(4)
         load_weight(("skin", 0, 1), [256, 256])
+        rest_cols = held([P, 2, 4], F32, "rest_cols")
+        nc.sync.dma_start(out=rest_cols[:], in_=rest.rearrange("(o p t) -> p o t", o=2, t=4))
         load_phase(5)
         load_weight(("skin", 1, 1), [512])
         load_phase(6)
@@ -392,8 +393,8 @@ def tile_list_keyframe_blend_skinning_kernel(
             words = out_1[:, :, half * GROUP : (half + 1) * GROUP, :].rearrange("o p j t -> p o (j t)").bitcast(I32)
             if half == 0 and at + n == GROUP:
                 nc.sync.dma_start(out=words[:, o, :], in_=codes)
-            elif at + n == GROUP and o == 0:
-                nc.sync.dma_start(out=words, in_=y_c[1][:])
+            elif at + n == GROUP:
+                nc.sync.dma_start(out=words[:, o, :], in_=codes)
 
         round_weight(("w1", 0), nc.scalar.copy, cols=(0, 192))
         round_weight(("w1", 0), nc.vector.tensor_copy, cols=(192, GROUP))
@@ -450,20 +451,19 @@ def tile_list_keyframe_blend_skinning_kernel(
         round_y(0, 0, WIDE, nc.vector.tensor_copy)
         quantise_h(7)
         last_y_passes(1)
-        skin_product(2, 0)
-        round_y(1, 0, 0, nc.vector.tensor_copy)
         quantise_y(0, 0, 0, GROUP, y_b[0, 0][:])
         round_y(0, 1, 0, nc.vector.tensor_copy)
+        skin_product(2, 0, (2,))
         skin_product(2, 1)
         round_y(0, 1, WIDE, nc.vector.tensor_copy)
-        round_y(1, 1, 0, nc.scalar.copy)
-        round_y(2, 0, 0, nc.scalar.copy)
-        quantise_y(1, 0, 0, WIDE, y_r[1, 0, 0])
+        round_y(1, 0, 0, nc.vector.tensor_copy)
         quantise_y(0, 1, 0, GROUP, y_b[0, 1][:])
-        round_y(2, 1, 0, nc.vector.tensor_copy)
-        quantise_y(1, 1, 0, WIDE, y_r[1, 1, 0])
-        for o in (1, 0):
-            quantise_y(2, o, 0, WIDE, y_r[2, o, 0])
+        round_y(1, 1, 0, nc.scalar.copy)
+        round_y(2, 0, 0, nc.vector.tensor_copy)
+        round_y(2, 1, 0, nc.scalar.copy)
+        for o in range(2):
+            for cc in (1, 2):
+                quantise_y(cc, o, 0, WIDE, y_r[cc, o, 0])
 
         for i in range(4):
             queue = nc.sync if i % 2 == 0 else nc.scalar

@@ -165,9 +165,9 @@ def tile_list_keyframe_blend_skinning_kernel(
         load_words(tab_w[0], tab_words[0])
         load_spread(tab_s, tab_scales[1])
         load_planes(tab_s, tab_scales[0:1])
-        load_words(tab2_w, tab2_words[0])
-        load_planes(w4_s_raw, w4_scales)
         load_words(tab_w[1], tab_words[1])
+        load_planes(w4_s_raw, w4_scales)
+        load_words(tab2_w, tab2_words[0])
         load_weight(("w1", 0), [512])
 
         deal_w4()
@@ -195,13 +195,12 @@ def tile_list_keyframe_blend_skinning_kernel(
         load_weight(("skin", 1, 1), [512])
         load_phase(6)
 
+        gather(v_c[1][:], tab_w[1][:].bitcast(U32), idx[:])
         nc.vector.tensor_copy(
             out=w4_s[:].rearrange("p (run t m) -> p run t m", run=4, t=4),
             in_=w4_s_raw[:].rearrange("p (run m t) -> p run t m", run=4, t=4),
         )
         gather(v2_c[:], tab2_w[:].bitcast(U32), idx2[:])
-        for j0, j1 in ((0, WIDE), (WIDE, S)):
-            gather(v_c[1][:, j0:j1], tab_w[1][:].bitcast(U32), idx[:, j0 // 16 : j1 // 16])
 
         def behind_terms(s, name, width, at):
             return placed([P, width], U32, name, phase_at(s) + at)
@@ -301,7 +300,7 @@ def tile_list_keyframe_blend_skinning_kernel(
 
         def quantise_h(s, parts=slice(None)):
             if s not in h_codes:
-                h_codes_at[s] = phase_at(s)
+                h_codes_at[s] = phase_at(0) + 4 * WIDE if s == 2 else phase_at(s)
                 h_codes[s] = (placed([P, WIDE], U32, "h_c%d" % s, h_codes_at[s]), held([P, WIDE], U8, "h_s%d" % s))
             codes, scales = h_codes[s]
             for c0, n, values in h_b[s][parts]:
@@ -396,8 +395,8 @@ def tile_list_keyframe_blend_skinning_kernel(
             elif at + n == GROUP:
                 nc.sync.dma_start(out=words[:, o, :], in_=codes)
 
-        round_weight(("w1", 0), nc.scalar.copy, cols=(0, 192))
-        round_weight(("w1", 0), nc.vector.tensor_copy, cols=(192, GROUP))
+        round_weight(("w1", 0), nc.scalar.copy, cols=(0, 256))
+        round_weight(("w1", 0), nc.vector.tensor_copy, cols=(256, GROUP))
         quantise_weight(("w1", 0), None)
         round_weight(("w1", 1), nc.scalar.copy)
         terms_of(0)

@@ -222,10 +222,7 @@ def tile_list_keyframe_blend_skinning_kernel(
                 skin_c[key[1:]], skin_s[key[1:]] = codes, scales
 
         def product(kind, s, u):
-            pair, second = divmod(len(made), 2)
-            made.append(kind)
-            swap = (max(pair // 2, 1) + 1) % 2
-            bank = psum.tile([P, 2, WIDE], F32, name="ab%d" % (2 * (pair % 2) + (second + swap) % 2), bufs=1)
+            bank = psum.tile([P, 2, WIDE], F32, name="ab%d" % (2 * "ab".index(kind) + u), bufs=1)
             g, j0 = BLENDS[s]
             for w in (WIDE,):
                 for e in range(2):
@@ -267,15 +264,9 @@ def tile_list_keyframe_blend_skinning_kernel(
                 nc.vector.scalar_tensor_tensor(terms[s, kind][:, u], ph, 1.0, bank[:].rearrange("p e j -> p j e"), SUB, MULT)
 
         def terms_of(s):
-            if s == 0:
-                for kind in "ab":
-                    for u in range(2):
-                        term(s, kind, u, product(kind, s, u))
-                return
-            for u in range(2):
-                banks = [(kind, product(kind, s, u)) for kind in "ab"]
-                for kind, bank in reversed(banks):
-                    term(s, kind, u, bank)
+            order = [(kind, u) for kind in "ab" for u in range(2)] if s == 0 else [(kind, u) for u in range(2) for kind in "ab"]
+            for kind, u in order:
+                term(s, kind, u, product(kind, s, u))
 
         def subtract(s, engine, place, cols):
             engine.tensor_tensor(

from contextlib import ExitStack

import concourse.mybir as mybir

F32 = mybir.dt.float32
BF16 = mybir.dt.bfloat16
I32 = mybir.dt.int32
U32 = mybir.dt.uint32
U16 = mybir.dt.uint16
U8 = mybir.dt.uint8
FP8X4 = mybir.dt.float8_e4m3fn_x4
FP4X4 = mybir.dt.float4_e2m1fn_x4
MULT = mybir.AluOpType.mult
SUB = mybir.AluOpType.subtract
ADD = mybir.AluOpType.add
IDENT = mybir.ActivationFunctionType.Identity

K, K2, H, N, T, T2, S = 1024, 512, 1024, 1024, 2048, 4096, 1024
P = 128
GROUP = 512
BANK = 512
WIDE = 256
NARROW = 128

BLENDS = [(g, j0) for g in range(2) for j0 in (0, 256)] + [(g, j0) for j0 in (512, 768) for g in range(2)]
PIECES = [(0, 0, 256), (0, 256, 256), (1, 0, 512)] + [(g, j0, 256) for g, j0 in BLENDS[4:]]
WEIGHTS = [("w1", 0), ("w1", 1), ("skin", 0, 0), ("skin", 1, 0), ("skin", 0, 1), ("skin", 1, 1)]
CHUNKS = [(0, 512), (512, 256), (768, 256)]
POOL_COLS = 152

FLOPS = 2 * S * (K * H + K2 * H + H * N)


def tile_list_keyframe_blend_skinning_kernel(
    tc, tab_words, tab_scales, tab2_words, tab2_scales, offs, offs2,
    w4_words, w4_scales, w1, phase, skin, rest, out_0, out_1, out_2,
):
    nc = tc.nc
    with ExitStack() as ctx:
        keep = ctx.enter_context(tc.tile_pool(name="keep", bufs=1))
        ring = ctx.enter_context(tc.tile_pool(name="ring", bufs=3))
        psum = ctx.enter_context(tc.psum_pool(name="psum", bufs=2))
        shared = ctx.enter_context(tc.tile_pool(name="shared", bufs=1))

        def held(shape, dtype, name):
            return keep.tile(shape, dtype, name=name, align_bytes=64)

        def placed(shape, dtype, name, offset):
            return shared.tile(shape, dtype, name=name, align_bytes=64, offset=offset)

        idx = held([P, S // 16], U16, "idx")
        idx2 = held([P, S // 16], U16, "idx2")
        tab_w = [placed([P, T], I32, "tab_w%d" % a, 4 * T * a) for a in range(2)]
        tab2_w = placed([P, T2], I32, "tab2_w", 8 * T)
        rows_at = 8 * T + 4 * T2
        tab_s = held([P, T], U8, "tab_s")
        tab2_s = held([P, T2], U8, "tab2_s")
        w4_raw = held([P, 4 * H], U8, "w4_raw")
        w4_s_raw = held([P, 2 * H], U8, "w4_s_raw")
        w4_c = held([P, 4 * H], U8, "w4_c")
        w4_s = held([P, 2 * H], U8, "w4_s")
        picked_s = held([P, 2 * S], U8, "picked_s")
        moved_s = held([P, 2 * S], U8, "moved_s")
        v_s = [picked_s[:, 0:S], moved_s[:, 0:S]]
        v2_s = moved_s[:, S : 2 * S]
        v_c = [held([P, S], U32, "v_c%d" % a) for a in range(2)]
        v2_c = held([P, S], U32, "v2_c")
        w1_c, w1_s, skin_c, skin_s = {}, {}, {}, {}
        y_s = held([P, 2 * S], U8, "y_s")
        raw, raw_at, dealt, y_f, y_r = {}, {}, {}, {}, {}
        terms, h_b, h_q, y_b, y_c, last_ps = {}, {}, {}, {}, {}, {}
        used = []
        term_tile = {}
        done = set()
        dealt_at = {}
        h_codes_at = {}
        h_codes = {}
        made = []

        for plane in (tab2_s, tab_s, w4_s_raw, moved_s):
            nc.vector.memset(plane[:].bitcast(I32), 0)

        def load_words(tile, words):
            nc.sync.dma_start(out=tile[:], in_=words.rearrange("p t i -> p (t i)").bitcast(I32))

        def load_planes(tile, scales):
            for i in range(4):
                nc.sync.dma_start(
                    out=tile[i:P:32, :].bitcast(I32).rearrange("q (a c) -> q a c", a=scales.shape[0]),
                    in_=scales[:, i:16:4, :].bitcast(I32).rearrange("a q c -> q a c"),
                )

        def load_spread(tile, rows):
            nc.sync.dma_start(out=tile[4:P:8, :].bitcast(I32), in_=rows.bitcast(I32))

        def load_rows(key, rows, first, width):
            at = rows_at + 16 * sum(used)
            used.append(width)
            place = placed([P, 4, width], F32, "raw%d" % len(used), at)
            nc.sync.dma_start(out=place[:], in_=rows[:, first : first + width].rearrange("(p t) c -> p t c", t=4))
            raw.setdefault(key, []).append((first, width, place))
            raw_at.setdefault(key, at)

        def load_phase(n):
            g, j0, w = PIECES[n]
            load_rows(n, phase[g * GROUP : (g + 1) * GROUP, j0 : j0 + w], 0, w)

        def piece_of(s):
            g, j0 = BLENDS[s]
            n = [n for n, (pg, pj, pw) in enumerate(PIECES) if pg == g and pj <= j0 < pj + pw][0]
            return n, j0 - PIECES[n][1]

        def phase_at(s):
            n, first = piece_of(s)
            return raw_at[n] + 16 * first

        def load_weight(key, widths, skip=0):
            if key[0] == "w1":
                rows = w1[:, key[1] * GROUP : (key[1] + 1) * GROUP]
            else:
                rows = skin[key[1] * GROUP : (key[1] + 1) * GROUP, key[2] * GROUP : (key[2] + 1) * GROUP]
            first = skip
            for width in widths:
                load_rows(key, rows, first, width)
                first = first + width

        def round_weight(key, copy, parts=slice(None), cols=None):
            if key not in dealt:
                before = WEIGHTS[WEIGHTS.index(key) - 1]
                if key == WEIGHTS[0]:
                    dealt[key] = held([P, 4 * GROUP], BF16, "dealt0")
                else:
                    dealt_at[key] = raw_at[before]
                    dealt[key] = placed([P, 4 * GROUP], BF16, "dealt%d" % WEIGHTS.index(key), dealt_at[key])
            places = dealt[key][:].rearrange("p (u e m i) -> p m u i e", u=2, e=2, i=4)
            for first, width, part in raw[key][parts]:
                c0, c1 = cols or (0, width)
                copy(
                    out=places[:, (first + c0) // 4 : (first + c1) // 4],
                    in_=part[:, :, c0:c1].rearrange("p i (m u e) -> p m u i e", u=2, e=2),
                )

        def load_w4():
            nc.sync.dma_start(
                out=w4_raw[:].bitcast(I32).rearrange("p (a c) -> p a c", a=2),
                in_=w4_words.bitcast(I32).rearrange("a p c -> p a c"),
            )

        def deal_w4():
            nc.scalar.copy(
                out=w4_c[:].bitcast(U16).rearrange("p (run t m) -> p run t m", run=4, t=4),
                in_=w4_raw[:].bitcast(U16).rearrange("p (run m t) -> p run t m", run=4, t=4),
            )

        def quantise(codes, scales, values):
            nc.vector.quantize_mx(out=codes.bitcast(FP8X4), scales=scales, in_=values)

        def gather(out, window, offsets):
            nc.vector.tensor_copy(out, window.indirect(offsets))

        nc.sync.dma_start(idx2[:], offs2)
        load_w4()
        load_spread(tab2_s, tab2_scales[0])
        nc.sync.dma_start(idx[:], offs)
        load_words(tab_w[0], tab_words[0])
        load_spread(tab_s, tab_scales[1])
        load_planes(tab_s, tab_scales[0:1])
        load_words(tab_w[1], tab_words[1])
        load_planes(w4_s_raw, w4_scales)
        load_words(tab2_w, tab2_words[0])
        load_weight(("w1", 0), [512])

        deal_w4()
        gather(picked_s[:, S : 2 * S], tab2_s[:], idx2[:])
        gather(v_c[0][:], tab_w[0][:].bitcast(U32), idx[:])
        gather(picked_s[:, 0:S], tab_s[:], idx[:])
        for i in range(4):
            nc.sync.dma_start(
                out=moved_s[i:P:32, :].bitcast(I32),
                in_=picked_s[4 + 8 * i : P : 32, :].bitcast(I32),
            )
        load_phase(0)
        load_weight(("w1", 1), [320])
        load_phase(1)
        load_weight(("w1", 1), [192], 320)
        load_phase(2)
        load_weight(("skin", 0, 0), [512])
        load_weight(("skin", 1, 0), [512])
        load_phase(3)
        load_phase(4)
        load_weight(("skin", 0, 1), [256, 256])
        rest_cols = held([P, 2, 4], F32, "rest_cols")
        nc.sync.dma_start(out=rest_cols[:], in_=rest.rearrange("(o p t) -> p o t", o=2, t=4))
        load_phase(5)
        load_weight(("skin", 1, 1), [512])
        load_phase(6)

        gather(v_c[1][:], tab_w[1][:].bitcast(U32), idx[:])
        nc.vector.tensor_copy(
            out=w4_s[:].rearrange("p (run t m) -> p run t m", run=4, t=4),
            in_=w4_s_raw[:].rearrange("p (run m t) -> p run t m", run=4, t=4),
        )
        gather(v2_c[:], tab2_w[:].bitcast(U32), idx2[:])

        def behind_terms(s, name, width, at):
            return placed([P, width], U32, name, phase_at(s) + at)

        h_at = 4 * WIDE
        after_h = 8 * WIDE - 64

        def quantise_weight(key, s):
            name = "_".join(str(x) for x in key)
            if s is None:
                codes = held([P, GROUP], U32, name + "_c")
            else:
                codes = behind_terms(s, name + "_c", GROUP, after_h)
            scales = held([P, GROUP], U8, name + "_s")
            quantise(codes[:], scales[:], dealt[key][:])
            if key[0] == "w1":
                w1_c[key[1]], w1_s[key[1]] = codes, scales
            else:
                skin_c[key[1:]], skin_s[key[1:]] = codes, scales

        def product(kind, s, u):
            bank = psum.tile([P, 2, WIDE], F32, name="ab%d" % (2 * "ab".index(kind) + u), bufs=1)
            g, j0 = BLENDS[s]
            for w in (WIDE,):
                for e in range(2):
                    t = 2 * u + e
                    place = bank[:, e, :]
                    if kind == "b":
                        nc.tensor.matmul_mx(
                            out=place,
                            lhsT=w1_c[g][:, t * P : (t + 1) * P].bitcast(FP8X4),
                            lhsT_scale=w1_s[g][:, t * P : (t + 1) * P],
                            rhs=v2_c[:, j0 : j0 + w].bitcast(FP8X4),
                            rhs_scale=v2_s[:, j0 : j0 + w],
                            start=True,
                            stop=True,
                        )
                    else:
                        for a in range(2):
                            m0 = a * H + g * GROUP + t * P
                            nc.tensor.matmul_mx(
                                out=place,
                                lhsT=w4_c[:, 2 * m0 : 2 * (m0 + P)].bitcast(FP4X4),
                                lhsT_scale=w4_s[:, m0 : m0 + P],
                                rhs=v_c[a][:, j0 : j0 + w].bitcast(FP8X4),
                                rhs_scale=v_s[a][:, j0 : j0 + w],
                                start=(a == 0),
                                stop=(a == 1),
                            )
            return bank

        def term(s, kind, u, bank):
            if (s, kind) not in terms:
                term_tile[s, kind] = ring.tile([P, 4 * WIDE + 2 * POOL_COLS], F32, name=kind + "_term", align_bytes=64)
                terms[s, kind] = term_tile[s, kind][:, 0 : 4 * WIDE].rearrange("p (u j e) -> p u j e", u=2, e=2)
            n, first = piece_of(s)
            ph = raw[n][0][2][:, 2 * u : 2 * u + 2, first : first + WIDE].rearrange("p e j -> p j e")
            if kind == "b":
                nc.vector.tensor_tensor(terms[s, kind][:, u], bank[:].rearrange("p e j -> p j e"), ph, MULT)
            else:
                nc.vector.scalar_tensor_tensor(terms[s, kind][:, u], ph, 1.0, bank[:].rearrange("p e j -> p j e"), SUB, MULT)

        def terms_of(s):
            order = [(kind, u) for kind in "ab" for u in range(2)] if s == 0 else [(kind, u) for u in range(2) for kind in "ab"]
            for kind, u in order:
                term(s, kind, u, product(kind, s, u))

        def subtract(s, engine, place, cols):
            engine.tensor_tensor(
                place.rearrange("p j (u e) -> p j u e", e=2),
                terms[s, "b"].rearrange("p u j e -> p j u e")[:, cols],
                terms[s, "a"].rearrange("p u j e -> p j u e")[:, cols],
                SUB,
            )

        def blend_sum(s):
            if s == len(BLENDS) - 1:
                whole = held([P, WIDE, 4], BF16, "h_last")
                h_b[s] = [(0, WIDE, whole[:])]
                for c0, n, place in h_b[s]:
                    subtract(s, nc.vector, place, slice(c0, c0 + n))
                return
            first = 2 * WIDE + 2 * POOL_COLS
            whole = term_tile[s, "a"][:, first : first + 2 * WIDE].bitcast(BF16).rearrange("p (j t) -> p j t", t=4)
            subtract(s, nc.vector, whole[:, POOL_COLS:WIDE, :], slice(POOL_COLS, WIDE))
            subtract(s, nc.gpsimd, whole[:, 0:POOL_COLS, :], slice(0, POOL_COLS))
            h_b[s] = [(0, WIDE, whole)]

        def quantise_h(s, parts=slice(None)):
            if s not in h_codes:
                h_codes_at[s] = phase_at(0) + 4 * WIDE if s == 2 else phase_at(s)
                h_codes[s] = (placed([P, WIDE], U32, "h_c%d" % s, h_codes_at[s]), held([P, WIDE], U8, "h_s%d" % s))
            codes, scales = h_codes[s]
            for c0, n, values in h_b[s][parts]:
                quantise(codes[:, c0 : c0 + n], scales[:, c0 : c0 + n], values.rearrange("p j t -> p (j t)"))
            h_q[BLENDS[s]] = (codes, scales, 0)

        def y_pass(place, j0, w, o, g, t, start, stop):
            codes, scales, c0 = h_q[g, j0]
            nc.tensor.matmul_mx(
                out=place,
                lhsT=skin_c[g, o][:, t * P : (t + 1) * P].bitcast(FP8X4),
                lhsT_scale=skin_s[g, o][:, t * P : (t + 1) * P],
                rhs=codes[:, c0 : c0 + w].bitcast(FP8X4),
                rhs_scale=scales[:, c0 : c0 + w],
                start=start,
                stop=stop,
            )

        def last_y_passes(g):
            cc = len(CHUNKS) - 1
            for o in range(2):
                for u in range(2):
                    if g == 0:
                        last_ps[o, u] = psum.tile([P, 2, WIDE], F32, name="ab%d" % (2 * o + u), bufs=1)
                    for e in range(2):
                        y_pass(last_ps[o, u][:, e, :], *CHUNKS[cc], o, g, 2 * u + e, g == 0 and e == 0, g == 1 and e == 1)

        def skin_product(cc, o, by_vector=()):
            j0, w = CHUNKS[cc]
            last_chunk = cc == len(CHUNKS) - 1
            per_bank = BANK // w
            y = placed([P, 4, w], F32, "y%d%d" % (cc, o), 16 * (2 * j0 + o * w))
            for t0 in range(0, 4, per_bank):
                if last_chunk:
                    y_ps = last_ps[o, t0 // 2]
                else:
                    y_ps = psum.tile([P, per_bank, w], F32, name="y_ps", bufs=4)
                    for k in range(per_bank):
                        for c0 in range(0, w, WIDE):
                            for g in range(2):
                                y_pass(y_ps[:, k, c0 : c0 + WIDE], j0 + c0, WIDE, o, g, t0 + k, g == 0, g == 1)
                if t0 in by_vector:
                    nc.vector.tensor_tensor(
                        y[:, t0 : t0 + per_bank, :],
                        y_ps[:],
                        rest_cols[:, o, t0 : t0 + per_bank].unsqueeze(2).to_broadcast([P, per_bank, w]),
                        ADD,
                    )
                else:
                    for k in range(per_bank):
                        t = t0 + k
                        nc.scalar.activation(y[:, t, :], y_ps[:, k, :], IDENT, bias=rest_cols[:, o, t : t + 1])
            rows = out_0[o * GROUP : (o + 1) * GROUP, j0 : j0 + w].rearrange("(p t) j -> p t j", t=4)
            per_store = 2 if (cc, o) == (0, 1) else 4
            for t0 in range(0, 4, per_store):
                nc.sync.dma_start(out=rows[:, t0 : t0 + per_store, :], in_=y[:, t0 : t0 + per_store, :])
            y_f[cc, o] = y

        def round_y(cc, o, c0, copy, at=None):
            w = min(CHUNKS[cc][1], WIDE)
            if at is not None:
                place = placed([P, w, 4], BF16, "y_late", at)[:]
            else:
                if (cc, o) not in y_b:
                    y_b[cc, o] = held([P, CHUNKS[cc][1], 4], BF16, "y_b%d%d" % (cc, o))
                place = y_b[cc, o][:, c0 : c0 + w, :]
            y_r[cc, o, c0] = place
            copy(
                out=place.rearrange("p (c i) t -> p c t i", i=4),
                in_=y_f[cc, o][:, :, c0 : c0 + w].rearrange("p t (c i) -> p c t i", i=4),
            )

        def quantise_y(cc, o, c0, n, values):
            j0, w = CHUNKS[cc]
            half, at = divmod(j0 + c0, GROUP)
            if half == 0:
                if (0, o) not in y_c:
                    y_c[0, o] = held([P, GROUP], I32, "y_c0%d" % o)
                codes = y_c[0, o][:]
            else:
                if 1 not in y_c:
                    y_c[1] = held([P, 2, GROUP], I32, "y_c1")
                codes = y_c[1][:, o, :]
            quantise(
                codes[:, at : at + n],
                y_s[:, o * S + j0 + c0 : o * S + j0 + c0 + n],
                values.rearrange("p j t -> p (j t)"),
            )
            words = out_1[:, :, half * GROUP : (half + 1) * GROUP, :].rearrange("o p j t -> p o (j t)").bitcast(I32)
            if half == 0 and at + n == GROUP:
                nc.sync.dma_start(out=words[:, o, :], in_=codes)
            elif at + n == GROUP:
                nc.sync.dma_start(out=words[:, o, :], in_=codes)

        round_weight(("w1", 0), nc.scalar.copy, cols=(0, 256))
        round_weight(("w1", 0), nc.vector.tensor_copy, cols=(256, GROUP))
        quantise_weight(("w1", 0), None)
        round_weight(("w1", 1), nc.scalar.copy)
        terms_of(0)
        blend_sum(0)

        terms_of(1)
        quantise_h(0)
        quantise_weight(("w1", 1), 1)
        blend_sum(1)
        round_weight(("skin", 0, 0), nc.scalar.copy)

        terms_of(2)
        quantise_h(1)
        blend_sum(2)
        round_weight(("skin", 1, 0), nc.scalar.copy)

        terms_of(3)
        quantise_h(2)
        quantise_weight(("skin", 0, 0), 3)
        blend_sum(3)
        round_weight(("skin", 0, 1), nc.scalar.copy)

        terms_of(4)
        quantise_h(3)
        quantise_weight(("skin", 1, 0), 4)
        blend_sum(4)

        terms_of(5)
        skin_product(0, 0)
        quantise_h(4)
        blend_sum(5)
        dealt["skin", 1, 1] = placed([P, 4 * GROUP], BF16, "last_b", phase_at(5) + 16 * WIDE - 64)
        round_weight(("skin", 1, 1), nc.scalar.copy, cols=(0, 192))
        round_y(0, 0, 0, nc.scalar.copy)

        terms_of(6)
        quantise_h(5)
        round_weight(("skin", 1, 1), nc.vector.tensor_copy, cols=(192, GROUP))
        quantise_weight(("skin", 0, 1), 5)
        quantise_weight(("skin", 1, 1), 6)
        blend_sum(6)
        skin_product(1, 0)

        terms_of(7)
        skin_product(0, 1)
        quantise_h(6)
        skin_product(1, 1)
        last_y_passes(0)

        blend_sum(7)
        round_y(0, 0, WIDE, nc.vector.tensor_copy)
        quantise_h(7)
        last_y_passes(1)
        quantise_y(0, 0, 0, GROUP, y_b[0, 0][:])
        round_y(0, 1, 0, nc.vector.tensor_copy)
        skin_product(2, 0, (2,))
        skin_product(2, 1)
        round_y(0, 1, WIDE, nc.vector.tensor_copy)
        round_y(1, 0, 0, nc.vector.tensor_copy)
        quantise_y(0, 1, 0, GROUP, y_b[0, 1][:])
        round_y(1, 1, 0, nc.scalar.copy)
        round_y(2, 0, 0, nc.vector.tensor_copy)
        round_y(2, 1, 0, nc.scalar.copy)
        for o in range(2):
            for cc in (1, 2):
                quantise_y(cc, o, 0, WIDE, y_r[cc, o, 0])

        for i in range(4):
            queue = nc.sync if i % 2 == 0 else nc.scalar
            queue.dma_start(
                out=out_2[:, i:16:4, :].bitcast(I32).rearrange("o q j -> q o j"),
                in_=y_s[i:P:32, :].bitcast(I32).rearrange("q (o j) -> q o j", o=2),
            )
